import numpy as np
import ml_dtypes


def mxq(x, axis, fmt="e4m3"):
    dtype, down = {"e4m3": (ml_dtypes.float8_e4m3fn, 7), "e5m2": (ml_dtypes.float8_e5m2, 14)}[fmt]
    v = np.moveaxis(np.asarray(x, np.float32).astype(ml_dtypes.bfloat16).astype(np.float64), axis, -1)
    blocks = v.reshape(v.shape[:-1] + (-1, 32))
    amax = np.abs(blocks).max(-1, keepdims=True)
    byte = np.maximum(np.where(amax > 0, np.frexp(amax)[1] - 1 + 127, 0) - down, 1)
    scale = np.exp2(byte - 127.0)
    codes = (blocks / scale).astype(np.float32).astype(dtype).astype(np.float64)
    return np.moveaxis((codes * scale).reshape(v.shape), -1, axis)


WIDE = False


def mx_kscale(k):
    if not WIDE:
        return np.ones(k)
    levels = np.array([10, -10, 5, -5, 0])
    if k % 512:
        return np.exp2(np.random.permutation(np.resize(levels, k // 32))).repeat(32)
    a = np.empty((k // 512, 16))
    for p in range(k // 512):
        a[p, :8] = np.random.permutation(np.resize(levels, 8))
        for g in range(8):
            far = levels[np.abs(levels - a[p, g]) >= 10]
            a[p, g + 8] = far[np.random.randint(len(far))]
    return np.exp2(a.ravel()).repeat(32)


def f64(x):
    return np.asarray(x).astype(np.float64)


def striped(idx):
    return np.tile(idx.reshape(-1, 16).T, (8, 1)).astype(np.uint16)


def unstriped(offs):
    return offs[:16].T.reshape(-1).astype(np.int64)


E2M1 = np.array([0.0, 0.5, 1.0, 1.5, 2.0, 3.0, 4.0, 6.0, -0.0, -0.5, -1.0, -1.5, -2.0, -3.0, -4.0, -6.0])


def pack_weight(w, fmt):
    k, n = w.shape
    w = f64(np.asarray(w, np.float32).astype(ml_dtypes.bfloat16)).reshape(k // 32, 32, n)
    amax = np.abs(w).max(1)
    if fmt == "e4m3":
        byte = np.frexp(amax)[1] - 1 + 127 - 7
    else:
        mant, ex = np.frexp(amax / 6.0)
        byte = np.where(mant > 0.5, ex, ex - 1) + 127
    byte = np.clip(np.where(amax > 0, byte, 1), 1, 254)
    scaled = (w * np.exp2(127.0 - byte)[:, None, :]).reshape(k, n).astype(np.float32)
    by_word = np.ascontiguousarray(scaled.reshape(k // 512, 128, 4, n).transpose(0, 1, 3, 2))
    if fmt == "e4m3":
        words = by_word.astype(ml_dtypes.float8_e4m3fn).view(np.uint8)
    else:
        c = by_word.astype(ml_dtypes.float4_e2m1fn).view(np.uint8) & 0xF
        words = (c[..., 0::2] | (c[..., 1::2] << 4)).reshape(k // 512, 128, 2 * n)
    return np.ascontiguousarray(words), np.ascontiguousarray(byte.astype(np.uint8).reshape(k // 512, 16, n))


def unpack_weight(words, scales, fmt):
    g, _, n = scales.shape
    words = np.ascontiguousarray(words).reshape(g, 128, n, -1)
    if fmt == "e4m3":
        vals = words.view(ml_dtypes.float8_e4m3fn).astype(np.float64)
    else:
        nib = np.empty((g, 128, n, 4), np.uint8)
        nib[..., 0::2] = words & 0xF
        nib[..., 1::2] = words >> 4
        vals = E2M1[nib]
    vals = vals * np.repeat(np.exp2(scales.astype(np.float64) - 127.0), 8, axis=1)[..., None]
    return vals.transpose(0, 1, 3, 2).reshape(g * 512, n)


def relu2(v):
    return np.maximum(v, 0.0) ** 2


K, T, E, C, H, N = 1024, 768, 9, 256, 512, 256
TOP = 3


def by_expert(wq, xq):
    return np.concatenate([wq[e].T @ xq[:, e * C:(e + 1) * C] for e in range(E)], axis=1)


def setup_inputs():
    n = np.random.standard_normal
    s = mx_kscale(K)[:, None]
    u = mx_kscale(H)
    deal = np.repeat(np.arange(E), C).reshape(TOP, T)[:, np.random.permutation(T)]
    deal = np.take_along_axis(deal, np.argsort(np.random.rand(TOP, T), axis=0), axis=0)
    for _ in range(8):
        s_, t_ = np.random.permutation(T).reshape(2, -1); r = np.random.randint(TOP, size=T // 2); x, y = deal[r, s_].copy(), deal[r, t_].copy()
        ok = ~((deal[:, s_] == y).any(0) | (deal[:, t_] == x).any(0)); deal[r[ok], s_[ok]] = y[ok]; deal[r[ok], t_[ok]] = x[ok]
    order = np.lexsort((np.random.rand(TOP * T), deal.reshape(-1)))
    slot_token = order % T; pos = np.empty(TOP * T, np.int64); pos[order] = np.arange(TOP * T); pos = pos.reshape(TOP, T)
    g = np.random.uniform(0.5, 1.5, (TOP, T)); g = g / g.sum(0)
    w1 = [pack_weight(m, "e2m1") for m in n((E, K, H)) / np.sqrt(K) / s[None] * u[None, None, :]]
    w2 = [pack_weight(m, "e2m1") for m in n((E, H, N)) / np.sqrt(H) / u[None, :, None] ** 2]
    x = pack_weight(n((K, T)) * s, "e4m3")
    return {
        "x_words": x[0],
        "x_scales": x[1],
        "w1_words": np.stack([m[0] for m in w1]),
        "w1_scales": np.stack([m[1] for m in w1]),
        "w2_words": np.stack([m[0] for m in w2]),
        "w2_scales": np.stack([m[1] for m in w2]),
        "gate": np.stack([np.tile(r, (N, 1)) for r in g]).astype(np.float32),
        "offs": striped(slot_token),
        "pos1": striped(pos[0]),
        "pos2": striped(pos[1]),
        "pos3": striped(pos[2]),
    }


def reference(x_words, x_scales, w1_words, w1_scales, w2_words, w2_scales, gate, offs, pos1, pos2, pos3):
    idx = unstriped(offs)
    w1 = np.stack([unpack_weight(w1_words[e], w1_scales[e], "e2m1") for e in range(E)])
    w2 = np.stack([unpack_weight(w2_words[e], w2_scales[e], "e2m1") for e in range(E)])
    xq = unpack_weight(x_words, x_scales, "e4m3")[:, idx]
    h = relu2(by_expert(w1, xq))
    y = by_expert(w2, mxq(h, 0, "e4m3"))
    return sum(f64(gate[r]) * y[:, unstriped(p)] for r, p in enumerate((pos1, pos2, pos3)))

@@ -1,0 +1,279 @@
+from contextlib import ExitStack
+
+import concourse.mybir as mybir
+from concourse.masks import make_identity
+
+K, T, E, C, H, N = 1024, 768, 9, 256, 512, 256
+TOP = 3
+S = E * C
+P = 128
+PASSES = K // 512
+FLOPS = 2 * S * (K * H + H * N)
+
+F32 = mybir.dt.float32
+BF16 = mybir.dt.bfloat16
+I32 = mybir.dt.int32
+U32 = mybir.dt.uint32
+U16 = mybir.dt.uint16
+U8 = mybir.dt.uint8
+FP8X4 = mybir.dt.float8_e4m3fn_x4
+FP4X4 = mybir.dt.float4_e2m1fn_x4
+ACT = mybir.ActivationFunctionType
+ALU = mybir.AluOpType
+
+BYTE_CUTS = [0, 256, 768, 1280, 1792, 2304]
+W1_CUTS = [0, 2, 4, 6, 9]
+EARLY = 2
+MOVED = 112
+RELU_ON_VECTOR = [7,11,13,14,15,16,17]
+LATE = 5
+
+
+def tile_moe_pkd_mlp_relu2_kernel(
+    tc, x_words, x_scales, w1_words, w1_scales, w2_words, w2_scales, gate, offs, pos1, pos2, pos3, out
+):
+    nc = tc.nc
+    with ExitStack() as ctx:
+        keep = ctx.enter_context(tc.tile_pool(name="keep", bufs=1))
+        turns = ctx.enter_context(tc.tile_pool(name="turns", bufs=1))
+        ring = ctx.enter_context(tc.tile_pool(name="ring", bufs=4))
+        ps_two = ctx.enter_context(tc.psum_pool(name="ps_two", bufs=2))
+        ps_one = ctx.enter_context(tc.psum_pool(name="ps_one", bufs=3))
+        ps_y = ctx.enter_context(tc.psum_pool(name="ps_y", bufs=1))
+
+        offs_t = keep.tile([P, S // 16], U16, name="offs_t")
+        pos_t = [keep.tile([P, T // 16], U16, name="pos_t%d" % r) for r in range(TOP)]
+        xw = [keep.tile([P, T], I32, name="xw%d" % s, align_bytes=64) for s in range(PASSES)]
+        xs = keep.tile([P, T], U8, name="xs", align_bytes=64)
+        w1s_b = keep.tile([P, (E - EARLY) * PASSES, H], U8, name="w1s_b", align_bytes=256)
+        w2s = keep.tile([P, E, N], U8, name="w2s", align_bytes=256)
+        sg1 = keep.tile([P, S], U8, name="sg1", align_bytes=256)
+        hb = keep.tile([P, S, 4], BF16, name="hb", align_bytes=256)
+        hs = keep.tile([P, S], U8, name="hs", align_bytes=256)
+        y = [keep.tile([P, S], F32, name="y%d" % a, align_bytes=64) for a in range(2)]
+        ident = keep.tile([P, P], F32, name="ident", align_bytes=64)
+
+        def shared(slot, shape, dtype, name):
+            return turns.tile(shape, dtype, name=name, tag=slot, align_bytes=256)
+
+        def load_scales(plane, src):
+            for q in range(4):
+                nc.sync.dma_start(
+                    out=plane[32 * q : 32 * q + 4, :, :].bitcast(I32),
+                    in_=src[:, 4 * q : 4 * q + 4, :].rearrange("a r c -> r a c").bitcast(I32),
+                )
+
+        w1w = {}
+
+        def load_w1(c, slot):
+            e0, e1 = W1_CUTS[c], W1_CUTS[c + 1]
+            tile = shared(slot, [P, PASSES * (e1 - e0), 2 * H], U8, "w1_%d" % c)
+            for e in range(e0, e1):
+                for s in range(PASSES):
+                    w1w[e, s] = tile[:, PASSES * (e - e0) + s, :]
+            nc.sync.dma_start(
+                out=tile[:].bitcast(I32), in_=w1_words[e0:e1].rearrange("e s p b -> p (e s) b").bitcast(I32)
+            )
+
+        w2w = {}
+
+        def load_w2(a, slot):
+            w2w[a] = shared(slot, [P, E, N], U8, "w2w%d" % a)
+            nc.sync.dma_start(
+                out=w2w[a][:].bitcast(I32),
+                in_=w2_words.rearrange("e s p b -> p (e s) b")[:, :, a * N : (a + 1) * N].bitcast(I32),
+            )
+
+        w1_planes = w1_scales.rearrange("e s q i -> (e s) q i")
+        w1s_a = shared("c", [P, EARLY * PASSES, H], U8, "w1s_a")
+        warm = shared("b", [P, 8], F32, "warm")
+        nc.vector.memset(xs[:].bitcast(I32), 0)
+        nc.vector.memset(w1s_a[:].rearrange("p a c -> p (a c)").bitcast(I32), 0)
+        nc.vector.memset(warm[:], 0.0)
+        nc.vector.memset(sg1[:].bitcast(I32), 0)
+        nc.scalar.activation(out=warm[:, 0:1], in_=warm[:, 1:2], func=ACT.Relu)
+        make_identity(nc, ident[:])
+        nc.gpsimd.memset(w1s_b[:].rearrange("p a c -> p (a c)").bitcast(I32), 0)
+        nc.gpsimd.memset(w2s[:].rearrange("p a c -> p (a c)").bitcast(I32), 0)
+
+        nc.sync.dma_start(offs_t[:], offs)
+        for q in range(4):
+            nc.sync.dma_start(
+                out=xs[32 * q : 32 * q + 8, :].bitcast(I32), in_=x_scales[:, 4 * q : 4 * q + 4, :].bitcast(I32)
+            )
+        for s in range(PASSES):
+            nc.sync.dma_start(out=xw[s][:], in_=x_words[s].rearrange("p t r -> p (t r)").bitcast(I32))
+        load_w1(0, "a")
+        load_scales(w1s_a, w1_planes[: EARLY * PASSES])
+
+        xg = {}
+        sg = {}
+        relu_t = {}
+        late = {}
+
+        def gather_words(e, pieces=1):
+            xg[e] = ring.tile([P, PASSES, C], U32, name="xg", bufs=3, align_bytes=256)
+            width = C // pieces
+            for lo in range(0, C, width):
+                o = offs_t[:, (e * C + lo) // 16 : (e * C + lo + width) // 16]
+                for s in range(PASSES):
+                    nc.vector.tensor_copy(xg[e][:, s, lo : lo + width], xw[s][:].bitcast(U32).indirect(o))
+
+        def gather_bytes(c, slot):
+            j0, j1 = BYTE_CUTS[c], BYTE_CUTS[c + 1]
+            tile = shared(slot, [P, j1 - j0], U8, "sg%d" % c)
+            for u in range(j0 // P, j1 // P):
+                sg[u] = tile[:, u * P - j0 : (u + 1) * P - j0]
+            nc.vector.tensor_copy(tile[:], xs[:].indirect(offs_t[:, j0 // 16 : j1 // 16]))
+            nc.sync.dma_start(out=sg1[0:MOVED, j0:j1].bitcast(I32), in_=tile[4 : 4 + MOVED, :].bitcast(I32))
+
+        def w1_scale(e, s):
+            return w1s_a[:, PASSES * e + s, :] if e < EARLY else w1s_b[:, PASSES * (e - EARLY) + s, :]
+
+        def layer1(e):
+            acc = ps_two.tile([P, 2, H], F32, name="acc", tag="two")
+            for half in range(2):
+                u = 2 * e + half
+                for s in range(PASSES):
+                    nc.tensor.matmul_mx(
+                        out=acc[:, half, :],
+                        lhsT=xg[e][:, s, half * P : (half + 1) * P].bitcast(FP8X4),
+                        lhsT_scale=(sg[u], sg1[:, u * P : (u + 1) * P])[s],
+                        rhs=w1w[e, s].bitcast(FP4X4),
+                        rhs_scale=w1_scale(e, s),
+                        start=(s == 0),
+                        stop=(s == PASSES - 1),
+                    )
+            for half in range(2):
+                u = 2 * e + half
+                relu_t[u] = ring.tile([P, 4, P], F32, name="r_t", align_bytes=64)
+                view = acc[:, half, :].rearrange("j (p t) -> j t p", t=4)
+                if u in RELU_ON_VECTOR:
+                    nc.vector.tensor_scalar_max(relu_t[u][:], view, 0.0)
+                else:
+                    nc.scalar.activation(out=relu_t[u][:], in_=view, func=ACT.Relu)
+
+        def turn(u):
+            turned = ps_one.tile([P, 4, P], F32, name="turned", tag="one")
+            for t in range(4):
+                nc.tensor.transpose(turned[:, t, :], relu_t[u][:, t, :], ident[:])
+            nc.scalar.activation(
+                out=hb[:, u * P : (u + 1) * P, :], in_=turned[:].rearrange("p t j -> p j t"), func=ACT.Square
+            )
+
+        def quantise(j0, j1):
+            nc.vector.quantize_mx(
+                out=late["hq"][:, j0:j1].bitcast(FP8X4), scales=hs[:, j0:j1], in_=hb[:, j0:j1, :].rearrange("p j t -> p (j t)")
+            )
+
+        def layer2(a, j0, j1, pool, tag):
+            bank = pool.tile([P, j1 - j0], F32, name="ybank", tag=tag)
+            for lo in range(j0, j1, C):
+                hi = min(lo + C, j1)
+                e = lo // C
+                nc.tensor.matmul_mx(
+                    out=bank[:, lo - j0 : hi - j0],
+                    lhsT=w2w[a][:, e, :].bitcast(FP4X4),
+                    lhsT_scale=w2s[:, e, a * P : (a + 1) * P],
+                    rhs=late["hq"][:, lo:hi].bitcast(FP8X4),
+                    rhs_scale=hs[:, lo:hi],
+                    start=True,
+                    stop=True,
+                )
+            nc.scalar.copy(out=y[a][:, j0:j1], in_=bank[:])
+
+        gather_bytes(0, "s0")
+        gather_words(0, pieces=2)
+        gather_bytes(1, "s1")
+        gather_words(1)
+        gather_words(2)
+        load_w1(1, "b")
+        load_scales(w1s_b, w1_planes[EARLY * PASSES :])
+        load_scales(w2s, w2_scales.rearrange("e s q n -> (e s) q n"))
+        for r, src in enumerate((pos1, pos2, pos3)):
+            nc.sync.dma_start(pos_t[r][:], src)
+
+        pairs_done = 0
+        late["hq"] = keep.tile([P, S], U32, name="hq", align_bytes=256)
+        for e in range(E + 1):
+            if e == 1:
+                gather_bytes(2, "s0")
+            if 1 <= e <= E - 3:
+                gather_words(e + 2)
+            if e == 2:
+                gather_bytes(3, "c")
+                load_w1(2, "a")
+            if e == 3:
+                load_w2(0, "s1")
+            if e == 4:
+                load_w1(3, "b")
+            if e == 5:
+                gather_bytes(4, "s0")
+            if e == 7:
+                g = shared("c", [P, 2, TOP, T], F32, "g")
+                for a in range(2):
+                    for r in range(TOP):
+                        nc.sync.dma_start(out=g[:, a, r, :], in_=gate[r, a * P : (a + 1) * P, :])
+            if e == E:
+                load_w2(1, "b")
+            if e < E:
+                layer1(e)
+            if e >= 1:
+                turn(2 * e - 2)
+                if e == E:
+                    quantise(S - C, S - P)
+                    layer2(0, S - C, S - P, ps_y, "y")
+                turn(2 * e - 1)
+                if e < E:
+                    quantise((e - 1) * C, e * C)
+            if LATE <= e < E:
+                for k in range(2):
+                    if 2 * pairs_done + 2 <= e:
+                        layer2(0, 2 * pairs_done * C, (2 * pairs_done + 2) * C, ps_y, "y")
+                        pairs_done += 1
+        assert pairs_done == E // 2
+        quantise(S - P, S)
+        layer2(0, S - P, S, ps_one, "one")
+        for j0 in range(0, S, 2 * C):
+            layer2(1, j0, min(j0 + 2 * C, S), ps_one, "one")
+
+        prod = [[keep.tile([P, T], F32, name="prod%d_%d" % (a, r), align_bytes=64) for r in range(TOP)] for a in range(2)]
+        sum_t = keep.tile([P, T], F32, name="sum_t", align_bytes=64)
+        part = keep.tile([P, T], F32, name="part", align_bytes=64)
+        res = [keep.tile([P, T], F32, name="res%d" % a, align_bytes=64) for a in range(2)]
+        HALF = T // 2
+
+        def product(a, r, t0, t1):
+            nc.vector.tensor_tensor(
+                prod[a][r][:, t0:t1], y[a][:].indirect(pos_t[r][:, t0 // 16 : t1 // 16]), g[:, a, r, t0:t1], ALU.mult
+            )
+
+        for t0 in range(0, T, HALF):
+            for r in range(TOP):
+                product(0, r, t0, t0 + HALF)
+            banks = ps_two.tile([P, 2, H], F32, name="sums", tag="two")
+            for lo in range(0, HALF, P):
+                for r in range(TOP):
+                    nc.tensor.matmul(
+                        banks[:, 0, lo : lo + P],
+                        lhsT=prod[0][r][:, t0 + lo : t0 + lo + P],
+                        rhs=ident[:],
+                        is_transpose=True,
+                        start=(r == 0),
+                        stop=(r == TOP - 1),
+                    )
+            nc.scalar.copy(out=sum_t[:, t0 : t0 + HALF], in_=banks[:, 0, :HALF])
+            for lo in range(0, HALF, P):
+                nc.tensor.transpose(banks[:, 1, lo : lo + P], sum_t[:, t0 + lo : t0 + lo + P], ident[:])
+            nc.scalar.copy(out=res[0][:, t0 : t0 + HALF], in_=banks[:, 1, :HALF])
+            nc.sync.dma_start(out=out[0:P, t0 : t0 + HALF], in_=res[0][:, t0 : t0 + HALF])
+        product(1, 0, 0, T)
+        product(1, 1, 0, T)
+        product(1, 2, 0, HALF)
+        nc.vector.tensor_tensor(part[:], prod[1][0][:], prod[1][1][:], ALU.add)
+        product(1, 2, HALF, T)
+        for t0 in range(0, T, HALF):
+            nc.vector.tensor_tensor(
+                res[1][:, t0 : t0 + HALF], part[:, t0 : t0 + HALF], prod[1][2][:, t0 : t0 + HALF], ALU.add
+            )
+            nc.sync.dma_start(out=out[P:, t0 : t0 + HALF], in_=res[1][:, t0 : t0 + HALF])

@@ -21,12 +21,12 @@ FP4X4 = mybir.dt.float4_e2m1fn_x4
 ACT = mybir.ActivationFunctionType
 ALU = mybir.AluOpType
 
-BYTE_CUTS = [0, 256, 768, 1280, 1792, 2304]
-W1_CUTS = [0, 2, 4, 6, 9]
-EARLY = 2
+BYTE_CUTS = [0,384,768,1280,1792,2304]
+W1_CUTS = [0,2,4,7,9]
+SCALE_CUTS = [0,2,9]
 MOVED = 112
-RELU_ON_VECTOR = [7,11,13,14,15,16,17]
-LATE = 5
+RELU_ON_VECTOR = [1,10,13,14,15,16,17]
+LAYER2_IN_ROUND = {5: (0, 2), 6: (2, 4), 7: (4, 6)}
 
 
 def tile_moe_pkd_mlp_relu2_kernel(
@@ -36,65 +36,88 @@ def tile_moe_pkd_mlp_relu2_kernel(
     with ExitStack() as ctx:
         keep = ctx.enter_context(tc.tile_pool(name="keep", bufs=1))
         turns = ctx.enter_context(tc.tile_pool(name="turns", bufs=1))
-        ring = ctx.enter_context(tc.tile_pool(name="ring", bufs=4))
-        ps_two = ctx.enter_context(tc.psum_pool(name="ps_two", bufs=2))
-        ps_one = ctx.enter_context(tc.psum_pool(name="ps_one", bufs=3))
+        ring = ctx.enter_context(tc.tile_pool(name="ring", bufs=2))
+        ps_a = ctx.enter_context(tc.psum_pool(name="ps_a", bufs=4))
+        ps_t = ctx.enter_context(tc.psum_pool(name="ps_t", bufs=3))
         ps_y = ctx.enter_context(tc.psum_pool(name="ps_y", bufs=1))
 
         offs_t = keep.tile([P, S // 16], U16, name="offs_t")
         pos_t = [keep.tile([P, T // 16], U16, name="pos_t%d" % r) for r in range(TOP)]
         xw = [keep.tile([P, T], I32, name="xw%d" % s, align_bytes=64) for s in range(PASSES)]
         xs = keep.tile([P, T], U8, name="xs", align_bytes=64)
-        w1s_b = keep.tile([P, (E - EARLY) * PASSES, H], U8, name="w1s_b", align_bytes=256)
         w2s = keep.tile([P, E, N], U8, name="w2s", align_bytes=256)
         sg1 = keep.tile([P, S], U8, name="sg1", align_bytes=256)
         hb = keep.tile([P, S, 4], BF16, name="hb", align_bytes=256)
+        hq = keep.tile([P, S], U32, name="hq", align_bytes=256)
         hs = keep.tile([P, S], U8, name="hs", align_bytes=256)
         y = [keep.tile([P, S], F32, name="y%d" % a, align_bytes=64) for a in range(2)]
         ident = keep.tile([P, P], F32, name="ident", align_bytes=64)
+        w1s_t = [
+            keep.tile([P, PASSES * (SCALE_CUTS[c + 1] - SCALE_CUTS[c]), H], U8, name="w1s%d" % c, align_bytes=256)
+            for c in range(len(SCALE_CUTS) - 1)
+        ]
+        w1s = {}
+        for c in range(len(SCALE_CUTS) - 1):
+            for e in range(SCALE_CUTS[c], SCALE_CUTS[c + 1]):
+                for s in range(PASSES):
+                    w1s[e, s] = w1s_t[c][:, PASSES * (e - SCALE_CUTS[c]) + s, :]
 
         def shared(slot, shape, dtype, name):
             return turns.tile(shape, dtype, name=name, tag=slot, align_bytes=256)
 
-        def load_scales(plane, src):
-            for q in range(4):
-                nc.sync.dma_start(
+        def zero(plane, engine):
+            engine.memset(plane[:].rearrange("p a c -> p (a c)").bitcast(I32), 0)
+
+        def load_scales(plane, src, queue):
+            for q in (0, 2, 1, 3):
+                queue.dma_start(
                     out=plane[32 * q : 32 * q + 4, :, :].bitcast(I32),
                     in_=src[:, 4 * q : 4 * q + 4, :].rearrange("a r c -> r a c").bitcast(I32),
                 )
 
-        w1w = {}
+        w1_planes = w1_scales.rearrange("e s q i -> (e s) q i")
 
-        def load_w1(c, slot):
+        def load_w1s(c, queue):
+            load_scales(w1s_t[c], w1_planes[PASSES * SCALE_CUTS[c] : PASSES * SCALE_CUTS[c + 1]], queue)
+
+        w1w = {}
+        w2w = keep.tile([P, E, 2 * N], U8, name="w2w", align_bytes=256)
+
+        def load_w1(c, slot, queue):
             e0, e1 = W1_CUTS[c], W1_CUTS[c + 1]
             tile = shared(slot, [P, PASSES * (e1 - e0), 2 * H], U8, "w1_%d" % c)
             for e in range(e0, e1):
                 for s in range(PASSES):
                     w1w[e, s] = tile[:, PASSES * (e - e0) + s, :]
-            nc.sync.dma_start(
+            queue.dma_start(
                 out=tile[:].bitcast(I32), in_=w1_words[e0:e1].rearrange("e s p b -> p (e s) b").bitcast(I32)
             )
 
-        w2w = {}
+        def load_w2(queue):
+            queue.dma_start(out=w2w[:].bitcast(I32), in_=w2_words.rearrange("e s p b -> p (e s) b").bitcast(I32))
 
-        def load_w2(a, slot):
-            w2w[a] = shared(slot, [P, E, N], U8, "w2w%d" % a)
-            nc.sync.dma_start(
-                out=w2w[a][:].bitcast(I32),
-                in_=w2_words.rearrange("e s p b -> p (e s) b")[:, :, a * N : (a + 1) * N].bitcast(I32),
-            )
+        def load_w2s(queue):
+            load_scales(w2s, w2_scales.rearrange("e s q n -> (e s) q n"), queue)
 
-        w1_planes = w1_scales.rearrange("e s q i -> (e s) q i")
-        w1s_a = shared("c", [P, EARLY * PASSES, H], U8, "w1s_a")
+        def load_pos():
+            for r, src in enumerate((pos1, pos2, pos3)):
+                nc.sync.dma_start(pos_t[r][:], src)
+
+        g = {}
+
+        def load_gate(a, slot):
+            g[a] = shared(slot, [P, TOP, T], F32, "g%d" % a)
+            nc.sync.dma_start(out=g[a][:], in_=gate[:, a * P : (a + 1) * P, :].rearrange("r p t -> p r t"))
+
         warm = shared("b", [P, 8], F32, "warm")
         nc.vector.memset(xs[:].bitcast(I32), 0)
-        nc.vector.memset(w1s_a[:].rearrange("p a c -> p (a c)").bitcast(I32), 0)
+        zero(w1s_t[0], nc.vector)
         nc.vector.memset(warm[:], 0.0)
         nc.vector.memset(sg1[:].bitcast(I32), 0)
         nc.scalar.activation(out=warm[:, 0:1], in_=warm[:, 1:2], func=ACT.Relu)
         make_identity(nc, ident[:])
-        nc.gpsimd.memset(w1s_b[:].rearrange("p a c -> p (a c)").bitcast(I32), 0)
-        nc.gpsimd.memset(w2s[:].rearrange("p a c -> p (a c)").bitcast(I32), 0)
+        zero(w1s_t[1], nc.gpsimd)
+        zero(w2s, nc.gpsimd)
 
         nc.sync.dma_start(offs_t[:], offs)
         for q in range(4):
@@ -103,21 +126,18 @@ def tile_moe_pkd_mlp_relu2_kernel(
             )
         for s in range(PASSES):
             nc.sync.dma_start(out=xw[s][:], in_=x_words[s].rearrange("p t r -> p (t r)").bitcast(I32))
-        load_w1(0, "a")
-        load_scales(w1s_a, w1_planes[: EARLY * PASSES])
+        load_w1(0, "a", nc.sync)
+        load_w1s(0, nc.sync)
 
         xg = {}
         sg = {}
         relu_t = {}
-        late = {}
 
-        def gather_words(e, pieces=1):
+        def gather_words(e):
             xg[e] = ring.tile([P, PASSES, C], U32, name="xg", bufs=3, align_bytes=256)
-            width = C // pieces
-            for lo in range(0, C, width):
-                o = offs_t[:, (e * C + lo) // 16 : (e * C + lo + width) // 16]
-                for s in range(PASSES):
-                    nc.vector.tensor_copy(xg[e][:, s, lo : lo + width], xw[s][:].bitcast(U32).indirect(o))
+            o = offs_t[:, e * C // 16 : (e + 1) * C // 16]
+            for s in range(PASSES):
+                nc.vector.tensor_copy(xg[e][:, s, :], xw[s][:].bitcast(U32).indirect(o))
 
         def gather_bytes(c, slot):
             j0, j1 = BYTE_CUTS[c], BYTE_CUTS[c + 1]
@@ -127,115 +147,106 @@ def tile_moe_pkd_mlp_relu2_kernel(
             nc.vector.tensor_copy(tile[:], xs[:].indirect(offs_t[:, j0 // 16 : j1 // 16]))
             nc.sync.dma_start(out=sg1[0:MOVED, j0:j1].bitcast(I32), in_=tile[4 : 4 + MOVED, :].bitcast(I32))
 
-        def w1_scale(e, s):
-            return w1s_a[:, PASSES * e + s, :] if e < EARLY else w1s_b[:, PASSES * (e - EARLY) + s, :]
-
-        def layer1(e):
-            acc = ps_two.tile([P, 2, H], F32, name="acc", tag="two")
-            for half in range(2):
-                u = 2 * e + half
-                for s in range(PASSES):
-                    nc.tensor.matmul_mx(
-                        out=acc[:, half, :],
-                        lhsT=xg[e][:, s, half * P : (half + 1) * P].bitcast(FP8X4),
-                        lhsT_scale=(sg[u], sg1[:, u * P : (u + 1) * P])[s],
-                        rhs=w1w[e, s].bitcast(FP4X4),
-                        rhs_scale=w1_scale(e, s),
-                        start=(s == 0),
-                        stop=(s == PASSES - 1),
-                    )
-            for half in range(2):
-                u = 2 * e + half
-                relu_t[u] = ring.tile([P, 4, P], F32, name="r_t", align_bytes=64)
-                view = acc[:, half, :].rearrange("j (p t) -> j t p", t=4)
-                if u in RELU_ON_VECTOR:
-                    nc.vector.tensor_scalar_max(relu_t[u][:], view, 0.0)
-                else:
-                    nc.scalar.activation(out=relu_t[u][:], in_=view, func=ACT.Relu)
-
-        def turn(u):
-            turned = ps_one.tile([P, 4, P], F32, name="turned", tag="one")
-            for t in range(4):
-                nc.tensor.transpose(turned[:, t, :], relu_t[u][:, t, :], ident[:])
-            nc.scalar.activation(
-                out=hb[:, u * P : (u + 1) * P, :], in_=turned[:].rearrange("p t j -> p j t"), func=ACT.Square
-            )
-
-        def quantise(j0, j1):
-            nc.vector.quantize_mx(
-                out=late["hq"][:, j0:j1].bitcast(FP8X4), scales=hs[:, j0:j1], in_=hb[:, j0:j1, :].rearrange("p j t -> p (j t)")
-            )
-
-        def layer2(a, j0, j1, pool, tag):
-            bank = pool.tile([P, j1 - j0], F32, name="ybank", tag=tag)
+        def layer2(a, j0, j1, bank):
             for lo in range(j0, j1, C):
                 hi = min(lo + C, j1)
                 e = lo // C
                 nc.tensor.matmul_mx(
                     out=bank[:, lo - j0 : hi - j0],
-                    lhsT=w2w[a][:, e, :].bitcast(FP4X4),
+                    lhsT=w2w[:, e, a * N : (a + 1) * N].bitcast(FP4X4),
                     lhsT_scale=w2s[:, e, a * P : (a + 1) * P],
-                    rhs=late["hq"][:, lo:hi].bitcast(FP8X4),
+                    rhs=hq[:, lo:hi].bitcast(FP8X4),
                     rhs_scale=hs[:, lo:hi],
                     start=True,
                     stop=True,
                 )
-            nc.scalar.copy(out=y[a][:, j0:j1], in_=bank[:])
+            nc.scalar.copy(out=y[a][:, j0:j1], in_=bank[:, : j1 - j0])
+
+        def bank(pool):
+            return pool.tile([P, H], F32, name="bank")[:]
+
+        def layer1(e):
+            acc = [bank(ps_a) for half in range(2)]
+            for s, half in ((0, 0), (0, 1), (1, 0), (1, 1)):
+                u = 2 * e + half
+                nc.tensor.matmul_mx(
+                    out=acc[half],
+                    lhsT=xg[e][:, s, half * P : (half + 1) * P].bitcast(FP8X4),
+                    lhsT_scale=(sg[u], sg1[:, u * P : (u + 1) * P])[s],
+                    rhs=w1w[e, s].bitcast(FP4X4),
+                    rhs_scale=w1s[e, s],
+                    start=(s == 0),
+                    stop=(s == PASSES - 1),
+                )
+            for half in range(2):
+                u = 2 * e + half
+                relu_t[u] = ring.tile([P, 4, P], F32, name="r_t", bufs=4, align_bytes=64)
+                view = acc[half].rearrange("j (c i t) -> j c t i", i=4, t=4)
+                dst = relu_t[u][:].rearrange("j t (c i) -> j c t i", i=4)
+                if u in RELU_ON_VECTOR:
+                    nc.vector.tensor_scalar_max(dst, view, 0.0)
+                else:
+                    nc.scalar.activation(out=dst, in_=view, func=ACT.Relu)
+
+        def quantise(j0, j1):
+            nc.vector.quantize_mx(
+                out=hq[:, j0:j1].bitcast(FP8X4), scales=hs[:, j0:j1], in_=hb[:, j0:j1, :].rearrange("p j t -> p (j t)")
+            )
+
+        def turn(u, pool):
+            turned = bank(pool).rearrange("p (t j) -> p t j", t=4)
+            for t in range(4):
+                nc.tensor.transpose(turned[:, t, :], relu_t[u][:, t, :], ident[:])
+            nc.scalar.activation(
+                out=hb[:, u * P : (u + 1) * P, :], in_=turned.rearrange("p t j -> p j t"), func=ACT.Square
+            )
 
         gather_bytes(0, "s0")
-        gather_words(0, pieces=2)
         gather_bytes(1, "s1")
+        gather_words(0)
         gather_words(1)
         gather_words(2)
-        load_w1(1, "b")
-        load_scales(w1s_b, w1_planes[EARLY * PASSES :])
-        load_scales(w2s, w2_scales.rearrange("e s q n -> (e s) q n"))
-        for r, src in enumerate((pos1, pos2, pos3)):
-            nc.sync.dma_start(pos_t[r][:], src)
-
-        pairs_done = 0
-        late["hq"] = keep.tile([P, S], U32, name="hq", align_bytes=256)
-        for e in range(E + 1):
-            if e == 1:
+        load_w1(1, "b", nc.sync)
+        load_w1s(1, nc.sync)
+        for k in range(E):
+            if k == 1:
+                gather_words(3)
+            if k == 2:
                 gather_bytes(2, "s0")
-            if 1 <= e <= E - 3:
-                gather_words(e + 2)
-            if e == 2:
-                gather_bytes(3, "c")
-                load_w1(2, "a")
-            if e == 3:
-                load_w2(0, "s1")
-            if e == 4:
-                load_w1(3, "b")
-            if e == 5:
+                gather_words(4)
+                load_w1(2, "a", nc.sync)
+            if k == 3:
+                gather_bytes(3, "s1")
+                gather_words(5)
+                load_w2s(nc.sync)
+                load_w2(nc.sync)
+            if k == 4:
+                gather_words(6)
+                load_w1(3, "b", nc.sync)
+            if k == 5:
                 gather_bytes(4, "s0")
-            if e == 7:
-                g = shared("c", [P, 2, TOP, T], F32, "g")
-                for a in range(2):
-                    for r in range(TOP):
-                        nc.sync.dma_start(out=g[:, a, r, :], in_=gate[r, a * P : (a + 1) * P, :])
-            if e == E:
-                load_w2(1, "b")
-            if e < E:
-                layer1(e)
-            if e >= 1:
-                turn(2 * e - 2)
-                if e == E:
-                    quantise(S - C, S - P)
-                    layer2(0, S - C, S - P, ps_y, "y")
-                turn(2 * e - 1)
-                if e < E:
-                    quantise((e - 1) * C, e * C)
-            if LATE <= e < E:
-                for k in range(2):
-                    if 2 * pairs_done + 2 <= e:
-                        layer2(0, 2 * pairs_done * C, (2 * pairs_done + 2) * C, ps_y, "y")
-                        pairs_done += 1
-        assert pairs_done == E // 2
-        quantise(S - P, S)
-        layer2(0, S - P, S, ps_one, "one")
+                gather_words(7)
+                load_pos()
+            if k == 6:
+                gather_words(8)
+            if k == 7:
+                load_gate(0, "a")
+                load_gate(1, "s1")
+            layer1(k)
+            if k >= 1:
+                turn(2 * k - 2, ps_t)
+                turn(2 * k - 1, ps_t)
+                quantise((k - 1) * C, k * C)
+            if k in LAYER2_IN_ROUND:
+                layer2(0, LAYER2_IN_ROUND[k][0] * C, LAYER2_IN_ROUND[k][1] * C, bank(ps_y))
+        turn(2 * E - 2, ps_a)
+        turn(2 * E - 1, ps_a)
+        layer2(0, 6 * C, 8 * C, bank(ps_y))
+        for lo in (S - C, S - P):
+            quantise(lo, lo + P)
+            layer2(0, lo, lo + P, bank(ps_t))
         for j0 in range(0, S, 2 * C):
-            layer2(1, j0, min(j0 + 2 * C, S), ps_one, "one")
+            layer2(1, j0, min(j0 + 2 * C, S), bank(ps_a))
 
         prod = [[keep.tile([P, T], F32, name="prod%d_%d" % (a, r), align_bytes=64) for r in range(TOP)] for a in range(2)]
         sum_t = keep.tile([P, T], F32, name="sum_t", align_bytes=64)
@@ -245,28 +256,29 @@ def tile_moe_pkd_mlp_relu2_kernel(
 
         def product(a, r, t0, t1):
             nc.vector.tensor_tensor(
-                prod[a][r][:, t0:t1], y[a][:].indirect(pos_t[r][:, t0 // 16 : t1 // 16]), g[:, a, r, t0:t1], ALU.mult
+                prod[a][r][:, t0:t1], y[a][:].indirect(pos_t[r][:, t0 // 16 : t1 // 16]), g[a][:, r, t0:t1], ALU.mult
             )
 
         for t0 in range(0, T, HALF):
             for r in range(TOP):
                 product(0, r, t0, t0 + HALF)
-            banks = ps_two.tile([P, 2, H], F32, name="sums", tag="two")
+            sums = bank(ps_t)[:, :HALF]
             for lo in range(0, HALF, P):
                 for r in range(TOP):
                     nc.tensor.matmul(
-                        banks[:, 0, lo : lo + P],
+                        sums[:, lo : lo + P],
                         lhsT=prod[0][r][:, t0 + lo : t0 + lo + P],
                         rhs=ident[:],
                         is_transpose=True,
                         start=(r == 0),
                         stop=(r == TOP - 1),
                     )
-            nc.scalar.copy(out=sum_t[:, t0 : t0 + HALF], in_=banks[:, 0, :HALF])
+            nc.scalar.copy(out=sum_t[:, t0 : t0 + HALF], in_=sums)
+            back = bank(ps_t)[:, :HALF]
             for lo in range(0, HALF, P):
-                nc.tensor.transpose(banks[:, 1, lo : lo + P], sum_t[:, t0 + lo : t0 + lo + P], ident[:])
-            nc.scalar.copy(out=res[0][:, t0 : t0 + HALF], in_=banks[:, 1, :HALF])
-            nc.sync.dma_start(out=out[0:P, t0 : t0 + HALF], in_=res[0][:, t0 : t0 + HALF])
+                nc.tensor.transpose(back[:, lo : lo + P], sum_t[:, t0 + lo : t0 + lo + P], ident[:])
+            nc.scalar.copy(out=res[0][:, t0 : t0 + HALF], in_=back)
+            nc.scalar.dma_start(out=out[0:P, t0 : t0 + HALF], in_=res[0][:, t0 : t0 + HALF])
         product(1, 0, 0, T)
         product(1, 1, 0, T)
         product(1, 2, 0, HALF)

@@ -8,6 +8,7 @@ TOP = 3
 S = E * C
 P = 128
 PASSES = K // 512
+HALF_T = T // 2
 FLOPS = 2 * S * (K * H + H * N)
 
 F32 = mybir.dt.float32
@@ -21,12 +22,16 @@ FP4X4 = mybir.dt.float4_e2m1fn_x4
 ACT = mybir.ActivationFunctionType
 ALU = mybir.AluOpType
 
-BYTE_CUTS = [0,384,768,1280,1792,2304]
-W1_CUTS = [0,2,4,7,9]
-SCALE_CUTS = [0,2,9]
+BYTE_CUTS = (0, 384, 768, 1280, 1792, 2304)
+W1_CUTS = (0, 2, 4, 7, 9)
+SCALE_CUTS = (0, 2, 9)
 MOVED = 112
-RELU_ON_VECTOR = [1,10,13,14,15,16,17]
-LAYER2_IN_ROUND = {5: (0, 2), 6: (2, 4), 7: (4, 6)}
+RELU_ON_VECTOR = (1, 10, 14, 15, 16, 17)
+WORDS_AHEAD = 3
+BYTES_IN_ROUND = {2: 2, 3: 3, 5: 4}
+W1_IN_ROUND = {2: 2, 4: 3}
+W2_ROUND, LISTS_ROUND, GATE_ROUND = 3, 5, 7
+LAYER2_FROM = 5
 
 
 def tile_moe_pkd_mlp_relu2_kernel(
@@ -56,142 +61,89 @@ def tile_moe_pkd_mlp_relu2_kernel(
             keep.tile([P, PASSES * (SCALE_CUTS[c + 1] - SCALE_CUTS[c]), H], U8, name="w1s%d" % c, align_bytes=256)
             for c in range(len(SCALE_CUTS) - 1)
         ]
+        w2w = keep.tile([P, E, 2 * N], U8, name="w2w", align_bytes=256)
         w1s = {}
-        for c in range(len(SCALE_CUTS) - 1):
+        for c, tile in enumerate(w1s_t):
             for e in range(SCALE_CUTS[c], SCALE_CUTS[c + 1]):
                 for s in range(PASSES):
-                    w1s[e, s] = w1s_t[c][:, PASSES * (e - SCALE_CUTS[c]) + s, :]
-
-        def shared(slot, shape, dtype, name):
-            return turns.tile(shape, dtype, name=name, tag=slot, align_bytes=256)
-
-        def zero(plane, engine):
-            engine.memset(plane[:].rearrange("p a c -> p (a c)").bitcast(I32), 0)
-
-        def load_scales(plane, src, queue):
-            for q in (0, 2, 1, 3):
-                queue.dma_start(
-                    out=plane[32 * q : 32 * q + 4, :, :].bitcast(I32),
-                    in_=src[:, 4 * q : 4 * q + 4, :].rearrange("a r c -> r a c").bitcast(I32),
-                )
-
-        w1_planes = w1_scales.rearrange("e s q i -> (e s) q i")
-
-        def load_w1s(c, queue):
-            load_scales(w1s_t[c], w1_planes[PASSES * SCALE_CUTS[c] : PASSES * SCALE_CUTS[c + 1]], queue)
-
+                    w1s[e, s] = tile[:, PASSES * (e - SCALE_CUTS[c]) + s, :]
         w1w = {}
-        w2w = keep.tile([P, E, 2 * N], U8, name="w2w", align_bytes=256)
-
-        def load_w1(c, slot, queue):
-            e0, e1 = W1_CUTS[c], W1_CUTS[c + 1]
-            tile = shared(slot, [P, PASSES * (e1 - e0), 2 * H], U8, "w1_%d" % c)
-            for e in range(e0, e1):
-                for s in range(PASSES):
-                    w1w[e, s] = tile[:, PASSES * (e - e0) + s, :]
-            queue.dma_start(
-                out=tile[:].bitcast(I32), in_=w1_words[e0:e1].rearrange("e s p b -> p (e s) b").bitcast(I32)
-            )
-
-        def load_w2(queue):
-            queue.dma_start(out=w2w[:].bitcast(I32), in_=w2_words.rearrange("e s p b -> p (e s) b").bitcast(I32))
-
-        def load_w2s(queue):
-            load_scales(w2s, w2_scales.rearrange("e s q n -> (e s) q n"), queue)
-
-        def load_pos():
-            for r, src in enumerate((pos1, pos2, pos3)):
-                nc.sync.dma_start(pos_t[r][:], src)
-
+        xg = {}
+        sg0 = {}
+        relu_t = {}
         g = {}
 
-        def load_gate(a, slot):
-            g[a] = shared(slot, [P, TOP, T], F32, "g%d" % a)
-            nc.sync.dma_start(out=g[a][:], in_=gate[:, a * P : (a + 1) * P, :].rearrange("r p t -> p r t"))
-
-        warm = shared("b", [P, 8], F32, "warm")
-        nc.vector.memset(xs[:].bitcast(I32), 0)
-        zero(w1s_t[0], nc.vector)
-        nc.vector.memset(warm[:], 0.0)
-        nc.vector.memset(sg1[:].bitcast(I32), 0)
-        nc.scalar.activation(out=warm[:, 0:1], in_=warm[:, 1:2], func=ACT.Relu)
-        make_identity(nc, ident[:])
-        zero(w1s_t[1], nc.gpsimd)
-        zero(w2s, nc.gpsimd)
-
-        nc.sync.dma_start(offs_t[:], offs)
-        for q in range(4):
-            nc.sync.dma_start(
-                out=xs[32 * q : 32 * q + 8, :].bitcast(I32), in_=x_scales[:, 4 * q : 4 * q + 4, :].bitcast(I32)
-            )
-        for s in range(PASSES):
-            nc.sync.dma_start(out=xw[s][:], in_=x_words[s].rearrange("p t r -> p (t r)").bitcast(I32))
-        load_w1(0, "a", nc.sync)
-        load_w1s(0, nc.sync)
-
-        xg = {}
-        sg = {}
-        relu_t = {}
-
-        def gather_words(e):
-            xg[e] = ring.tile([P, PASSES, C], U32, name="xg", bufs=3, align_bytes=256)
-            o = offs_t[:, e * C // 16 : (e + 1) * C // 16]
-            for s in range(PASSES):
-                nc.vector.tensor_copy(xg[e][:, s, :], xw[s][:].bitcast(U32).indirect(o))
-
-        def gather_bytes(c, slot):
-            j0, j1 = BYTE_CUTS[c], BYTE_CUTS[c + 1]
-            tile = shared(slot, [P, j1 - j0], U8, "sg%d" % c)
-            for u in range(j0 // P, j1 // P):
-                sg[u] = tile[:, u * P - j0 : (u + 1) * P - j0]
-            nc.vector.tensor_copy(tile[:], xs[:].indirect(offs_t[:, j0 // 16 : j1 // 16]))
-            nc.sync.dma_start(out=sg1[0:MOVED, j0:j1].bitcast(I32), in_=tile[4 : 4 + MOVED, :].bitcast(I32))
-
-        def layer2(a, j0, j1, bank):
-            for lo in range(j0, j1, C):
-                hi = min(lo + C, j1)
-                e = lo // C
-                nc.tensor.matmul_mx(
-                    out=bank[:, lo - j0 : hi - j0],
-                    lhsT=w2w[:, e, a * N : (a + 1) * N].bitcast(FP4X4),
-                    lhsT_scale=w2s[:, e, a * P : (a + 1) * P],
-                    rhs=hq[:, lo:hi].bitcast(FP8X4),
-                    rhs_scale=hs[:, lo:hi],
-                    start=True,
-                    stop=True,
-                )
-            nc.scalar.copy(out=y[a][:, j0:j1], in_=bank[:, : j1 - j0])
+        def shared(place, shape, dtype, name):
+            return turns.tile(shape, dtype, name=name, tag=place, align_bytes=256)
 
         def bank(pool):
             return pool.tile([P, H], F32, name="bank")[:]
 
+        def zero(planes, engine):
+            engine.memset(planes[:].rearrange("p a c -> p (a c)").bitcast(I32), 0)
+
+        def load_scales(planes, src):
+            for q in (0, 2, 1, 3):
+                nc.sync.dma_start(
+                    out=planes[32 * q : 32 * q + 4, :, :].bitcast(I32),
+                    in_=src[:, 4 * q : 4 * q + 4, :].rearrange("a r c -> r a c").bitcast(I32),
+                )
+
+        def load_w1s(c):
+            rows = w1_scales.rearrange("e s q i -> (e s) q i")
+            load_scales(w1s_t[c], rows[PASSES * SCALE_CUTS[c] : PASSES * SCALE_CUTS[c + 1]])
+
+        def load_w1(c):
+            e0, e1 = W1_CUTS[c], W1_CUTS[c + 1]
+            tile = shared(("a", "b")[c % 2], [P, PASSES * (e1 - e0), 2 * H], U8, "w1_%d" % c)
+            for e in range(e0, e1):
+                for s in range(PASSES):
+                    w1w[e, s] = tile[:, PASSES * (e - e0) + s, :]
+            nc.sync.dma_start(
+                out=tile[:].bitcast(I32), in_=w1_words[e0:e1].rearrange("e s p b -> p (e s) b").bitcast(I32)
+            )
+
+        def load_gate(a, place):
+            g[a] = shared(place, [P, TOP, T], F32, "g%d" % a)
+            nc.sync.dma_start(out=g[a][:], in_=gate[:, a * P : (a + 1) * P, :].rearrange("r p t -> p r t"))
+
+        def gather_words(e):
+            xg[e] = ring.tile([P, PASSES, C], U32, name="xg", bufs=WORDS_AHEAD, align_bytes=256)
+            entries = offs_t[:, e * C // 16 : (e + 1) * C // 16]
+            for s in range(PASSES):
+                nc.vector.tensor_copy(xg[e][:, s, :], xw[s][:].bitcast(U32).indirect(entries))
+
+        def gather_bytes(c):
+            j0, j1 = BYTE_CUTS[c], BYTE_CUTS[c + 1]
+            tile = shared("s%d" % (c % 2), [P, j1 - j0], U8, "sg%d" % c)
+            for u in range(j0 // P, j1 // P):
+                sg0[u] = tile[:, u * P - j0 : (u + 1) * P - j0]
+            nc.vector.tensor_copy(tile[:], xs[:].indirect(offs_t[:, j0 // 16 : j1 // 16]))
+            nc.sync.dma_start(out=sg1[0:MOVED, j0:j1].bitcast(I32), in_=tile[4 : 4 + MOVED, :].bitcast(I32))
+
         def layer1(e):
             acc = [bank(ps_a) for half in range(2)]
-            for s, half in ((0, 0), (0, 1), (1, 0), (1, 1)):
-                u = 2 * e + half
-                nc.tensor.matmul_mx(
-                    out=acc[half],
-                    lhsT=xg[e][:, s, half * P : (half + 1) * P].bitcast(FP8X4),
-                    lhsT_scale=(sg[u], sg1[:, u * P : (u + 1) * P])[s],
-                    rhs=w1w[e, s].bitcast(FP4X4),
-                    rhs_scale=w1s[e, s],
-                    start=(s == 0),
-                    stop=(s == PASSES - 1),
-                )
+            for s in range(PASSES):
+                for half in range(2):
+                    u = 2 * e + half
+                    nc.tensor.matmul_mx(
+                        out=acc[half],
+                        lhsT=xg[e][:, s, half * P : (half + 1) * P].bitcast(FP8X4),
+                        lhsT_scale=(sg0[u], sg1[:, u * P : (u + 1) * P])[s],
+                        rhs=w1w[e, s].bitcast(FP4X4),
+                        rhs_scale=w1s[e, s],
+                        start=(s == 0),
+                        stop=(s == PASSES - 1),
+                    )
             for half in range(2):
                 u = 2 * e + half
                 relu_t[u] = ring.tile([P, 4, P], F32, name="r_t", bufs=4, align_bytes=64)
-                view = acc[half].rearrange("j (c i t) -> j c t i", i=4, t=4)
-                dst = relu_t[u][:].rearrange("j t (c i) -> j c t i", i=4)
+                src = acc[half].rearrange("j (c d t) -> j c t d", d=4, t=4)
+                dst = relu_t[u][:].rearrange("j t (c d) -> j c t d", d=4)
                 if u in RELU_ON_VECTOR:
-                    nc.vector.tensor_scalar_max(dst, view, 0.0)
+                    nc.vector.tensor_scalar_max(dst, src, 0.0)
                 else:
-                    nc.scalar.activation(out=dst, in_=view, func=ACT.Relu)
-
-        def quantise(j0, j1):
-            nc.vector.quantize_mx(
-                out=hq[:, j0:j1].bitcast(FP8X4), scales=hs[:, j0:j1], in_=hb[:, j0:j1, :].rearrange("p j t -> p (j t)")
-            )
+                    nc.scalar.activation(out=dst, in_=src, func=ACT.Relu)
 
         def turn(u, pool):
             turned = bank(pool).rearrange("p (t j) -> p t j", t=4)
@@ -201,69 +153,101 @@ def tile_moe_pkd_mlp_relu2_kernel(
                 out=hb[:, u * P : (u + 1) * P, :], in_=turned.rearrange("p t j -> p j t"), func=ACT.Square
             )
 
-        gather_bytes(0, "s0")
-        gather_bytes(1, "s1")
-        gather_words(0)
-        gather_words(1)
-        gather_words(2)
-        load_w1(1, "b", nc.sync)
-        load_w1s(1, nc.sync)
-        for k in range(E):
-            if k == 1:
-                gather_words(3)
-            if k == 2:
-                gather_bytes(2, "s0")
-                gather_words(4)
-                load_w1(2, "a", nc.sync)
-            if k == 3:
-                gather_bytes(3, "s1")
-                gather_words(5)
-                load_w2s(nc.sync)
-                load_w2(nc.sync)
-            if k == 4:
-                gather_words(6)
-                load_w1(3, "b", nc.sync)
-            if k == 5:
-                gather_bytes(4, "s0")
-                gather_words(7)
-                load_pos()
-            if k == 6:
-                gather_words(8)
-            if k == 7:
+        def quantise(j0, j1):
+            nc.vector.quantize_mx(
+                out=hq[:, j0:j1].bitcast(FP8X4), scales=hs[:, j0:j1], in_=hb[:, j0:j1, :].rearrange("p j t -> p (j t)")
+            )
+
+        def layer2(a, j0, j1, pool, copy):
+            acc = bank(pool)
+            for lo in range(j0, j1, C):
+                hi = min(lo + C, j1)
+                e = lo // C
+                nc.tensor.matmul_mx(
+                    out=acc[:, lo - j0 : hi - j0],
+                    lhsT=w2w[:, e, a * N : (a + 1) * N].bitcast(FP4X4),
+                    lhsT_scale=w2s[:, e, a * P : (a + 1) * P],
+                    rhs=hq[:, lo:hi].bitcast(FP8X4),
+                    rhs_scale=hs[:, lo:hi],
+                    start=True,
+                    stop=True,
+                )
+            copy(y[a][:, j0:j1], acc[:, : j1 - j0])
+
+        nc.vector.memset(xs[:].bitcast(I32), 0)
+        zero(w1s_t[0], nc.vector)
+        nc.vector.memset(sg1[:].bitcast(I32), 0)
+        ident_src = shared("b", [P, P], F32, "ident_src")
+        make_identity(nc, ident_src[:])
+        nc.scalar.activation(out=ident[:], in_=ident_src[:], func=ACT.Relu)
+        zero(w1s_t[1], nc.vector)
+        zero(w2s, nc.gpsimd)
+
+        nc.sync.dma_start(offs_t[:], offs)
+        for q in range(4):
+            nc.sync.dma_start(
+                out=xs[32 * q : 32 * q + 8, :].bitcast(I32), in_=x_scales[:, 4 * q : 4 * q + 4, :].bitcast(I32)
+            )
+        for s in range(PASSES):
+            nc.sync.dma_start(out=xw[s][:], in_=x_words[s].rearrange("p t r -> p (t r)").bitcast(I32))
+        load_w1(0)
+        load_w1s(0)
+        gather_bytes(0)
+        gather_bytes(1)
+        for e in range(WORDS_AHEAD):
+            gather_words(e)
+        load_w1(1)
+        load_w1s(1)
+
+        for e in range(E):
+            if e in BYTES_IN_ROUND:
+                gather_bytes(BYTES_IN_ROUND[e])
+            if 1 <= e <= E - WORDS_AHEAD:
+                gather_words(e + WORDS_AHEAD - 1)
+            if e in W1_IN_ROUND:
+                load_w1(W1_IN_ROUND[e])
+            if e == W2_ROUND:
+                load_scales(w2s, w2_scales.rearrange("e s q n -> (e s) q n"))
+                nc.sync.dma_start(out=w2w[:].bitcast(I32), in_=w2_words.rearrange("e s p b -> p (e s) b").bitcast(I32))
+            if e == LISTS_ROUND:
+                for r, src in enumerate((pos1, pos2, pos3)):
+                    nc.sync.dma_start(pos_t[r][:], src)
+            if e == GATE_ROUND:
                 load_gate(0, "a")
                 load_gate(1, "s1")
-            layer1(k)
-            if k >= 1:
-                turn(2 * k - 2, ps_t)
-                turn(2 * k - 1, ps_t)
-                quantise((k - 1) * C, k * C)
-            if k in LAYER2_IN_ROUND:
-                layer2(0, LAYER2_IN_ROUND[k][0] * C, LAYER2_IN_ROUND[k][1] * C, bank(ps_y))
+            layer1(e)
+            if e >= 1:
+                turn(2 * e - 2, ps_t)
+                turn(2 * e - 1, ps_t)
+                quantise((e - 1) * C, e * C)
+            if LAYER2_FROM <= e < E - 1:
+                pair = e - LAYER2_FROM
+                layer2(0, 2 * pair * C, (2 * pair + 2) * C, ps_y, nc.scalar.copy)
+
         turn(2 * E - 2, ps_a)
         turn(2 * E - 1, ps_a)
-        layer2(0, 6 * C, 8 * C, bank(ps_y))
+        layer2(0, S - 3 * C, S - C, ps_y, nc.scalar.copy)
         for lo in (S - C, S - P):
             quantise(lo, lo + P)
-            layer2(0, lo, lo + P, bank(ps_t))
+            layer2(0, lo, lo + P, ps_t, nc.vector.tensor_copy)
         for j0 in range(0, S, 2 * C):
-            layer2(1, j0, min(j0 + 2 * C, S), bank(ps_a))
+            layer2(1, j0, min(j0 + 2 * C, S), ps_a, nc.scalar.copy)
 
         prod = [[keep.tile([P, T], F32, name="prod%d_%d" % (a, r), align_bytes=64) for r in range(TOP)] for a in range(2)]
         sum_t = keep.tile([P, T], F32, name="sum_t", align_bytes=64)
         part = keep.tile([P, T], F32, name="part", align_bytes=64)
         res = [keep.tile([P, T], F32, name="res%d" % a, align_bytes=64) for a in range(2)]
-        HALF = T // 2
 
         def product(a, r, t0, t1):
             nc.vector.tensor_tensor(
                 prod[a][r][:, t0:t1], y[a][:].indirect(pos_t[r][:, t0 // 16 : t1 // 16]), g[a][:, r, t0:t1], ALU.mult
             )
 
-        for t0 in range(0, T, HALF):
+        for t0 in range(0, T, HALF_T):
             for r in range(TOP):
-                product(0, r, t0, t0 + HALF)
-            sums = bank(ps_t)[:, :HALF]
-            for lo in range(0, HALF, P):
+                product(0, r, t0, t0 + HALF_T)
+            sums = bank(ps_t)[:, :HALF_T]
+            for lo in range(0, HALF_T, P):
                 for r in range(TOP):
                     nc.tensor.matmul(
                         sums[:, lo : lo + P],
@@ -273,19 +257,20 @@ def tile_moe_pkd_mlp_relu2_kernel(
                         start=(r == 0),
                         stop=(r == TOP - 1),
                     )
-            nc.scalar.copy(out=sum_t[:, t0 : t0 + HALF], in_=sums)
-            back = bank(ps_t)[:, :HALF]
-            for lo in range(0, HALF, P):
+            nc.scalar.copy(out=sum_t[:, t0 : t0 + HALF_T], in_=sums)
+            back = bank(ps_t)[:, :HALF_T]
+            for lo in range(0, HALF_T, P):
                 nc.tensor.transpose(back[:, lo : lo + P], sum_t[:, t0 + lo : t0 + lo + P], ident[:])
-            nc.scalar.copy(out=res[0][:, t0 : t0 + HALF], in_=back)
-            nc.scalar.dma_start(out=out[0:P, t0 : t0 + HALF], in_=res[0][:, t0 : t0 + HALF])
+            nc.scalar.copy(out=res[0][:, t0 : t0 + HALF_T], in_=back)
+            nc.scalar.dma_start(out=out[0:P, t0 : t0 + HALF_T], in_=res[0][:, t0 : t0 + HALF_T])
+
         product(1, 0, 0, T)
         product(1, 1, 0, T)
-        product(1, 2, 0, HALF)
+        product(1, 2, 0, HALF_T)
         nc.vector.tensor_tensor(part[:], prod[1][0][:], prod[1][1][:], ALU.add)
-        product(1, 2, HALF, T)
-        for t0 in range(0, T, HALF):
+        product(1, 2, HALF_T, T)
+        for t0 in range(0, T, HALF_T):
             nc.vector.tensor_tensor(
-                res[1][:, t0 : t0 + HALF], part[:, t0 : t0 + HALF], prod[1][2][:, t0 : t0 + HALF], ALU.add
+                res[1][:, t0 : t0 + HALF_T], part[:, t0 : t0 + HALF_T], prod[1][2][:, t0 : t0 + HALF_T], ALU.add
             )
-            nc.sync.dma_start(out=out[P:, t0 : t0 + HALF], in_=res[1][:, t0 : t0 + HALF])
+            nc.sync.dma_start(out=out[P:, t0 : t0 + HALF_T], in_=res[1][:, t0 : t0 + HALF_T])

@@ -22,16 +22,14 @@ FP4X4 = mybir.dt.float4_e2m1fn_x4
 ACT = mybir.ActivationFunctionType
 ALU = mybir.AluOpType
 
-BYTE_CUTS = (0, 384, 768, 1280, 1792, 2304)
-W1_CUTS = (0, 2, 4, 7, 9)
+BYTE_CUTS = (0, 512, 1024, 1536, 2048, 2304)
+EARLY = 2 * C
+WORD_CUTS = (512, 768, 1024, 1536, 2048, 2304)
+W1_CUTS = (0, 1, 2, 4, 6, 9)
 SCALE_CUTS = (0, 2, 9)
 MOVED = 112
-RELU_ON_VECTOR = (1, 10, 14, 15, 16, 17)
-WORDS_AHEAD = 3
-BYTES_IN_ROUND = {2: 2, 3: 3, 5: 4}
-W1_IN_ROUND = {2: 2, 4: 3}
-W2_ROUND, LISTS_ROUND, GATE_ROUND = 3, 5, 7
-LAYER2_FROM = 5
+RELU_ON_VECTOR = (12, 13, 14, 15)
+HELD = 6 * C
 
 
 def tile_moe_pkd_mlp_relu2_kernel(
@@ -42,9 +40,8 @@ def tile_moe_pkd_mlp_relu2_kernel(
         keep = ctx.enter_context(tc.tile_pool(name="keep", bufs=1))
         turns = ctx.enter_context(tc.tile_pool(name="turns", bufs=1))
         ring = ctx.enter_context(tc.tile_pool(name="ring", bufs=2))
-        ps_a = ctx.enter_context(tc.psum_pool(name="ps_a", bufs=4))
-        ps_t = ctx.enter_context(tc.psum_pool(name="ps_t", bufs=3))
-        ps_y = ctx.enter_context(tc.psum_pool(name="ps_y", bufs=1))
+        psum = ctx.enter_context(tc.psum_pool(name="psum", bufs=1))
+        banks = [psum.tile([P, H], F32, name="bank%d" % b)[:] for b in range(8)]
 
         offs_t = keep.tile([P, S // 16], U16, name="offs_t")
         pos_t = [keep.tile([P, T // 16], U16, name="pos_t%d" % r) for r in range(TOP)]
@@ -53,31 +50,30 @@ def tile_moe_pkd_mlp_relu2_kernel(
         w2s = keep.tile([P, E, N], U8, name="w2s", align_bytes=256)
         sg1 = keep.tile([P, S], U8, name="sg1", align_bytes=256)
         hb = keep.tile([P, S, 4], BF16, name="hb", align_bytes=256)
-        hq = keep.tile([P, S], U32, name="hq", align_bytes=256)
         hs = keep.tile([P, S], U8, name="hs", align_bytes=256)
         y = [keep.tile([P, S], F32, name="y%d" % a, align_bytes=64) for a in range(2)]
         ident = keep.tile([P, P], F32, name="ident", align_bytes=64)
+        ident_src = keep.tile([P, P], F32, name="ident_src", align_bytes=64)
         w1s_t = [
             keep.tile([P, PASSES * (SCALE_CUTS[c + 1] - SCALE_CUTS[c]), H], U8, name="w1s%d" % c, align_bytes=256)
             for c in range(len(SCALE_CUTS) - 1)
         ]
+        w1w_t = [
+            keep.tile([P, PASSES * (W1_CUTS[c + 1] - W1_CUTS[c]), 2 * H], U8, name="w1w%d" % c, align_bytes=256)
+            for c in range(len(W1_CUTS) - 1)
+        ]
         w2w = keep.tile([P, E, 2 * N], U8, name="w2w", align_bytes=256)
+        g = keep.tile([P, TOP, T], F32, name="g", align_bytes=64)
         w1s = {}
-        for c, tile in enumerate(w1s_t):
-            for e in range(SCALE_CUTS[c], SCALE_CUTS[c + 1]):
-                for s in range(PASSES):
-                    w1s[e, s] = tile[:, PASSES * (e - SCALE_CUTS[c]) + s, :]
         w1w = {}
+        for cuts, tiles, planes in ((SCALE_CUTS, w1s_t, w1s), (W1_CUTS, w1w_t, w1w)):
+            for c, tile in enumerate(tiles):
+                for e in range(cuts[c], cuts[c + 1]):
+                    for s in range(PASSES):
+                        planes[e, s] = tile[:, PASSES * (e - cuts[c]) + s, :]
         xg = {}
         sg0 = {}
         relu_t = {}
-        g = {}
-
-        def shared(place, shape, dtype, name):
-            return turns.tile(shape, dtype, name=name, tag=place, align_bytes=256)
-
-        def bank(pool):
-            return pool.tile([P, H], F32, name="bank")[:]
 
         def zero(planes, engine):
             engine.memset(planes[:].rearrange("p a c -> p (a c)").bitcast(I32), 0)
@@ -94,63 +90,61 @@ def tile_moe_pkd_mlp_relu2_kernel(
             load_scales(w1s_t[c], rows[PASSES * SCALE_CUTS[c] : PASSES * SCALE_CUTS[c + 1]])
 
         def load_w1(c):
-            e0, e1 = W1_CUTS[c], W1_CUTS[c + 1]
-            tile = shared(("a", "b")[c % 2], [P, PASSES * (e1 - e0), 2 * H], U8, "w1_%d" % c)
-            for e in range(e0, e1):
-                for s in range(PASSES):
-                    w1w[e, s] = tile[:, PASSES * (e - e0) + s, :]
             nc.sync.dma_start(
-                out=tile[:].bitcast(I32), in_=w1_words[e0:e1].rearrange("e s p b -> p (e s) b").bitcast(I32)
+                out=w1w_t[c][:].bitcast(I32),
+                in_=w1_words[W1_CUTS[c] : W1_CUTS[c + 1]].rearrange("e s p b -> p (e s) b").bitcast(I32),
             )
 
-        def load_gate(a, place):
-            g[a] = shared(place, [P, TOP, T], F32, "g%d" % a)
-            nc.sync.dma_start(out=g[a][:], in_=gate[:, a * P : (a + 1) * P, :].rearrange("r p t -> p r t"))
+        def load_words(s):
+            nc.sync.dma_start(out=xw[s][:], in_=x_words[s].rearrange("p t r -> p (t r)").bitcast(I32))
 
-        def gather_words(e):
-            xg[e] = ring.tile([P, PASSES, C], U32, name="xg", bufs=WORDS_AHEAD, align_bytes=256)
-            entries = offs_t[:, e * C // 16 : (e + 1) * C // 16]
-            for s in range(PASSES):
-                nc.vector.tensor_copy(xg[e][:, s, :], xw[s][:].bitcast(U32).indirect(entries))
-
-        def gather_bytes(c):
-            j0, j1 = BYTE_CUTS[c], BYTE_CUTS[c + 1]
-            tile = shared("s%d" % (c % 2), [P, j1 - j0], U8, "sg%d" % c)
+        def gather_words(s, j0, j1, dst):
             for u in range(j0 // P, j1 // P):
-                sg0[u] = tile[:, u * P - j0 : (u + 1) * P - j0]
-            nc.vector.tensor_copy(tile[:], xs[:].indirect(offs_t[:, j0 // 16 : j1 // 16]))
-            nc.sync.dma_start(out=sg1[0:MOVED, j0:j1].bitcast(I32), in_=tile[4 : 4 + MOVED, :].bitcast(I32))
+                xg[u, s] = dst[:, u * P - j0 : (u + 1) * P - j0]
+            nc.vector.tensor_copy(dst, xw[s][:].bitcast(U32).indirect(offs_t[:, j0 // 16 : j1 // 16]))
 
-        def layer1(e):
-            acc = [bank(ps_a) for half in range(2)]
+        def gather_bytes(c, dst):
+            j0, j1 = BYTE_CUTS[c], BYTE_CUTS[c + 1]
+            for u in range(j0 // P, j1 // P):
+                sg0[u] = dst[:, u * P - j0 : (u + 1) * P - j0]
+            nc.vector.tensor_copy(dst, xs[:].indirect(offs_t[:, j0 // 16 : j1 // 16]))
+
+        def move_bytes(c, src):
+            j0, j1 = BYTE_CUTS[c], BYTE_CUTS[c + 1]
+            for p0, p1 in ((0, 64), (64, 96), (96, 100)) if c == 0 else ((0, MOVED),):
+                nc.sync.dma_start(out=sg1[p0:p1, j0:j1].bitcast(I32), in_=src[4 + p0 : 4 + p1, :].bitcast(I32))
+
+        def layer1(u):
             for s in range(PASSES):
-                for half in range(2):
-                    u = 2 * e + half
-                    nc.tensor.matmul_mx(
-                        out=acc[half],
-                        lhsT=xg[e][:, s, half * P : (half + 1) * P].bitcast(FP8X4),
-                        lhsT_scale=(sg0[u], sg1[:, u * P : (u + 1) * P])[s],
-                        rhs=w1w[e, s].bitcast(FP4X4),
-                        rhs_scale=w1s[e, s],
-                        start=(s == 0),
-                        stop=(s == PASSES - 1),
-                    )
-            for half in range(2):
-                u = 2 * e + half
-                relu_t[u] = ring.tile([P, 4, P], F32, name="r_t", bufs=4, align_bytes=64)
-                src = acc[half].rearrange("j (c d t) -> j c t d", d=4, t=4)
-                dst = relu_t[u][:].rearrange("j t (c d) -> j c t d", d=4)
-                if u in RELU_ON_VECTOR:
-                    nc.vector.tensor_scalar_max(dst, src, 0.0)
-                else:
-                    nc.scalar.activation(out=dst, in_=src, func=ACT.Relu)
+                nc.tensor.matmul_mx(
+                    out=banks[u % 4],
+                    lhsT=xg[u, s].bitcast(FP8X4),
+                    lhsT_scale=(sg0[u], sg1[:, u * P : (u + 1) * P])[s],
+                    rhs=w1w[u // 2, s].bitcast(FP4X4),
+                    rhs_scale=w1s[u // 2, s],
+                    start=(s == 0),
+                    stop=(s == PASSES - 1),
+                )
 
-        def turn(u, pool):
-            turned = bank(pool).rearrange("p (t j) -> p t j", t=4)
+        def relu(u):
+            relu_t[u] = ring.tile([P, 4, P], F32, name="r_t", bufs=4, align_bytes=64)
+            src = banks[u % 4].rearrange("j (c d t) -> j c t d", d=4, t=4)
+            dst = relu_t[u][:].rearrange("j t (c d) -> j c t d", d=4)
+            if u in RELU_ON_VECTOR:
+                nc.vector.tensor_scalar_max(dst, src, 0.0)
+            else:
+                nc.scalar.activation(out=dst, in_=src, func=ACT.Relu)
+
+        def turned(u):
+            return banks[4 + u % 4].rearrange("p (t j) -> p t j", t=4)
+
+        def turn(u):
             for t in range(4):
-                nc.tensor.transpose(turned[:, t, :], relu_t[u][:, t, :], ident[:])
+                nc.tensor.transpose(turned(u)[:, t, :], relu_t[u][:, t, :], ident[:])
+
+        def square(u):
             nc.scalar.activation(
-                out=hb[:, u * P : (u + 1) * P, :], in_=turned.rearrange("p t j -> p j t"), func=ACT.Square
+                out=hb[:, u * P : (u + 1) * P, :], in_=turned(u).rearrange("p t j -> p j t"), func=ACT.Square
             )
 
         def quantise(j0, j1):
@@ -158,8 +152,7 @@ def tile_moe_pkd_mlp_relu2_kernel(
                 out=hq[:, j0:j1].bitcast(FP8X4), scales=hs[:, j0:j1], in_=hb[:, j0:j1, :].rearrange("p j t -> p (j t)")
             )
 
-        def layer2(a, j0, j1, pool, copy):
-            acc = bank(pool)
+        def layer2(a, j0, j1, acc, copy):
             for lo in range(j0, j1, C):
                 hi = min(lo + C, j1)
                 e = lo // C
@@ -174,10 +167,9 @@ def tile_moe_pkd_mlp_relu2_kernel(
                 )
             copy(y[a][:, j0:j1], acc[:, : j1 - j0])
 
-        nc.vector.memset(xs[:].bitcast(I32), 0)
+        nc.gpsimd.memset(xs[:].bitcast(I32), 0)
         zero(w1s_t[0], nc.vector)
         nc.vector.memset(sg1[:].bitcast(I32), 0)
-        ident_src = shared("b", [P, P], F32, "ident_src")
         make_identity(nc, ident_src[:])
         nc.scalar.activation(out=ident[:], in_=ident_src[:], func=ACT.Relu)
         zero(w1s_t[1], nc.vector)
@@ -188,50 +180,84 @@ def tile_moe_pkd_mlp_relu2_kernel(
             nc.sync.dma_start(
                 out=xs[32 * q : 32 * q + 8, :].bitcast(I32), in_=x_scales[:, 4 * q : 4 * q + 4, :].bitcast(I32)
             )
-        for s in range(PASSES):
-            nc.sync.dma_start(out=xw[s][:], in_=x_words[s].rearrange("p t r -> p (t r)").bitcast(I32))
+        load_words(0)
         load_w1(0)
         load_w1s(0)
-        gather_bytes(0)
-        gather_bytes(1)
-        for e in range(WORDS_AHEAD):
-            gather_words(e)
+        load_words(1)
+
+        sg_early = turns.tile([P, EARLY], U8, name="sg_early", tag="held", align_bytes=256)
+        gather_bytes(0, sg_early[:])
+        move_bytes(0, sg_early)
         load_w1(1)
+        for s, places in enumerate((("first", "second"), ("planes", "words"))):
+            for u, place in enumerate(places):
+                tile = turns.tile([P, P], U32, name="xg_first", tag=place, align_bytes=256)
+                gather_words(s, u * P, (u + 1) * P, tile[:])
+        xg_early = keep.tile([P, PASSES, C], U32, name="xg_early", align_bytes=256)
+        for s in range(PASSES):
+            gather_words(s, C, 2 * C, xg_early[:, s, :])
+        for u in range(EARLY // P):
+            layer1(u)
+
+        xg_late = turns.tile([P, PASSES, S - EARLY], U32, name="xg_late", tag="words", align_bytes=256)
+        sg_late = turns.tile([P, S - EARLY], U8, name="sg_late", tag="planes", align_bytes=256)
+        for c in range(len(WORD_CUTS) - 1):
+            j0, j1 = WORD_CUTS[c], WORD_CUTS[c + 1]
+            if j0 in BYTE_CUTS:
+                b = BYTE_CUTS.index(j0)
+                gather_bytes(b, sg_late[:, j0 - EARLY : BYTE_CUTS[b + 1] - EARLY])
+            if j0 == HELD:
+                xg_held = turns.tile([P, PASSES, j1 - j0], U32, name="xg_held", tag="held", align_bytes=256)
+            for s in range(PASSES):
+                dst = xg_held[:, s, :] if j0 == HELD else xg_late[:, s, j0 - EARLY : j1 - EARLY]
+                gather_words(s, j0, j1, dst)
+
+        def move_late(b):
+            move_bytes(b, sg_late[:, BYTE_CUTS[b] - EARLY : BYTE_CUTS[b + 1] - EARLY])
+
+        load_w1(2)
         load_w1s(1)
+        move_late(1)
+        load_w1(3)
+        load_w1(4)
+        move_late(2)
+        load_scales(w2s, w2_scales.rearrange("e s q n -> (e s) q n"))
+        nc.sync.dma_start(out=w2w[:].bitcast(I32), in_=w2_words.rearrange("e s p b -> p (e s) b").bitcast(I32))
+        for r, src in enumerate((pos1, pos2, pos3)):
+            nc.sync.dma_start(pos_t[r][:], src)
+        nc.sync.dma_start(out=g[:], in_=gate[:, 0:P, :].rearrange("r p t -> p r t"))
+        move_late(3)
+        move_late(4)
 
-        for e in range(E):
-            if e in BYTES_IN_ROUND:
-                gather_bytes(BYTES_IN_ROUND[e])
-            if 1 <= e <= E - WORDS_AHEAD:
-                gather_words(e + WORDS_AHEAD - 1)
-            if e in W1_IN_ROUND:
-                load_w1(W1_IN_ROUND[e])
-            if e == W2_ROUND:
-                load_scales(w2s, w2_scales.rearrange("e s q n -> (e s) q n"))
-                nc.sync.dma_start(out=w2w[:].bitcast(I32), in_=w2_words.rearrange("e s p b -> p (e s) b").bitcast(I32))
-            if e == LISTS_ROUND:
-                for r, src in enumerate((pos1, pos2, pos3)):
-                    nc.sync.dma_start(pos_t[r][:], src)
-            if e == GATE_ROUND:
-                load_gate(0, "a")
-                load_gate(1, "s1")
-            layer1(e)
+        for e in range(E + 1):
             if e >= 1:
-                turn(2 * e - 2, ps_t)
-                turn(2 * e - 1, ps_t)
-                quantise((e - 1) * C, e * C)
-            if LAYER2_FROM <= e < E - 1:
-                pair = e - LAYER2_FROM
-                layer2(0, 2 * pair * C, (2 * pair + 2) * C, ps_y, nc.scalar.copy)
+                turn(2 * e - 2)
+                turn(2 * e - 1)
+            if 1 <= e < E - 1:
+                layer1(2 * e + 2)
+                layer1(2 * e + 3)
+            if e < E:
+                relu(2 * e)
+                relu(2 * e + 1)
+            if 1 <= e < E:
+                square(2 * e - 2)
+                square(2 * e - 1)
+            if e == E - 2:
+                hq = turns.tile([P, S], U32, name="hq", tag="held", align_bytes=256)
+                for pair in range(3):
+                    quantise(2 * pair * C, (2 * pair + 2) * C)
+                    layer2(0, 2 * pair * C, (2 * pair + 2) * C, banks[2 + pair % 2], nc.vector.tensor_copy)
+                quantise(6 * C, 7 * C)
+            if e == E - 1:
+                quantise(7 * C, 8 * C)
 
-        turn(2 * E - 2, ps_a)
-        turn(2 * E - 1, ps_a)
-        layer2(0, S - 3 * C, S - C, ps_y, nc.scalar.copy)
-        for lo in (S - C, S - P):
-            quantise(lo, lo + P)
-            layer2(0, lo, lo + P, ps_t, nc.vector.tensor_copy)
-        for j0 in range(0, S, 2 * C):
-            layer2(1, j0, min(j0 + 2 * C, S), ps_a, nc.scalar.copy)
+        for u in (2 * E - 2, 2 * E - 1):
+            square(u)
+            quantise(u * P, (u + 1) * P)
+            layer2(0, u * P, (u + 1) * P, banks[1 + 2 * (u % 2)], nc.vector.tensor_copy)
+        layer2(0, 6 * C, 8 * C, banks[0], nc.scalar.copy)
+        for k, j0 in enumerate(range(0, S, 2 * C)):
+            layer2(1, j0, min(j0 + 2 * C, S), banks[(6, 7, 4, 5, 2)[k]], nc.scalar.copy)
 
         prod = [[keep.tile([P, T], F32, name="prod%d_%d" % (a, r), align_bytes=64) for r in range(TOP)] for a in range(2)]
         sum_t = keep.tile([P, T], F32, name="sum_t", align_bytes=64)
@@ -240,13 +266,13 @@ def tile_moe_pkd_mlp_relu2_kernel(
 
         def product(a, r, t0, t1):
             nc.vector.tensor_tensor(
-                prod[a][r][:, t0:t1], y[a][:].indirect(pos_t[r][:, t0 // 16 : t1 // 16]), g[a][:, r, t0:t1], ALU.mult
+                prod[a][r][:, t0:t1], y[a][:].indirect(pos_t[r][:, t0 // 16 : t1 // 16]), g[:, r, t0:t1], ALU.mult
             )
 
-        for t0 in range(0, T, HALF_T):
+        for k, t0 in enumerate(range(0, T, HALF_T)):
             for r in range(TOP):
                 product(0, r, t0, t0 + HALF_T)
-            sums = bank(ps_t)[:, :HALF_T]
+            sums = banks[2 * k][:, :HALF_T]
             for lo in range(0, HALF_T, P):
                 for r in range(TOP):
                     nc.tensor.matmul(
@@ -258,7 +284,7 @@ def tile_moe_pkd_mlp_relu2_kernel(
                         stop=(r == TOP - 1),
                     )
             nc.scalar.copy(out=sum_t[:, t0 : t0 + HALF_T], in_=sums)
-            back = bank(ps_t)[:, :HALF_T]
+            back = banks[1 + 2 * k][:, :HALF_T]
             for lo in range(0, HALF_T, P):
                 nc.tensor.transpose(back[:, lo : lo + P], sum_t[:, t0 + lo : t0 + lo + P], ident[:])
             nc.scalar.copy(out=res[0][:, t0 : t0 + HALF_T], in_=back)

@@ -30,6 +30,8 @@ SCALE_CUTS = (0, 2, 9)
 MOVED = 112
 RELU_ON_VECTOR = (12, 13, 14, 15)
 HELD = 6 * C
+DIRECT_FROM = HALF_T
+SUMMED = ((0, 0, HALF_T), (0, HALF_T, T), (1, 0, HALF_T))
 
 
 def tile_moe_pkd_mlp_relu2_kernel(
@@ -111,7 +113,7 @@ def tile_moe_pkd_mlp_relu2_kernel(
 
         def move_bytes(c, src):
             j0, j1 = BYTE_CUTS[c], BYTE_CUTS[c + 1]
-            for p0, p1 in ((0, 64), (64, 96), (96, 100)) if c == 0 else ((0, MOVED),):
+            for p0, p1 in ((0, 64), (64, 96), (96, 100)) if c <= 1 else ((0, MOVED),):
                 nc.sync.dma_start(out=sg1[p0:p1, j0:j1].bitcast(I32), in_=src[4 + p0 : 4 + p1, :].bitcast(I32))
 
         def layer1(u):
@@ -181,21 +183,20 @@ def tile_moe_pkd_mlp_relu2_kernel(
                 out=xs[32 * q : 32 * q + 8, :].bitcast(I32), in_=x_scales[:, 4 * q : 4 * q + 4, :].bitcast(I32)
             )
         load_words(0)
+        load_words(1)
         load_w1(0)
         load_w1s(0)
-        load_words(1)
 
         sg_early = turns.tile([P, EARLY], U8, name="sg_early", tag="held", align_bytes=256)
         gather_bytes(0, sg_early[:])
         move_bytes(0, sg_early)
         load_w1(1)
-        for s, places in enumerate((("first", "second"), ("planes", "words"))):
-            for u, place in enumerate(places):
-                tile = turns.tile([P, P], U32, name="xg_first", tag=place, align_bytes=256)
-                gather_words(s, u * P, (u + 1) * P, tile[:])
-        xg_early = keep.tile([P, PASSES, C], U32, name="xg_early", align_bytes=256)
-        for s in range(PASSES):
-            gather_words(s, C, 2 * C, xg_early[:, s, :])
+        for u, place in enumerate(("planes", "words")):
+            gather_words(0, u * P, (u + 1) * P, turns.tile([P, P], U32, name="xg_first", tag=place, align_bytes=256)[:])
+        xg_early = keep.tile([P, 3, C], U32, name="xg_early", align_bytes=256)
+        gather_words(1, 0, C, xg_early[:, 0, :])
+        gather_words(0, C, 2 * C, xg_early[:, 1, :])
+        gather_words(1, C, 2 * C, xg_early[:, 2, :])
         for u in range(EARLY // P):
             layer1(u)
 
@@ -246,21 +247,23 @@ def tile_moe_pkd_mlp_relu2_kernel(
                 hq = turns.tile([P, S], U32, name="hq", tag="held", align_bytes=256)
                 for pair in range(3):
                     quantise(2 * pair * C, (2 * pair + 2) * C)
-                    layer2(0, 2 * pair * C, (2 * pair + 2) * C, banks[2 + pair % 2], nc.vector.tensor_copy)
                 quantise(6 * C, 7 * C)
+                for pair in range(2):
+                    layer2(0, 2 * pair * C, (2 * pair + 2) * C, banks[2 + pair], nc.vector.tensor_copy)
             if e == E - 1:
                 quantise(7 * C, 8 * C)
 
         for u in (2 * E - 2, 2 * E - 1):
             square(u)
             quantise(u * P, (u + 1) * P)
-            layer2(0, u * P, (u + 1) * P, banks[1 + 2 * (u % 2)], nc.vector.tensor_copy)
-        layer2(0, 6 * C, 8 * C, banks[0], nc.scalar.copy)
+            layer2(0, u * P, (u + 1) * P, banks[2 + u % 2], nc.vector.tensor_copy)
+        for pair in (2, 3):
+            layer2(0, 2 * pair * C, (2 * pair + 2) * C, banks[pair % 2], nc.scalar.copy)
         for k, j0 in enumerate(range(0, S, 2 * C)):
             layer2(1, j0, min(j0 + 2 * C, S), banks[(6, 7, 4, 5, 2)[k]], nc.scalar.copy)
 
         prod = [[keep.tile([P, T], F32, name="prod%d_%d" % (a, r), align_bytes=64) for r in range(TOP)] for a in range(2)]
-        sum_t = keep.tile([P, T], F32, name="sum_t", align_bytes=64)
+        sum_t = [keep.tile([P, T], F32, name="sum_t%d" % a, align_bytes=64) for a in range(2)]
         part = keep.tile([P, T], F32, name="part", align_bytes=64)
         res = [keep.tile([P, T], F32, name="res%d" % a, align_bytes=64) for a in range(2)]
 
@@ -269,34 +272,31 @@ def tile_moe_pkd_mlp_relu2_kernel(
                 prod[a][r][:, t0:t1], y[a][:].indirect(pos_t[r][:, t0 // 16 : t1 // 16]), g[:, r, t0:t1], ALU.mult
             )
 
-        for k, t0 in enumerate(range(0, T, HALF_T)):
+        for (a, t0, t1), (sum_banks, back_bank) in zip(SUMMED, (((2, 0, 1), 3), ((4, 5, 6), 7), ((0, 1, 2), 3))):
             for r in range(TOP):
-                product(0, r, t0, t0 + HALF_T)
-            sums = banks[2 * k][:, :HALF_T]
-            for lo in range(0, HALF_T, P):
-                for r in range(TOP):
+                product(a, r, t0, t1)
+                for lo, b in zip(range(t0, t1, P), sum_banks):
                     nc.tensor.matmul(
-                        sums[:, lo : lo + P],
-                        lhsT=prod[0][r][:, t0 + lo : t0 + lo + P],
+                        banks[b][:, :P],
+                        lhsT=prod[a][r][:, lo : lo + P],
                         rhs=ident[:],
                         is_transpose=True,
                         start=(r == 0),
                         stop=(r == TOP - 1),
                     )
-            nc.scalar.copy(out=sum_t[:, t0 : t0 + HALF_T], in_=sums)
-            back = banks[1 + 2 * k][:, :HALF_T]
-            for lo in range(0, HALF_T, P):
-                nc.tensor.transpose(back[:, lo : lo + P], sum_t[:, t0 + lo : t0 + lo + P], ident[:])
-            nc.scalar.copy(out=res[0][:, t0 : t0 + HALF_T], in_=back)
-            nc.scalar.dma_start(out=out[0:P, t0 : t0 + HALF_T], in_=res[0][:, t0 : t0 + HALF_T])
+            back = banks[back_bank][:, : t1 - t0]
+            for lo, b in zip(range(t0, t1, P), sum_banks):
+                nc.scalar.copy(out=sum_t[a][:, lo : lo + P], in_=banks[b][:, :P])
+                nc.tensor.transpose(back[:, lo - t0 : lo - t0 + P], sum_t[a][:, lo : lo + P], ident[:])
+            nc.scalar.copy(out=res[a][:, t0:t1], in_=back)
+            nc.scalar.dma_start(out=out[a * P : (a + 1) * P, t0:t1], in_=res[a][:, t0:t1])
 
-        product(1, 0, 0, T)
-        product(1, 1, 0, T)
-        product(1, 2, 0, HALF_T)
-        nc.vector.tensor_tensor(part[:], prod[1][0][:], prod[1][1][:], ALU.add)
-        product(1, 2, HALF_T, T)
-        for t0 in range(0, T, HALF_T):
-            nc.vector.tensor_tensor(
-                res[1][:, t0 : t0 + HALF_T], part[:, t0 : t0 + HALF_T], prod[1][2][:, t0 : t0 + HALF_T], ALU.add
-            )
-            nc.sync.dma_start(out=out[P:, t0 : t0 + HALF_T], in_=res[1][:, t0 : t0 + HALF_T])
+        middle = (DIRECT_FROM + T) // 2
+        product(1, 0, DIRECT_FROM, T)
+        product(1, 1, DIRECT_FROM, T)
+        product(1, 2, DIRECT_FROM, middle)
+        nc.vector.tensor_tensor(part[:, DIRECT_FROM:], prod[1][0][:, DIRECT_FROM:], prod[1][1][:, DIRECT_FROM:], ALU.add)
+        product(1, 2, middle, T)
+        for t0, t1 in ((DIRECT_FROM, middle), (middle, T)):
+            nc.vector.tensor_tensor(res[1][:, t0:t1], part[:, t0:t1], prod[1][2][:, t0:t1], ALU.add)
+            nc.sync.dma_start(out=out[P:, t0:t1], in_=res[1][:, t0:t1])

@@ -28,8 +28,8 @@ WORD_CUTS = (512, 768, 1024, 1536, 2048, 2304)
 W1_CUTS = (0, 1, 2, 4, 6, 9)
 SCALE_CUTS = (0, 2, 9)
 MOVED = 112
-RELU_ON_VECTOR = (12, 13, 14, 15)
-HELD = 6 * C
+RELU_ON_VECTOR = (12, 13, 14, 15, 16, 17)
+HELD = 8 * C
 DIRECT_FROM = HALF_T
 SUMMED = ((0, 0, HALF_T), (0, HALF_T, T), (1, 0, HALF_T))
 
@@ -221,14 +221,13 @@ def tile_moe_pkd_mlp_relu2_kernel(
         move_late(1)
         load_w1(3)
         load_w1(4)
-        move_late(2)
+        for b in range(2, len(BYTE_CUTS) - 1):
+            move_late(b)
         load_scales(w2s, w2_scales.rearrange("e s q n -> (e s) q n"))
         nc.sync.dma_start(out=w2w[:].bitcast(I32), in_=w2_words.rearrange("e s p b -> p (e s) b").bitcast(I32))
         for r, src in enumerate((pos1, pos2, pos3)):
             nc.sync.dma_start(pos_t[r][:], src)
         nc.sync.dma_start(out=g[:], in_=gate[:, 0:P, :].rearrange("r p t -> p r t"))
-        move_late(3)
-        move_late(4)
 
         for e in range(E + 1):
             if e >= 1:
@@ -243,24 +242,21 @@ def tile_moe_pkd_mlp_relu2_kernel(
             if 1 <= e < E:
                 square(2 * e - 2)
                 square(2 * e - 1)
-            if e == E - 2:
+            if e == E - 1:
                 hq = turns.tile([P, S], U32, name="hq", tag="held", align_bytes=256)
                 for pair in range(3):
                     quantise(2 * pair * C, (2 * pair + 2) * C)
                 quantise(6 * C, 7 * C)
-                for pair in range(2):
-                    layer2(0, 2 * pair * C, (2 * pair + 2) * C, banks[2 + pair], nc.vector.tensor_copy)
-            if e == E - 1:
                 quantise(7 * C, 8 * C)
 
         for u in (2 * E - 2, 2 * E - 1):
             square(u)
             quantise(u * P, (u + 1) * P)
-            layer2(0, u * P, (u + 1) * P, banks[2 + u % 2], nc.vector.tensor_copy)
-        for pair in (2, 3):
-            layer2(0, 2 * pair * C, (2 * pair + 2) * C, banks[pair % 2], nc.scalar.copy)
+            layer2(0, u * P, (u + 1) * P, banks[6 + u % 2], nc.vector.tensor_copy)
+        for pair in range(4):
+            layer2(0, 2 * pair * C, (2 * pair + 2) * C, banks[(pair + 2) % 4], nc.scalar.copy)
         for k, j0 in enumerate(range(0, S, 2 * C)):
-            layer2(1, j0, min(j0 + 2 * C, S), banks[(6, 7, 4, 5, 2)[k]], nc.scalar.copy)
+            layer2(1, j0, min(j0 + 2 * C, S), banks[(3, 4, 5, 0, 2)[k]], nc.scalar.copy)
 
         prod = [[keep.tile([P, T], F32, name="prod%d_%d" % (a, r), align_bytes=64) for r in range(TOP)] for a in range(2)]
         sum_t = [keep.tile([P, T], F32, name="sum_t%d" % a, align_bytes=64) for a in range(2)]
@@ -272,7 +268,7 @@ def tile_moe_pkd_mlp_relu2_kernel(
                 prod[a][r][:, t0:t1], y[a][:].indirect(pos_t[r][:, t0 // 16 : t1 // 16]), g[:, r, t0:t1], ALU.mult
             )
 
-        for (a, t0, t1), (sum_banks, back_bank) in zip(SUMMED, (((2, 0, 1), 3), ((4, 5, 6), 7), ((0, 1, 2), 3))):
+        for (a, t0, t1), (sum_banks, back_bank) in zip(SUMMED, (((2, 1, 6), 7), ((3, 4, 5), 0), ((1, 2, 6), 7))):
             for r in range(TOP):
                 product(a, r, t0, t1)
                 for lo, b in zip(range(t0, t1, P), sum_banks):

@@ -22,14 +22,15 @@ FP4X4 = mybir.dt.float4_e2m1fn_x4
 ACT = mybir.ActivationFunctionType
 ALU = mybir.AluOpType
 
-BYTE_CUTS = (0, 512, 1024, 1536, 2048, 2304)
-EARLY = 2 * C
-WORD_CUTS = (512, 768, 1024, 1536, 2048, 2304)
-W1_CUTS = (0, 1, 2, 4, 6, 9)
-SCALE_CUTS = (0, 2, 9)
+PAIR = 2 * C
+W1_CUTS = (0, 1, 2, 4, 6, 8, 9)
+SCALE_CUTS = (0, 4, 6, 8, 9)
+QUANTISE_AT = {6: ((0, "after10"),), 7: ((1, "after12"), (2, "after13"))}
 MOVED = 112
-RELU_ON_VECTOR = (12, 13, 14, 15, 16, 17)
-HELD = 8 * C
+RELU_ON_VECTOR = (5, 9, 13, 17)
+COPY_ON_VECTOR = (1,)
+W2_FIRST = 6
+WARM_UP = (5, 2)
 DIRECT_FROM = HALF_T
 SUMMED = ((0, 0, HALF_T), (0, HALF_T, T), (1, 0, HALF_T))
 
@@ -41,7 +42,6 @@ def tile_moe_pkd_mlp_relu2_kernel(
     with ExitStack() as ctx:
         keep = ctx.enter_context(tc.tile_pool(name="keep", bufs=1))
         turns = ctx.enter_context(tc.tile_pool(name="turns", bufs=1))
-        ring = ctx.enter_context(tc.tile_pool(name="ring", bufs=2))
         psum = ctx.enter_context(tc.psum_pool(name="psum", bufs=1))
         banks = [psum.tile([P, H], F32, name="bank%d" % b)[:] for b in range(8)]
 
@@ -60,21 +60,18 @@ def tile_moe_pkd_mlp_relu2_kernel(
             keep.tile([P, PASSES * (SCALE_CUTS[c + 1] - SCALE_CUTS[c]), H], U8, name="w1s%d" % c, align_bytes=256)
             for c in range(len(SCALE_CUTS) - 1)
         ]
-        w1w_t = [
-            keep.tile([P, PASSES * (W1_CUTS[c + 1] - W1_CUTS[c]), 2 * H], U8, name="w1w%d" % c, align_bytes=256)
-            for c in range(len(W1_CUTS) - 1)
-        ]
         w2w = keep.tile([P, E, 2 * N], U8, name="w2w", align_bytes=256)
         g = keep.tile([P, TOP, T], F32, name="g", align_bytes=64)
         w1s = {}
         w1w = {}
-        for cuts, tiles, planes in ((SCALE_CUTS, w1s_t, w1s), (W1_CUTS, w1w_t, w1w)):
-            for c, tile in enumerate(tiles):
-                for e in range(cuts[c], cuts[c + 1]):
-                    for s in range(PASSES):
-                        planes[e, s] = tile[:, PASSES * (e - cuts[c]) + s, :]
+        for c, tile in enumerate(w1s_t):
+            for e in range(SCALE_CUTS[c], SCALE_CUTS[c + 1]):
+                for s in range(PASSES):
+                    w1s[e, s] = tile[:, PASSES * (e - SCALE_CUTS[c]) + s, :]
         xg = {}
         sg0 = {}
+        planes0 = {}
+        hq = {}
         relu_t = {}
 
         def zero(planes, engine):
@@ -92,9 +89,13 @@ def tile_moe_pkd_mlp_relu2_kernel(
             load_scales(w1s_t[c], rows[PASSES * SCALE_CUTS[c] : PASSES * SCALE_CUTS[c + 1]])
 
         def load_w1(c):
+            e0, e1 = W1_CUTS[c], W1_CUTS[c + 1]
+            words = keep.tile([P, PASSES * (e1 - e0), 2 * H], U8, name="w1w%d" % c, align_bytes=256)
+            for e in range(e0, e1):
+                for s in range(PASSES):
+                    w1w[e, s] = words[:, PASSES * (e - e0) + s, :]
             nc.sync.dma_start(
-                out=w1w_t[c][:].bitcast(I32),
-                in_=w1_words[W1_CUTS[c] : W1_CUTS[c + 1]].rearrange("e s p b -> p (e s) b").bitcast(I32),
+                out=words[:].bitcast(I32), in_=w1_words[e0:e1].rearrange("e s p b -> p (e s) b").bitcast(I32)
             )
 
         def load_words(s):
@@ -105,31 +106,38 @@ def tile_moe_pkd_mlp_relu2_kernel(
                 xg[u, s] = dst[:, u * P - j0 : (u + 1) * P - j0]
             nc.vector.tensor_copy(dst, xw[s][:].bitcast(U32).indirect(offs_t[:, j0 // 16 : j1 // 16]))
 
-        def gather_bytes(c, dst):
-            j0, j1 = BYTE_CUTS[c], BYTE_CUTS[c + 1]
+        def gather_bytes(c, place):
+            j0, j1 = c * PAIR, min((c + 1) * PAIR, S)
+            planes0[c] = turns.tile([P, j1 - j0], U8, name="sg0", tag=place, align_bytes=256)
             for u in range(j0 // P, j1 // P):
-                sg0[u] = dst[:, u * P - j0 : (u + 1) * P - j0]
-            nc.vector.tensor_copy(dst, xs[:].indirect(offs_t[:, j0 // 16 : j1 // 16]))
+                sg0[u] = planes0[c][:, u * P - j0 : (u + 1) * P - j0]
+            nc.vector.tensor_copy(planes0[c][:], xs[:].indirect(offs_t[:, j0 // 16 : j1 // 16]))
 
-        def move_bytes(c, src):
-            j0, j1 = BYTE_CUTS[c], BYTE_CUTS[c + 1]
-            for p0, p1 in ((0, 64), (64, 96), (96, 100)) if c <= 1 else ((0, MOVED),):
-                nc.sync.dma_start(out=sg1[p0:p1, j0:j1].bitcast(I32), in_=src[4 + p0 : 4 + p1, :].bitcast(I32))
+        def move_bytes(c, queue, cuts):
+            j0, j1 = c * PAIR, min((c + 1) * PAIR, S)
+            for p0, p1 in cuts:
+                queue.dma_start(out=sg1[p0:p1, j0:j1].bitcast(I32), in_=planes0[c][4 + p0 : 4 + p1, :].bitcast(I32))
+
+        def gather_expert(e, place):
+            words = turns.tile([P, PASSES, C], U32, name="xg", tag=place, align_bytes=256)
+            for s in (0, 1) if e < 2 else (1, 0):
+                gather_words(s, e * C, (e + 1) * C, words[:, s, :])
 
         def layer1(u):
-            for s in range(PASSES):
+            order = (0, 1) if u < 4 else (1, 0)
+            for s in order:
                 nc.tensor.matmul_mx(
                     out=banks[u % 4],
                     lhsT=xg[u, s].bitcast(FP8X4),
                     lhsT_scale=(sg0[u], sg1[:, u * P : (u + 1) * P])[s],
                     rhs=w1w[u // 2, s].bitcast(FP4X4),
                     rhs_scale=w1s[u // 2, s],
-                    start=(s == 0),
-                    stop=(s == PASSES - 1),
+                    start=(s == order[0]),
+                    stop=(s == order[1]),
                 )
 
         def relu(u):
-            relu_t[u] = ring.tile([P, 4, P], F32, name="r_t", bufs=4, align_bytes=64)
+            relu_t[u] = turns.tile([P, 4, P], F32, name="r_t", tag="after%d" % u, align_bytes=256)
             src = banks[u % 4].rearrange("j (c d t) -> j c t d", d=4, t=4)
             dst = relu_t[u][:].rearrange("j t (c d) -> j c t d", d=4)
             if u in RELU_ON_VECTOR:
@@ -149,20 +157,24 @@ def tile_moe_pkd_mlp_relu2_kernel(
                 out=hb[:, u * P : (u + 1) * P, :], in_=turned(u).rearrange("p t j -> p j t"), func=ACT.Square
             )
 
-        def quantise(j0, j1):
+        def quantise(j0, j1, place):
+            codes = turns.tile([P, j1 - j0], U32, name="hq", tag=place, align_bytes=256)
+            for lo in range(j0, j1, P):
+                hq[lo] = codes[:, lo - j0 :]
             nc.vector.quantize_mx(
-                out=hq[:, j0:j1].bitcast(FP8X4), scales=hs[:, j0:j1], in_=hb[:, j0:j1, :].rearrange("p j t -> p (j t)")
+                out=codes[:].bitcast(FP8X4), scales=hs[:, j0:j1], in_=hb[:, j0:j1, :].rearrange("p j t -> p (j t)")
             )
 
         def layer2(a, j0, j1, acc, copy):
-            for lo in range(j0, j1, C):
-                hi = min(lo + C, j1)
+            step = C if j0 < 8 * C else P
+            for lo in range(j0, j1, step):
+                hi = lo + step
                 e = lo // C
                 nc.tensor.matmul_mx(
                     out=acc[:, lo - j0 : hi - j0],
                     lhsT=w2w[:, e, a * N : (a + 1) * N].bitcast(FP4X4),
                     lhsT_scale=w2s[:, e, a * P : (a + 1) * P],
-                    rhs=hq[:, lo:hi].bitcast(FP8X4),
+                    rhs=hq[lo][:, :step].bitcast(FP8X4),
                     rhs_scale=hs[:, lo:hi],
                     start=True,
                     stop=True,
@@ -174,8 +186,27 @@ def tile_moe_pkd_mlp_relu2_kernel(
         nc.vector.memset(sg1[:].bitcast(I32), 0)
         make_identity(nc, ident_src[:])
         nc.scalar.activation(out=ident[:], in_=ident_src[:], func=ACT.Relu)
-        zero(w1s_t[1], nc.vector)
+        for planes in w1s_t[1:]:
+            zero(planes, nc.vector)
         zero(w2s, nc.gpsimd)
+
+        first_pass1 = turns.tile([P, C], U32, name="xg_first", tag="first_pass1", align_bytes=256)
+        nc.vector.memset(first_pass1[:, :P], 0)
+        nc.vector.memset(w2w[:, 0:2, :].rearrange("p a c -> p (a c)").bitcast(I32), 0)
+
+        def warm_up(count, words):
+            for i in range(count):
+                nc.tensor.matmul_mx(
+                    out=banks[7],
+                    lhsT=first_pass1[:, :P].bitcast(FP8X4),
+                    lhsT_scale=w1s_t[-1][:, 0, :P],
+                    rhs=words.bitcast(FP4X4),
+                    rhs_scale=w1s_t[-1][:, 1, :],
+                    start=True,
+                    stop=True,
+                )
+
+        warm_up(WARM_UP[0], w2w[:, 0:2, :].rearrange("p a c -> p (a c)"))
 
         nc.sync.dma_start(offs_t[:], offs)
         for q in range(4):
@@ -185,78 +216,89 @@ def tile_moe_pkd_mlp_relu2_kernel(
         load_words(0)
         load_words(1)
         load_w1(0)
+        warm_up(WARM_UP[1], w1w[0, 0])
         load_w1s(0)
 
-        sg_early = turns.tile([P, EARLY], U8, name="sg_early", tag="held", align_bytes=256)
-        gather_bytes(0, sg_early[:])
-        move_bytes(0, sg_early)
+        in_three = ((0, 64), (64, 96), (96, 100))
+        at_once = ((0, MOVED),)
+        gather_bytes(0, "planes0")
+        move_bytes(0, nc.sync, in_three)
+        gather_bytes(1, "planes1")
         load_w1(1)
-        for u, place in enumerate(("planes", "words")):
-            gather_words(0, u * P, (u + 1) * P, turns.tile([P, P], U32, name="xg_first", tag=place, align_bytes=256)[:])
-        xg_early = keep.tile([P, 3, C], U32, name="xg_early", align_bytes=256)
-        gather_words(1, 0, C, xg_early[:, 0, :])
-        gather_words(0, C, 2 * C, xg_early[:, 1, :])
-        gather_words(1, C, 2 * C, xg_early[:, 2, :])
-        for u in range(EARLY // P):
+        move_bytes(1, nc.sync, at_once)
+        for u in range(2):
+            first = turns.tile([P, P], U32, name="xg_first", tag="words%d" % u, align_bytes=256)
+            gather_words(0, u * P, (u + 1) * P, first[:])
+        gather_words(1, 0, C, first_pass1[:])
+        gather_expert(1, "words_early")
+        for u in range(4):
             layer1(u)
-
-        xg_late = turns.tile([P, PASSES, S - EARLY], U32, name="xg_late", tag="words", align_bytes=256)
-        sg_late = turns.tile([P, S - EARLY], U8, name="sg_late", tag="planes", align_bytes=256)
-        for c in range(len(WORD_CUTS) - 1):
-            j0, j1 = WORD_CUTS[c], WORD_CUTS[c + 1]
-            if j0 in BYTE_CUTS:
-                b = BYTE_CUTS.index(j0)
-                gather_bytes(b, sg_late[:, j0 - EARLY : BYTE_CUTS[b + 1] - EARLY])
-            if j0 == HELD:
-                xg_held = turns.tile([P, PASSES, j1 - j0], U32, name="xg_held", tag="held", align_bytes=256)
-            for s in range(PASSES):
-                dst = xg_held[:, s, :] if j0 == HELD else xg_late[:, s, j0 - EARLY : j1 - EARLY]
-                gather_words(s, j0, j1, dst)
-
-        def move_late(b):
-            move_bytes(b, sg_late[:, BYTE_CUTS[b] - EARLY : BYTE_CUTS[b + 1] - EARLY])
-
+        gather_expert(2, "words0")
+        gather_expert(3, "words1")
+        gather_bytes(2, "first_pass1")
         load_w1(2)
-        load_w1s(1)
-        move_late(1)
         load_w1(3)
+        load_w1s(1)
+        move_bytes(2, nc.sync, at_once)
         load_w1(4)
-        for b in range(2, len(BYTE_CUTS) - 1):
-            move_late(b)
-        load_scales(w2s, w2_scales.rearrange("e s q n -> (e s) q n"))
-        nc.sync.dma_start(out=w2w[:].bitcast(I32), in_=w2_words.rearrange("e s p b -> p (e s) b").bitcast(I32))
-        for r, src in enumerate((pos1, pos2, pos3)):
-            nc.sync.dma_start(pos_t[r][:], src)
-        nc.sync.dma_start(out=g[:], in_=gate[:, 0:P, :].rearrange("r p t -> p r t"))
+        load_w1s(2)
 
-        for e in range(E + 1):
+        for e in range(E):
             if e >= 1:
                 turn(2 * e - 2)
                 turn(2 * e - 1)
             if 1 <= e < E - 1:
                 layer1(2 * e + 2)
                 layer1(2 * e + 3)
-            if e < E:
-                relu(2 * e)
-                relu(2 * e + 1)
-            if 1 <= e < E:
+            relu(2 * e)
+            relu(2 * e + 1)
+            if e == 2:
+                gather_expert(4, "words0")
+                gather_expert(5, "after2")
+                gather_bytes(3, "after3")
+                move_bytes(3, nc.sync, at_once)
+                load_w1(5)
+                load_w1s(3)
+            if e == 3:
+                gather_bytes(4, "words1")
+                move_bytes(4, nc.sync, at_once)
+                load_scales(w2s, w2_scales.rearrange("e s q n -> (e s) q n"))
+                for e0, e1 in ((0, W2_FIRST), (W2_FIRST, E)):
+                    nc.sync.dma_start(
+                        out=w2w[:, e0:e1, :].bitcast(I32),
+                        in_=w2_words[e0:e1].rearrange("e s p b -> p (e s) b").bitcast(I32),
+                    )
+                for r, src in enumerate((pos1, pos2, pos3)):
+                    nc.sync.dma_start(pos_t[r][:], src)
+                nc.sync.dma_start(out=g[:], in_=gate[:, 0:P, :].rearrange("r p t -> p r t"))
+            if e == 4:
+                gather_expert(6, "words0")
+                gather_expert(7, "after6")
+            if e == 5:
+                gather_expert(8, "after2")
+            if e in QUANTISE_AT:
+                for pair, place in QUANTISE_AT[e]:
+                    quantise(pair * PAIR, (pair + 1) * PAIR, place)
+            if e >= 1:
                 square(2 * e - 2)
                 square(2 * e - 1)
-            if e == E - 1:
-                hq = turns.tile([P, S], U32, name="hq", tag="held", align_bytes=256)
-                for pair in range(3):
-                    quantise(2 * pair * C, (2 * pair + 2) * C)
-                quantise(6 * C, 7 * C)
-                quantise(7 * C, 8 * C)
+
+        def first_half(pair):
+            copy = nc.vector.tensor_copy if pair in COPY_ON_VECTOR else nc.scalar.copy
+            layer2(0, pair * PAIR, (pair + 1) * PAIR, banks[(2, 3, 0, 1)[pair]], copy)
 
         for u in (2 * E - 2, 2 * E - 1):
+            turn(u)
+        quantise(3 * PAIR, 4 * PAIR, "hq3")
+        for u in (2 * E - 2, 2 * E - 1):
             square(u)
-            quantise(u * P, (u + 1) * P)
-            layer2(0, u * P, (u + 1) * P, banks[6 + u % 2], nc.vector.tensor_copy)
         for pair in range(4):
-            layer2(0, 2 * pair * C, (2 * pair + 2) * C, banks[(pair + 2) % 4], nc.scalar.copy)
+            first_half(pair)
+        for u in (2 * E - 2, 2 * E - 1):
+            quantise(u * P, (u + 1) * P, "hq%d" % u)
+            layer2(0, u * P, (u + 1) * P, banks[6 + u % 2], nc.vector.tensor_copy)
         for k, j0 in enumerate(range(0, S, 2 * C)):
-            layer2(1, j0, min(j0 + 2 * C, S), banks[(3, 4, 5, 0, 2)[k]], nc.scalar.copy)
+            layer2(1, j0, min(j0 + 2 * C, S), banks[(4, 5, 2, 3, 0)[k]], nc.scalar.copy)
 
         prod = [[keep.tile([P, T], F32, name="prod%d_%d" % (a, r), align_bytes=64) for r in range(TOP)] for a in range(2)]
         sum_t = [keep.tile([P, T], F32, name="sum_t%d" % a, align_bytes=64) for a in range(2)]

@@ -27,12 +27,13 @@ W1_CUTS = (0, 1, 2, 4, 6, 8, 9)
 SCALE_CUTS = (0, 4, 6, 8, 9)
 QUANTISE_AT = {6: ((0, "after10"),), 7: ((1, "after12"), (2, "after13"))}
 MOVED = 112
-RELU_ON_VECTOR = (5, 9, 13, 17)
-COPY_ON_VECTOR = (1,)
-W2_FIRST = 6
+RELU_ON_VECTOR = (5, 9, 13, 15, 16, 17)
+COPY_ON_VECTOR = (0, 1)
+W2_FIRST = 4
 WARM_UP = (5, 2)
 DIRECT_FROM = HALF_T
-SUMMED = ((0, 0, HALF_T), (0, HALF_T, T), (1, 0, HALF_T))
+LAST = 128
+SUMMED = ((0, 0, HALF_T), (0, HALF_T, T), (1, 0, DIRECT_FROM))
 
 
 def tile_moe_pkd_mlp_relu2_kernel(
@@ -106,9 +107,9 @@ def tile_moe_pkd_mlp_relu2_kernel(
                 xg[u, s] = dst[:, u * P - j0 : (u + 1) * P - j0]
             nc.vector.tensor_copy(dst, xw[s][:].bitcast(U32).indirect(offs_t[:, j0 // 16 : j1 // 16]))
 
-        def gather_bytes(c, place):
+        def gather_bytes(c, tag):
             j0, j1 = c * PAIR, min((c + 1) * PAIR, S)
-            planes0[c] = turns.tile([P, j1 - j0], U8, name="sg0", tag=place, align_bytes=256)
+            planes0[c] = turns.tile([P, j1 - j0], U8, name="sg0", tag=tag, align_bytes=256)
             for u in range(j0 // P, j1 // P):
                 sg0[u] = planes0[c][:, u * P - j0 : (u + 1) * P - j0]
             nc.vector.tensor_copy(planes0[c][:], xs[:].indirect(offs_t[:, j0 // 16 : j1 // 16]))
@@ -118,8 +119,8 @@ def tile_moe_pkd_mlp_relu2_kernel(
             for p0, p1 in cuts:
                 queue.dma_start(out=sg1[p0:p1, j0:j1].bitcast(I32), in_=planes0[c][4 + p0 : 4 + p1, :].bitcast(I32))
 
-        def gather_expert(e, place):
-            words = turns.tile([P, PASSES, C], U32, name="xg", tag=place, align_bytes=256)
+        def gather_expert(e, tag):
+            words = turns.tile([P, PASSES, C], U32, name="xg", tag=tag, align_bytes=256)
             for s in (0, 1) if e < 2 else (1, 0):
                 gather_words(s, e * C, (e + 1) * C, words[:, s, :])
 
@@ -157,8 +158,10 @@ def tile_moe_pkd_mlp_relu2_kernel(
                 out=hb[:, u * P : (u + 1) * P, :], in_=turned(u).rearrange("p t j -> p j t"), func=ACT.Square
             )
 
-        def quantise(j0, j1, place):
-            codes = turns.tile([P, j1 - j0], U32, name="hq", tag=place, align_bytes=256)
+        def place(name, slots):
+            return turns.tile([P, slots], U32, name="hq", tag=name, align_bytes=256)
+
+        def quantise(j0, j1, codes):
             for lo in range(j0, j1, P):
                 hq[lo] = codes[:, lo - j0 :]
             nc.vector.quantize_mx(
@@ -190,15 +193,15 @@ def tile_moe_pkd_mlp_relu2_kernel(
             zero(planes, nc.vector)
         zero(w2s, nc.gpsimd)
 
-        first_pass1 = turns.tile([P, C], U32, name="xg_first", tag="first_pass1", align_bytes=256)
-        nc.vector.memset(first_pass1[:, :P], 0)
+        last_codes = keep.tile([P, P], U32, name="last_codes", align_bytes=256)
+        nc.vector.memset(last_codes[:], 0)
         nc.vector.memset(w2w[:, 0:2, :].rearrange("p a c -> p (a c)").bitcast(I32), 0)
 
         def warm_up(count, words):
             for i in range(count):
                 nc.tensor.matmul_mx(
                     out=banks[7],
-                    lhsT=first_pass1[:, :P].bitcast(FP8X4),
+                    lhsT=last_codes[:].bitcast(FP8X4),
                     lhsT_scale=w1s_t[-1][:, 0, :P],
                     rhs=words.bitcast(FP4X4),
                     rhs_scale=w1s_t[-1][:, 1, :],
@@ -229,7 +232,7 @@ def tile_moe_pkd_mlp_relu2_kernel(
         for u in range(2):
             first = turns.tile([P, P], U32, name="xg_first", tag="words%d" % u, align_bytes=256)
             gather_words(0, u * P, (u + 1) * P, first[:])
-        gather_words(1, 0, C, first_pass1[:])
+        gather_words(1, 0, C, turns.tile([P, C], U32, name="xg_first", tag="first_pass1", align_bytes=256)[:])
         gather_expert(1, "words_early")
         for u in range(4):
             layer1(u)
@@ -243,14 +246,18 @@ def tile_moe_pkd_mlp_relu2_kernel(
         load_w1(4)
         load_w1s(2)
 
-        for e in range(E):
-            if e >= 1:
-                turn(2 * e - 2)
-                turn(2 * e - 1)
+        turn_cuts = (0, 0, 2, 4, 6, 8, 10, 12, 15)
+        for e in range(E - 1):
+            turned_now = range(turn_cuts[e], turn_cuts[e + 1])
+            if e == E - 2:
+                relu(2 * e)
+            for u in turned_now:
+                turn(u)
             if 1 <= e < E - 1:
                 layer1(2 * e + 2)
                 layer1(2 * e + 3)
-            relu(2 * e)
+            if e < E - 2:
+                relu(2 * e)
             relu(2 * e + 1)
             if e == 2:
                 gather_expert(4, "words0")
@@ -262,8 +269,8 @@ def tile_moe_pkd_mlp_relu2_kernel(
             if e == 3:
                 gather_bytes(4, "words1")
                 move_bytes(4, nc.sync, at_once)
-                load_scales(w2s, w2_scales.rearrange("e s q n -> (e s) q n"))
                 for e0, e1 in ((0, W2_FIRST), (W2_FIRST, E)):
+                    load_scales(w2s[:, e0:e1, :], w2_scales.rearrange("e s q n -> (e s) q n")[e0:e1])
                     nc.sync.dma_start(
                         out=w2w[:, e0:e1, :].bitcast(I32),
                         in_=w2_words[e0:e1].rearrange("e s p b -> p (e s) b").bitcast(I32),
@@ -277,28 +284,31 @@ def tile_moe_pkd_mlp_relu2_kernel(
             if e == 5:
                 gather_expert(8, "after2")
             if e in QUANTISE_AT:
-                for pair, place in QUANTISE_AT[e]:
-                    quantise(pair * PAIR, (pair + 1) * PAIR, place)
-            if e >= 1:
-                square(2 * e - 2)
-                square(2 * e - 1)
+                for pair, name in QUANTISE_AT[e]:
+                    quantise(pair * PAIR, (pair + 1) * PAIR, place(name, PAIR))
+            for u in turned_now:
+                square(u)
 
         def first_half(pair):
             copy = nc.vector.tensor_copy if pair in COPY_ON_VECTOR else nc.scalar.copy
             layer2(0, pair * PAIR, (pair + 1) * PAIR, banks[(2, 3, 0, 1)[pair]], copy)
 
         for u in (2 * E - 2, 2 * E - 1):
+            relu(u)
+        for u in range(2 * E - 3, 2 * E):
             turn(u)
-        quantise(3 * PAIR, 4 * PAIR, "hq3")
+        quantise(6 * C, 7 * C, place("after15", C))
+        square(2 * E - 3)
+        quantise(7 * C, 8 * C, place("hq7", C))
         for u in (2 * E - 2, 2 * E - 1):
             square(u)
+            quantise(u * P, (u + 1) * P, last_codes if u % 2 else place("hq16", P))
         for pair in range(4):
             first_half(pair)
         for u in (2 * E - 2, 2 * E - 1):
-            quantise(u * P, (u + 1) * P, "hq%d" % u)
             layer2(0, u * P, (u + 1) * P, banks[6 + u % 2], nc.vector.tensor_copy)
         for k, j0 in enumerate(range(0, S, 2 * C)):
-            layer2(1, j0, min(j0 + 2 * C, S), banks[(4, 5, 2, 3, 0)[k]], nc.scalar.copy)
+            layer2(1, j0, min(j0 + 2 * C, S), banks[k], nc.scalar.copy)
 
         prod = [[keep.tile([P, T], F32, name="prod%d_%d" % (a, r), align_bytes=64) for r in range(TOP)] for a in range(2)]
         sum_t = [keep.tile([P, T], F32, name="sum_t%d" % a, align_bytes=64) for a in range(2)]
@@ -310,7 +320,7 @@ def tile_moe_pkd_mlp_relu2_kernel(
                 prod[a][r][:, t0:t1], y[a][:].indirect(pos_t[r][:, t0 // 16 : t1 // 16]), g[:, r, t0:t1], ALU.mult
             )
 
-        for (a, t0, t1), (sum_banks, back_bank) in zip(SUMMED, (((2, 1, 6), 7), ((3, 4, 5), 0), ((1, 2, 6), 7))):
+        for (a, t0, t1), (sum_banks, back_bank) in zip(SUMMED, (((1, 6, 7), 4), ((5, 2, 3), 0), ((1, 6, 7, 4), 5))):
             for r in range(TOP):
                 product(a, r, t0, t1)
                 for lo, b in zip(range(t0, t1, P), sum_banks):
@@ -327,9 +337,9 @@ def tile_moe_pkd_mlp_relu2_kernel(
                 nc.scalar.copy(out=sum_t[a][:, lo : lo + P], in_=banks[b][:, :P])
                 nc.tensor.transpose(back[:, lo - t0 : lo - t0 + P], sum_t[a][:, lo : lo + P], ident[:])
             nc.scalar.copy(out=res[a][:, t0:t1], in_=back)
-            nc.scalar.dma_start(out=out[a * P : (a + 1) * P, t0:t1], in_=res[a][:, t0:t1])
+            (nc.scalar if a else nc.sync).dma_start(out=out[a * P : (a + 1) * P, t0:t1], in_=res[a][:, t0:t1])
 
-        middle = (DIRECT_FROM + T) // 2
+        middle = T - LAST
         product(1, 0, DIRECT_FROM, T)
         product(1, 1, DIRECT_FROM, T)
         product(1, 2, DIRECT_FROM, middle)

@@ -27,7 +27,7 @@ W1_CUTS = (0, 1, 2, 4, 6, 8, 9)
 SCALE_CUTS = (0, 4, 6, 8, 9)
 QUANTISE_AT = {6: ((0, "after10"),), 7: ((1, "after12"), (2, "after13"))}
 MOVED = 112
-RELU_ON_VECTOR = (5, 9, 13, 15, 16, 17)
+RELU_ON_VECTOR = (5, 9, 13, 16)
 COPY_ON_VECTOR = (0, 1)
 W2_FIRST = 4
 WARM_UP = (5, 2)
@@ -139,11 +139,13 @@ def tile_moe_pkd_mlp_relu2_kernel(
 
         def relu(u):
             relu_t[u] = turns.tile([P, 4, P], F32, name="r_t", tag="after%d" % u, align_bytes=256)
-            src = banks[u % 4].rearrange("j (c d t) -> j c t d", d=4, t=4)
-            dst = relu_t[u][:].rearrange("j t (c d) -> j c t d", d=4)
             if u in RELU_ON_VECTOR:
+                src = banks[u % 4].rearrange("j (p h e) -> j h p e", h=2, e=2)
+                dst = relu_t[u][:].rearrange("j (h e) p -> j h p e", h=2)
                 nc.vector.tensor_scalar_max(dst, src, 0.0)
             else:
+                src = banks[u % 4].rearrange("j (c d t) -> j c t d", d=4, t=4)
+                dst = relu_t[u][:].rearrange("j t (c d) -> j c t d", d=4)
                 nc.scalar.activation(out=dst, in_=src, func=ACT.Relu)
 
         def turned(u):
@@ -237,8 +239,8 @@ def tile_moe_pkd_mlp_relu2_kernel(
         for u in range(4):
             layer1(u)
         gather_expert(2, "words0")
-        gather_expert(3, "words1")
-        gather_bytes(2, "first_pass1")
+        gather_bytes(2, "words1")
+        gather_expert(3, "first_pass1")
         load_w1(2)
         load_w1(3)
         load_w1s(1)
@@ -261,13 +263,13 @@ def tile_moe_pkd_mlp_relu2_kernel(
             relu(2 * e + 1)
             if e == 2:
                 gather_expert(4, "words0")
-                gather_expert(5, "after2")
-                gather_bytes(3, "after3")
+                gather_bytes(3, "after2")
+                gather_expert(5, "after3")
                 move_bytes(3, nc.sync, at_once)
                 load_w1(5)
                 load_w1s(3)
             if e == 3:
-                gather_bytes(4, "words1")
+                gather_bytes(4, "first_pass1")
                 move_bytes(4, nc.sync, at_once)
                 for e0, e1 in ((0, W2_FIRST), (W2_FIRST, E)):
                     load_scales(w2s[:, e0:e1, :], w2_scales.rearrange("e s q n -> (e s) q n")[e0:e1])
@@ -282,7 +284,7 @@ def tile_moe_pkd_mlp_relu2_kernel(
                 gather_expert(6, "words0")
                 gather_expert(7, "after6")
             if e == 5:
-                gather_expert(8, "after2")
+                gather_expert(8, "after3")
             if e in QUANTISE_AT:
                 for pair, name in QUANTISE_AT[e]:
                     quantise(pair * PAIR, (pair + 1) * PAIR, place(name, PAIR))

@@ -24,11 +24,11 @@ ALU = mybir.AluOpType
 
 PAIR = 2 * C
 W1_CUTS = (0, 1, 2, 4, 6, 8, 9)
-SCALE_CUTS = (0, 4, 6, 8, 9)
+SCALE_CUTS = (0, 5, 7, 9)
 QUANTISE_AT = {6: ((0, "after10"),), 7: ((1, "after12"), (2, "after13"))}
 MOVED = 112
 RELU_ON_VECTOR = (5, 9, 13, 16)
-COPY_ON_VECTOR = (0, 1)
+COPY_ON_VECTOR = (0,)
 W2_FIRST = 4
 WARM_UP = (5, 2)
 DIRECT_FROM = HALF_T
@@ -139,13 +139,11 @@ def tile_moe_pkd_mlp_relu2_kernel(
 
         def relu(u):
             relu_t[u] = turns.tile([P, 4, P], F32, name="r_t", tag="after%d" % u, align_bytes=256)
+            src = banks[u % 4].rearrange("j (c d t) -> j c t d", d=4, t=4)
+            dst = relu_t[u][:].rearrange("j t (c d) -> j c t d", d=4)
             if u in RELU_ON_VECTOR:
-                src = banks[u % 4].rearrange("j (p h e) -> j h p e", h=2, e=2)
-                dst = relu_t[u][:].rearrange("j (h e) p -> j h p e", h=2)
                 nc.vector.tensor_scalar_max(dst, src, 0.0)
             else:
-                src = banks[u % 4].rearrange("j (c d t) -> j c t d", d=4, t=4)
-                dst = relu_t[u][:].rearrange("j t (c d) -> j c t d", d=4)
                 nc.scalar.activation(out=dst, in_=src, func=ACT.Relu)
 
         def turned(u):
@@ -185,6 +183,10 @@ def tile_moe_pkd_mlp_relu2_kernel(
                     stop=True,
                 )
             copy(y[a][:, j0:j1], acc[:, : j1 - j0])
+
+        def first_half(pair):
+            copy = nc.vector.tensor_copy if pair in COPY_ON_VECTOR else nc.scalar.copy
+            layer2(0, pair * PAIR, (pair + 1) * PAIR, banks[(2, 3, 0, 1)[pair]], copy)
 
         nc.gpsimd.memset(xs[:].bitcast(I32), 0)
         zero(w1s_t[0], nc.vector)
@@ -231,22 +233,19 @@ def tile_moe_pkd_mlp_relu2_kernel(
         gather_bytes(1, "planes1")
         load_w1(1)
         move_bytes(1, nc.sync, at_once)
-        for u in range(2):
-            first = turns.tile([P, P], U32, name="xg_first", tag="words%d" % u, align_bytes=256)
-            gather_words(0, u * P, (u + 1) * P, first[:])
-        gather_words(1, 0, C, turns.tile([P, C], U32, name="xg_first", tag="first_pass1", align_bytes=256)[:])
+        for s in range(PASSES):
+            gather_words(s, 0, C, turns.tile([P, C], U32, name="xg_first", tag="words%d" % s, align_bytes=256)[:])
         gather_expert(1, "words_early")
         for u in range(4):
             layer1(u)
         gather_expert(2, "words0")
         gather_bytes(2, "words1")
-        gather_expert(3, "first_pass1")
+        gather_expert(3, "words_early")
         load_w1(2)
         load_w1(3)
-        load_w1s(1)
         move_bytes(2, nc.sync, at_once)
+        load_w1s(1)
         load_w1(4)
-        load_w1s(2)
 
         turn_cuts = (0, 0, 2, 4, 6, 8, 10, 12, 15)
         for e in range(E - 1):
@@ -258,7 +257,9 @@ def tile_moe_pkd_mlp_relu2_kernel(
             if 1 <= e < E - 1:
                 layer1(2 * e + 2)
                 layer1(2 * e + 3)
-            if e < E - 2:
+            if e == E - 2:
+                first_half(0)
+            else:
                 relu(2 * e)
             relu(2 * e + 1)
             if e == 2:
@@ -266,10 +267,10 @@ def tile_moe_pkd_mlp_relu2_kernel(
                 gather_bytes(3, "after2")
                 gather_expert(5, "after3")
                 move_bytes(3, nc.sync, at_once)
+                load_w1s(2)
                 load_w1(5)
-                load_w1s(3)
             if e == 3:
-                gather_bytes(4, "first_pass1")
+                gather_bytes(4, "words_early")
                 move_bytes(4, nc.sync, at_once)
                 for e0, e1 in ((0, W2_FIRST), (W2_FIRST, E)):
                     load_scales(w2s[:, e0:e1, :], w2_scales.rearrange("e s q n -> (e s) q n")[e0:e1])
@@ -291,9 +292,6 @@ def tile_moe_pkd_mlp_relu2_kernel(
             for u in turned_now:
                 square(u)
 
-        def first_half(pair):
-            copy = nc.vector.tensor_copy if pair in COPY_ON_VECTOR else nc.scalar.copy
-            layer2(0, pair * PAIR, (pair + 1) * PAIR, banks[(2, 3, 0, 1)[pair]], copy)
 
         for u in (2 * E - 2, 2 * E - 1):
             relu(u)
@@ -305,7 +303,7 @@ def tile_moe_pkd_mlp_relu2_kernel(
         for u in (2 * E - 2, 2 * E - 1):
             square(u)
             quantise(u * P, (u + 1) * P, last_codes if u % 2 else place("hq16", P))
-        for pair in range(4):
+        for pair in range(1, 4):
             first_half(pair)
         for u in (2 * E - 2, 2 * E - 1):
             layer2(0, u * P, (u + 1) * P, banks[6 + u % 2], nc.vector.tensor_copy)
@@ -322,24 +320,38 @@ def tile_moe_pkd_mlp_relu2_kernel(
                 prod[a][r][:, t0:t1], y[a][:].indirect(pos_t[r][:, t0 // 16 : t1 // 16]), g[:, r, t0:t1], ALU.mult
             )
 
-        for (a, t0, t1), (sum_banks, back_bank) in zip(SUMMED, (((1, 6, 7), 4), ((5, 2, 3), 0), ((1, 6, 7, 4), 5))):
-            for r in range(TOP):
-                product(a, r, t0, t1)
-                for lo, b in zip(range(t0, t1, P), sum_banks):
-                    nc.tensor.matmul(
-                        banks[b][:, :P],
-                        lhsT=prod[a][r][:, lo : lo + P],
-                        rhs=ident[:],
-                        is_transpose=True,
-                        start=(r == 0),
-                        stop=(r == TOP - 1),
-                    )
-            back = banks[back_bank][:, : t1 - t0]
-            for lo, b in zip(range(t0, t1, P), sum_banks):
-                nc.scalar.copy(out=sum_t[a][:, lo : lo + P], in_=banks[b][:, :P])
-                nc.tensor.transpose(back[:, lo - t0 : lo - t0 + P], sum_t[a][:, lo : lo + P], ident[:])
-            nc.scalar.copy(out=res[a][:, t0:t1], in_=back)
-            (nc.scalar if a else nc.sync).dma_start(out=out[a * P : (a + 1) * P, t0:t1], in_=res[a][:, t0:t1])
+        def add_on_tensor(a, r, t0, sum_banks):
+            for lo, bank in zip(range(t0, t0 + HALF_T, P), sum_banks):
+                nc.tensor.matmul(
+                    banks[bank][:, :P],
+                    lhsT=prod[a][r][:, lo : lo + P],
+                    rhs=ident[:],
+                    is_transpose=True,
+                    start=(r == 0),
+                    stop=(r == TOP - 1),
+                )
+
+        def turn_back(a, t0, sum_banks, back_bank, queue):
+            t1 = t0 + HALF_T
+            for lo, bank in zip(range(t0, t1, P), sum_banks):
+                nc.scalar.copy(out=sum_t[a][:, lo : lo + P], in_=banks[bank][:, :P])
+                nc.tensor.transpose(banks[back_bank][:, lo - t0 : lo - t0 + P], sum_t[a][:, lo : lo + P], ident[:])
+            nc.scalar.copy(out=res[a][:, t0:t1], in_=banks[back_bank][:, :HALF_T])
+            queue.dma_start(out=out[a * P : (a + 1) * P, t0:t1], in_=res[a][:, t0:t1])
+
+        early, late = (5, 6, 7), (2, 0, 1)
+        for r in range(TOP - 1):
+            product(0, r, 0, T)
+            add_on_tensor(0, r, 0, early)
+            add_on_tensor(0, r, HALF_T, late)
+        for t0, sum_banks, back_bank in ((0, early, 3), (HALF_T, late, 4)):
+            product(0, TOP - 1, t0, t0 + HALF_T)
+            add_on_tensor(0, TOP - 1, t0, sum_banks)
+            turn_back(0, t0, sum_banks, back_bank, nc.scalar if t0 else nc.sync)
+        for r in range(TOP):
+            product(1, r, 0, HALF_T)
+            add_on_tensor(1, r, 0, late)
+        turn_back(1, 0, late, 5, nc.scalar)
 
         middle = T - LAST
         product(1, 0, DIRECT_FROM, T)

@@ -30,7 +30,6 @@ MOVED = 112
 RELU_ON_VECTOR = (5, 9, 13, 16)
 COPY_ON_VECTOR = (0,)
 W2_FIRST = 4
-WARM_UP = (5, 2)
 DIRECT_FROM = HALF_T
 LAST = 128
 SUMMED = ((0, 0, HALF_T), (0, HALF_T, T), (1, 0, DIRECT_FROM))
@@ -198,22 +197,6 @@ def tile_moe_pkd_mlp_relu2_kernel(
         zero(w2s, nc.gpsimd)
 
         last_codes = keep.tile([P, P], U32, name="last_codes", align_bytes=256)
-        nc.vector.memset(last_codes[:], 0)
-        nc.vector.memset(w2w[:, 0:2, :].rearrange("p a c -> p (a c)").bitcast(I32), 0)
-
-        def warm_up(count, words):
-            for i in range(count):
-                nc.tensor.matmul_mx(
-                    out=banks[7],
-                    lhsT=last_codes[:].bitcast(FP8X4),
-                    lhsT_scale=w1s_t[-1][:, 0, :P],
-                    rhs=words.bitcast(FP4X4),
-                    rhs_scale=w1s_t[-1][:, 1, :],
-                    start=True,
-                    stop=True,
-                )
-
-        warm_up(WARM_UP[0], w2w[:, 0:2, :].rearrange("p a c -> p (a c)"))
 
         nc.sync.dma_start(offs_t[:], offs)
         for q in range(4):
@@ -223,7 +206,6 @@ def tile_moe_pkd_mlp_relu2_kernel(
         load_words(0)
         load_words(1)
         load_w1(0)
-        warm_up(WARM_UP[1], w1w[0, 0])
         load_w1s(0)
 
         in_three = ((0, 64), (64, 96), (96, 100))

@@ -32,7 +32,6 @@ COPY_ON_VECTOR = (0,)
 W2_FIRST = 4
 DIRECT_FROM = HALF_T
 LAST = 128
-SUMMED = ((0, 0, HALF_T), (0, HALF_T, T), (1, 0, DIRECT_FROM))
 
 
 def tile_moe_pkd_mlp_relu2_kernel(
@@ -289,9 +288,6 @@ def tile_moe_pkd_mlp_relu2_kernel(
             first_half(pair)
         for u in (2 * E - 2, 2 * E - 1):
             layer2(0, u * P, (u + 1) * P, banks[6 + u % 2], nc.vector.tensor_copy)
-        for k, j0 in enumerate(range(0, S, 2 * C)):
-            layer2(1, j0, min(j0 + 2 * C, S), banks[k], nc.scalar.copy)
-
         prod = [[keep.tile([P, T], F32, name="prod%d_%d" % (a, r), align_bytes=64) for r in range(TOP)] for a in range(2)]
         sum_t = [keep.tile([P, T], F32, name="sum_t%d" % a, align_bytes=64) for a in range(2)]
         part = keep.tile([P, T], F32, name="part", align_bytes=64)
@@ -302,45 +298,73 @@ def tile_moe_pkd_mlp_relu2_kernel(
                 prod[a][r][:, t0:t1], y[a][:].indirect(pos_t[r][:, t0 // 16 : t1 // 16]), g[:, r, t0:t1], ALU.mult
             )
 
-        def add_on_tensor(a, r, t0, sum_banks):
-            for lo, bank in zip(range(t0, t0 + HALF_T, P), sum_banks):
+        fetched = {
+            (a, r): keep.tile([P, T], F32, name="fetched%d_%d" % (a, r), align_bytes=64)
+            for a, r in ((0, 2), (1, 2), (1, 1))
+        }
+        last_r = TOP - 1
+
+        def fetch(a, r, t0, t1):
+            nc.scalar.activation(
+                out=fetched[a, r][:, t0:t1], in_=y[a][:].indirect(pos_t[r][:, t0 // 16 : t1 // 16]), func=ACT.Copy
+            )
+
+        def weigh(a, r, t0, t1):
+            nc.vector.tensor_tensor(prod[a][r][:, t0:t1], fetched[a, r][:, t0:t1], g[:, r, t0:t1], ALU.mult)
+
+        def add_on_tensor(a, r, t0, bank, start, stop):
+            for lo in range(t0, t0 + HALF_T, P):
                 nc.tensor.matmul(
-                    banks[bank][:, :P],
+                    banks[bank][:, lo - t0 : lo - t0 + P],
                     lhsT=prod[a][r][:, lo : lo + P],
                     rhs=ident[:],
                     is_transpose=True,
-                    start=(r == 0),
-                    stop=(r == TOP - 1),
+                    start=(start and lo == t0),
+                    stop=(stop and lo == t0 + HALF_T - P),
                 )
 
-        def turn_back(a, t0, sum_banks, back_bank, queue):
+        def take_sum(a, t0, bank):
+            nc.scalar.copy(out=sum_t[a][:, t0 : t0 + HALF_T], in_=banks[bank][:, :HALF_T])
+
+        def turn_back(a, t0, back_bank, queue):
             t1 = t0 + HALF_T
-            for lo, bank in zip(range(t0, t1, P), sum_banks):
-                nc.scalar.copy(out=sum_t[a][:, lo : lo + P], in_=banks[bank][:, :P])
+            for lo in range(t0, t1, P):
                 nc.tensor.transpose(banks[back_bank][:, lo - t0 : lo - t0 + P], sum_t[a][:, lo : lo + P], ident[:])
             nc.scalar.copy(out=res[a][:, t0:t1], in_=banks[back_bank][:, :HALF_T])
             queue.dma_start(out=out[a * P : (a + 1) * P, t0:t1], in_=res[a][:, t0:t1])
 
-        early, late = (5, 6, 7), (2, 0, 1)
+        fetch(0, last_r, 0, T)
+        for k, j0 in enumerate(range(0, S, 2 * C)):
+            layer2(1, j0, min(j0 + 2 * C, S), banks[k], nc.scalar.copy)
+        fetch(1, last_r, 0, HALF_T)
         for r in range(TOP - 1):
             product(0, r, 0, T)
-            add_on_tensor(0, r, 0, early)
-            add_on_tensor(0, r, HALF_T, late)
-        for t0, sum_banks, back_bank in ((0, early, 3), (HALF_T, late, 4)):
-            product(0, TOP - 1, t0, t0 + HALF_T)
-            add_on_tensor(0, TOP - 1, t0, sum_banks)
-            turn_back(0, t0, sum_banks, back_bank, nc.scalar if t0 else nc.sync)
-        for r in range(TOP):
-            product(1, r, 0, HALF_T)
-            add_on_tensor(1, r, 0, late)
-        turn_back(1, 0, late, 5, nc.scalar)
+            add_on_tensor(0, r, 0, 5, r == 0, False)
+            add_on_tensor(0, r, HALF_T, 6, r == 0, False)
+        weigh(0, last_r, 0, T)
+        add_on_tensor(0, last_r, 0, 5, False, True)
+        add_on_tensor(0, last_r, HALF_T, 6, False, True)
+        take_sum(0, 0, 5)
+        take_sum(0, HALF_T, 6)
+        fetch(1, last_r, HALF_T, T)
+        fetch(1, 1, HALF_T, T)
+        product(1, 0, 0, HALF_T)
+        add_on_tensor(1, 0, 0, 7, True, False)
+        turn_back(0, 0, 0, nc.sync)
+        product(1, 1, 0, HALF_T)
+        add_on_tensor(1, 1, 0, 7, False, False)
+        weigh(1, last_r, 0, HALF_T)
+        add_on_tensor(1, last_r, 0, 7, False, True)
+        take_sum(1, 0, 7)
+        turn_back(0, HALF_T, 1, nc.scalar)
+        turn_back(1, 0, 2, nc.scalar)
 
-        middle = T - LAST
         product(1, 0, DIRECT_FROM, T)
-        product(1, 1, DIRECT_FROM, T)
-        product(1, 2, DIRECT_FROM, middle)
-        nc.vector.tensor_tensor(part[:, DIRECT_FROM:], prod[1][0][:, DIRECT_FROM:], prod[1][1][:, DIRECT_FROM:], ALU.add)
-        product(1, 2, middle, T)
-        for t0, t1 in ((DIRECT_FROM, middle), (middle, T)):
-            nc.vector.tensor_tensor(res[1][:, t0:t1], part[:, t0:t1], prod[1][2][:, t0:t1], ALU.add)
+        weigh(1, last_r, DIRECT_FROM, T)
+        weigh(1, 1, DIRECT_FROM, T)
+        pieces = ((DIRECT_FROM, T - LAST), (T - LAST, T))
+        for t0, t1 in pieces:
+            nc.vector.tensor_tensor(part[:, t0:t1], prod[1][0][:, t0:t1], prod[1][2][:, t0:t1], ALU.add)
+        for t0, t1 in pieces:
+            nc.vector.tensor_tensor(res[1][:, t0:t1], part[:, t0:t1], prod[1][1][:, t0:t1], ALU.add)
             nc.sync.dma_start(out=out[P:, t0:t1], in_=res[1][:, t0:t1])

@@ -23,12 +23,13 @@ ACT = mybir.ActivationFunctionType
 ALU = mybir.AluOpType
 
 PAIR = 2 * C
+BYTE_CUTS = (0, 2, 4, 6, 8, 9)
 W1_CUTS = (0, 1, 2, 4, 6, 8, 9)
 SCALE_CUTS = (0, 5, 7, 9)
 QUANTISE_AT = {6: ((0, "after10"),), 7: ((1, "after12"), (2, "after13"))}
 MOVED = 112
 RELU_ON_VECTOR = (5, 9, 13, 16)
-COPY_ON_VECTOR = (0,)
+COPY_ON_VECTOR = (0, 1)
 W2_FIRST = 4
 DIRECT_FROM = HALF_T
 LAST = 128
@@ -46,7 +47,7 @@ def tile_moe_pkd_mlp_relu2_kernel(
 
         offs_t = keep.tile([P, S // 16], U16, name="offs_t")
         pos_t = [keep.tile([P, T // 16], U16, name="pos_t%d" % r) for r in range(TOP)]
-        xw = [keep.tile([P, T], I32, name="xw%d" % s, align_bytes=64) for s in range(PASSES)]
+        xw = keep.tile([P, PASSES, T], I32, name="xw", align_bytes=64)
         xs = keep.tile([P, T], U8, name="xs", align_bytes=64)
         w2s = keep.tile([P, E, N], U8, name="w2s", align_bytes=256)
         sg1 = keep.tile([P, S], U8, name="sg1", align_bytes=256)
@@ -97,42 +98,38 @@ def tile_moe_pkd_mlp_relu2_kernel(
                 out=words[:].bitcast(I32), in_=w1_words[e0:e1].rearrange("e s p b -> p (e s) b").bitcast(I32)
             )
 
-        def load_words(s):
-            nc.sync.dma_start(out=xw[s][:], in_=x_words[s].rearrange("p t r -> p (t r)").bitcast(I32))
-
         def gather_words(s, j0, j1, dst):
             for u in range(j0 // P, j1 // P):
                 xg[u, s] = dst[:, u * P - j0 : (u + 1) * P - j0]
-            nc.vector.tensor_copy(dst, xw[s][:].bitcast(U32).indirect(offs_t[:, j0 // 16 : j1 // 16]))
+            nc.vector.tensor_copy(dst, xw[:, s, :].bitcast(U32).indirect(offs_t[:, j0 // 16 : j1 // 16]))
 
         def gather_bytes(c, tag):
-            j0, j1 = c * PAIR, min((c + 1) * PAIR, S)
+            j0, j1 = BYTE_CUTS[c] * C, BYTE_CUTS[c + 1] * C
             planes0[c] = turns.tile([P, j1 - j0], U8, name="sg0", tag=tag, align_bytes=256)
             for u in range(j0 // P, j1 // P):
                 sg0[u] = planes0[c][:, u * P - j0 : (u + 1) * P - j0]
             nc.vector.tensor_copy(planes0[c][:], xs[:].indirect(offs_t[:, j0 // 16 : j1 // 16]))
 
         def move_bytes(c, queue, cuts):
-            j0, j1 = c * PAIR, min((c + 1) * PAIR, S)
+            j0, j1 = BYTE_CUTS[c] * C, BYTE_CUTS[c + 1] * C
             for p0, p1 in cuts:
                 queue.dma_start(out=sg1[p0:p1, j0:j1].bitcast(I32), in_=planes0[c][4 + p0 : 4 + p1, :].bitcast(I32))
 
         def gather_expert(e, tag):
             words = turns.tile([P, PASSES, C], U32, name="xg", tag=tag, align_bytes=256)
-            for s in (0, 1) if e < 2 else (1, 0):
+            for s in range(PASSES):
                 gather_words(s, e * C, (e + 1) * C, words[:, s, :])
 
         def layer1(u):
-            order = (0, 1) if u < 4 else (1, 0)
-            for s in order:
+            for s in range(PASSES):
                 nc.tensor.matmul_mx(
                     out=banks[u % 4],
                     lhsT=xg[u, s].bitcast(FP8X4),
                     lhsT_scale=(sg0[u], sg1[:, u * P : (u + 1) * P])[s],
                     rhs=w1w[u // 2, s].bitcast(FP4X4),
                     rhs_scale=w1s[u // 2, s],
-                    start=(s == order[0]),
-                    stop=(s == order[1]),
+                    start=(s == 0),
+                    stop=(s == PASSES - 1),
                 )
 
         def relu(u):
@@ -202,9 +199,8 @@ def tile_moe_pkd_mlp_relu2_kernel(
             nc.sync.dma_start(
                 out=xs[32 * q : 32 * q + 8, :].bitcast(I32), in_=x_scales[:, 4 * q : 4 * q + 4, :].bitcast(I32)
             )
-        load_words(0)
-        load_words(1)
         load_w1(0)
+        nc.sync.dma_start(out=xw[:], in_=x_words.rearrange("s p t r -> p s (t r)").bitcast(I32))
         load_w1s(0)
 
         in_three = ((0, 64), (64, 96), (96, 100))
@@ -214,30 +210,32 @@ def tile_moe_pkd_mlp_relu2_kernel(
         gather_bytes(1, "planes1")
         load_w1(1)
         move_bytes(1, nc.sync, at_once)
-        for s in range(PASSES):
-            gather_words(s, 0, C, turns.tile([P, C], U32, name="xg_first", tag="words%d" % s, align_bytes=256)[:])
-        gather_expert(1, "words_early")
+        load_w1(2)
+        for e in range(2):
+            for s in range(PASSES):
+                first = turns.tile([P, C], U32, name="xg_first", tag="words%d" % (2 * e + s), align_bytes=256)
+                gather_words(s, e * C, (e + 1) * C, first[:])
         for u in range(4):
             layer1(u)
         gather_expert(2, "words0")
         gather_bytes(2, "words1")
-        gather_expert(3, "words_early")
-        load_w1(2)
+        gather_expert(3, "words2")
+        relu(0)
+        relu(1)
         load_w1(3)
-        move_bytes(2, nc.sync, at_once)
+        move_bytes(2, nc.sync, in_three)
         load_w1s(1)
         load_w1(4)
 
         turn_cuts = (0, 0, 2, 4, 6, 8, 10, 12, 15)
-        for e in range(E - 1):
+        for e in range(1, E - 1):
             turned_now = range(turn_cuts[e], turn_cuts[e + 1])
             if e == E - 2:
                 relu(2 * e)
             for u in turned_now:
                 turn(u)
-            if 1 <= e < E - 1:
-                layer1(2 * e + 2)
-                layer1(2 * e + 3)
+            layer1(2 * e + 2)
+            layer1(2 * e + 3)
             if e == E - 2:
                 first_half(0)
             else:
@@ -251,10 +249,10 @@ def tile_moe_pkd_mlp_relu2_kernel(
                 load_w1s(2)
                 load_w1(5)
             if e == 3:
-                gather_bytes(4, "words_early")
+                gather_bytes(4, "words2")
                 move_bytes(4, nc.sync, at_once)
+                load_scales(w2s, w2_scales.rearrange("e s q n -> (e s) q n"))
                 for e0, e1 in ((0, W2_FIRST), (W2_FIRST, E)):
-                    load_scales(w2s[:, e0:e1, :], w2_scales.rearrange("e s q n -> (e s) q n")[e0:e1])
                     nc.sync.dma_start(
                         out=w2w[:, e0:e1, :].bitcast(I32),
                         in_=w2_words[e0:e1].rearrange("e s p b -> p (e s) b").bitcast(I32),
@@ -273,9 +271,9 @@ def tile_moe_pkd_mlp_relu2_kernel(
             for u in turned_now:
                 square(u)
 
-
         for u in (2 * E - 2, 2 * E - 1):
             relu(u)
+        first_half(1)
         for u in range(2 * E - 3, 2 * E):
             turn(u)
         quantise(6 * C, 7 * C, place("after15", C))
@@ -284,7 +282,7 @@ def tile_moe_pkd_mlp_relu2_kernel(
         for u in (2 * E - 2, 2 * E - 1):
             square(u)
             quantise(u * P, (u + 1) * P, last_codes if u % 2 else place("hq16", P))
-        for pair in range(1, 4):
+        for pair in range(2, 4):
             first_half(pair)
         for u in (2 * E - 2, 2 * E - 1):
             layer2(0, u * P, (u + 1) * P, banks[6 + u % 2], nc.vector.tensor_copy)
@@ -300,7 +298,7 @@ def tile_moe_pkd_mlp_relu2_kernel(
 
         fetched = {
             (a, r): keep.tile([P, T], F32, name="fetched%d_%d" % (a, r), align_bytes=64)
-            for a, r in ((0, 2), (1, 2), (1, 1))
+            for a, r in ((0, 2), (1, 2))
         }
         last_r = TOP - 1
 
@@ -346,8 +344,6 @@ def tile_moe_pkd_mlp_relu2_kernel(
         add_on_tensor(0, last_r, HALF_T, 6, False, True)
         take_sum(0, 0, 5)
         take_sum(0, HALF_T, 6)
-        fetch(1, last_r, HALF_T, T)
-        fetch(1, 1, HALF_T, T)
         product(1, 0, 0, HALF_T)
         add_on_tensor(1, 0, 0, 7, True, False)
         turn_back(0, 0, 0, nc.sync)
@@ -360,11 +356,10 @@ def tile_moe_pkd_mlp_relu2_kernel(
         turn_back(1, 0, 2, nc.scalar)
 
         product(1, 0, DIRECT_FROM, T)
-        weigh(1, last_r, DIRECT_FROM, T)
-        weigh(1, 1, DIRECT_FROM, T)
-        pieces = ((DIRECT_FROM, T - LAST), (T - LAST, T))
-        for t0, t1 in pieces:
-            nc.vector.tensor_tensor(part[:, t0:t1], prod[1][0][:, t0:t1], prod[1][2][:, t0:t1], ALU.add)
-        for t0, t1 in pieces:
-            nc.vector.tensor_tensor(res[1][:, t0:t1], part[:, t0:t1], prod[1][1][:, t0:t1], ALU.add)
+        product(1, 1, DIRECT_FROM, T)
+        product(1, 2, DIRECT_FROM, T - LAST)
+        nc.vector.tensor_tensor(part[:, DIRECT_FROM:], prod[1][0][:, DIRECT_FROM:], prod[1][1][:, DIRECT_FROM:], ALU.add)
+        product(1, 2, T - LAST, T)
+        for t0, t1 in ((DIRECT_FROM, T - LAST), (T - LAST, T)):
+            nc.vector.tensor_tensor(res[1][:, t0:t1], part[:, t0:t1], prod[1][2][:, t0:t1], ALU.add)
             nc.sync.dma_start(out=out[P:, t0:t1], in_=res[1][:, t0:t1])

@@ -8,6 +8,7 @@ TOP = 3
 S = E * C
 P = 128
 PASSES = K // 512
+PAIR = 2 * C
 HALF_T = T // 2
 FLOPS = 2 * S * (K * H + H * N)
 
@@ -22,16 +23,10 @@ FP4X4 = mybir.dt.float4_e2m1fn_x4
 ACT = mybir.ActivationFunctionType
 ALU = mybir.AluOpType
 
-PAIR = 2 * C
-BYTE_CUTS = (0, 2, 4, 6, 8, 9)
-W1_CUTS = (0, 1, 2, 4, 6, 8, 9)
-SCALE_CUTS = (0, 5, 7, 9)
-QUANTISE_AT = {6: ((0, "after10"),), 7: ((1, "after12"), (2, "after13"))}
-MOVED = 112
+SCALE_CUTS = (0, 3, 5, 7, 9)
+LIVE = 100
 RELU_ON_VECTOR = (5, 9, 13, 16)
-COPY_ON_VECTOR = (0, 1)
 W2_FIRST = 4
-DIRECT_FROM = HALF_T
 LAST = 128
 
 
@@ -63,16 +58,18 @@ def tile_moe_pkd_mlp_relu2_kernel(
         w2w = keep.tile([P, E, 2 * N], U8, name="w2w", align_bytes=256)
         g = keep.tile([P, TOP, T], F32, name="g", align_bytes=64)
         w1s = {}
-        w1w = {}
         for c, tile in enumerate(w1s_t):
             for e in range(SCALE_CUTS[c], SCALE_CUTS[c + 1]):
                 for s in range(PASSES):
                     w1s[e, s] = tile[:, PASSES * (e - SCALE_CUTS[c]) + s, :]
+        w1w = {}
         xg = {}
         sg0 = {}
-        planes0 = {}
         hq = {}
         relu_t = {}
+
+        def slots_of(pair):
+            return pair * PAIR, min((pair + 1) * PAIR, S)
 
         def zero(planes, engine):
             engine.memset(planes[:].rearrange("p a c -> p (a c)").bitcast(I32), 0)
@@ -84,49 +81,49 @@ def tile_moe_pkd_mlp_relu2_kernel(
                     in_=src[:, 4 * q : 4 * q + 4, :].rearrange("a r c -> r a c").bitcast(I32),
                 )
 
-        def load_w1s(c):
+        def load_w1_scales(c):
             rows = w1_scales.rearrange("e s q i -> (e s) q i")
             load_scales(w1s_t[c], rows[PASSES * SCALE_CUTS[c] : PASSES * SCALE_CUTS[c + 1]])
 
-        def load_w1(c):
-            e0, e1 = W1_CUTS[c], W1_CUTS[c + 1]
-            words = keep.tile([P, PASSES * (e1 - e0), 2 * H], U8, name="w1w%d" % c, align_bytes=256)
-            for e in range(e0, e1):
-                for s in range(PASSES):
-                    w1w[e, s] = words[:, PASSES * (e - e0) + s, :]
+        def load_w1(e):
+            w1w[e] = keep.tile([P, PASSES, 2 * H], U8, name="w1w%d" % e, align_bytes=256)
+            nc.sync.dma_start(out=w1w[e][:].bitcast(I32), in_=w1_words[e].rearrange("s p b -> p s b").bitcast(I32))
+
+        def load_w2(e0, e1):
+            load_scales(w2s[:, e0:e1, :], w2_scales.rearrange("e s q n -> (e s) q n")[e0:e1])
             nc.sync.dma_start(
-                out=words[:].bitcast(I32), in_=w1_words[e0:e1].rearrange("e s p b -> p (e s) b").bitcast(I32)
+                out=w2w[:, e0:e1, :].bitcast(I32), in_=w2_words[e0:e1].rearrange("e s p b -> p (e s) b").bitcast(I32)
             )
 
-        def gather_words(s, j0, j1, dst):
-            for u in range(j0 // P, j1 // P):
-                xg[u, s] = dst[:, u * P - j0 : (u + 1) * P - j0]
-            nc.vector.tensor_copy(dst, xw[:, s, :].bitcast(U32).indirect(offs_t[:, j0 // 16 : j1 // 16]))
-
-        def gather_bytes(c, tag):
-            j0, j1 = BYTE_CUTS[c] * C, BYTE_CUTS[c + 1] * C
-            planes0[c] = turns.tile([P, j1 - j0], U8, name="sg0", tag=tag, align_bytes=256)
-            for u in range(j0 // P, j1 // P):
-                sg0[u] = planes0[c][:, u * P - j0 : (u + 1) * P - j0]
-            nc.vector.tensor_copy(planes0[c][:], xs[:].indirect(offs_t[:, j0 // 16 : j1 // 16]))
-
-        def move_bytes(c, queue, cuts):
-            j0, j1 = BYTE_CUTS[c] * C, BYTE_CUTS[c + 1] * C
-            for p0, p1 in cuts:
-                queue.dma_start(out=sg1[p0:p1, j0:j1].bitcast(I32), in_=planes0[c][4 + p0 : 4 + p1, :].bitcast(I32))
+        def gather_words(e, s, dst):
+            for u in (2 * e, 2 * e + 1):
+                xg[u, s] = dst[:, u * P - e * C : (u + 1) * P - e * C]
+            nc.vector.tensor_copy(dst, xw[:, s, :].bitcast(U32).indirect(offs_t[:, e * C // 16 : (e + 1) * C // 16]))
 
         def gather_expert(e, tag):
             words = turns.tile([P, PASSES, C], U32, name="xg", tag=tag, align_bytes=256)
             for s in range(PASSES):
-                gather_words(s, e * C, (e + 1) * C, words[:, s, :])
+                gather_words(e, s, words[:, s, :])
+
+        def gather_bytes(pair, tag):
+            j0, j1 = slots_of(pair)
+            sg0[pair] = turns.tile([P, j1 - j0], U8, name="sg0", tag=tag, align_bytes=256)
+            nc.vector.tensor_copy(sg0[pair][:], xs[:].indirect(offs_t[:, j0 // 16 : j1 // 16]))
+
+        def move_bytes(pair, cuts):
+            j0, j1 = slots_of(pair)
+            for p0, p1 in cuts:
+                nc.sync.dma_start(out=sg1[p0:p1, j0:j1].bitcast(I32), in_=sg0[pair][4 + p0 : 4 + p1, :].bitcast(I32))
 
         def layer1(u):
+            in_pair = u % 4 * P
+            token_scales = (sg0[u // 4][:, in_pair : in_pair + P], sg1[:, u * P : (u + 1) * P])
             for s in range(PASSES):
                 nc.tensor.matmul_mx(
                     out=banks[u % 4],
                     lhsT=xg[u, s].bitcast(FP8X4),
-                    lhsT_scale=(sg0[u], sg1[:, u * P : (u + 1) * P])[s],
-                    rhs=w1w[u // 2, s].bitcast(FP4X4),
+                    lhsT_scale=token_scales[s],
+                    rhs=w1w[u // 2][:, s, :].bitcast(FP4X4),
                     rhs_scale=w1s[u // 2, s],
                     start=(s == 0),
                     stop=(s == PASSES - 1),
@@ -153,46 +150,43 @@ def tile_moe_pkd_mlp_relu2_kernel(
                 out=hb[:, u * P : (u + 1) * P, :], in_=turned(u).rearrange("p t j -> p j t"), func=ACT.Square
             )
 
-        def place(name, slots):
-            return turns.tile([P, slots], U32, name="hq", tag=name, align_bytes=256)
-
-        def quantise(j0, j1, codes):
+        def quantise(j0, j1, tag):
+            codes = turns.tile([P, j1 - j0], U32, name="hq", tag=tag, align_bytes=256)
             for lo in range(j0, j1, P):
                 hq[lo] = codes[:, lo - j0 :]
             nc.vector.quantize_mx(
                 out=codes[:].bitcast(FP8X4), scales=hs[:, j0:j1], in_=hb[:, j0:j1, :].rearrange("p j t -> p (j t)")
             )
 
-        def layer2(a, j0, j1, acc, copy):
-            step = C if j0 < 8 * C else P
+        def layer2(a, j0, j1, bank, copy):
+            step = C if j0 < (E - 1) * C else P
             for lo in range(j0, j1, step):
-                hi = lo + step
                 e = lo // C
                 nc.tensor.matmul_mx(
-                    out=acc[:, lo - j0 : hi - j0],
+                    out=banks[bank][:, lo - j0 : lo - j0 + step],
                     lhsT=w2w[:, e, a * N : (a + 1) * N].bitcast(FP4X4),
                     lhsT_scale=w2s[:, e, a * P : (a + 1) * P],
                     rhs=hq[lo][:, :step].bitcast(FP8X4),
-                    rhs_scale=hs[:, lo:hi],
+                    rhs_scale=hs[:, lo : lo + step],
                     start=True,
                     stop=True,
                 )
-            copy(y[a][:, j0:j1], acc[:, : j1 - j0])
+            copy(y[a][:, j0:j1], banks[bank][:, : j1 - j0])
 
         def first_half(pair):
-            copy = nc.vector.tensor_copy if pair in COPY_ON_VECTOR else nc.scalar.copy
-            layer2(0, pair * PAIR, (pair + 1) * PAIR, banks[(2, 3, 0, 1)[pair]], copy)
+            copy = nc.vector.tensor_copy if 2 * pair < W2_FIRST else nc.scalar.copy
+            j0, j1 = slots_of(pair)
+            layer2(0, j0, j1, (pair + 2) % 4, copy)
 
         nc.gpsimd.memset(xs[:].bitcast(I32), 0)
         zero(w1s_t[0], nc.vector)
         nc.vector.memset(sg1[:].bitcast(I32), 0)
         make_identity(nc, ident_src[:])
         nc.scalar.activation(out=ident[:], in_=ident_src[:], func=ACT.Relu)
-        for planes in w1s_t[1:]:
-            zero(planes, nc.vector)
+        zero(w1s_t[1], nc.vector)
+        zero(w1s_t[2], nc.vector)
+        zero(w1s_t[3], nc.gpsimd)
         zero(w2s, nc.gpsimd)
-
-        last_codes = keep.tile([P, P], U32, name="last_codes", align_bytes=256)
 
         nc.sync.dma_start(offs_t[:], offs)
         for q in range(4):
@@ -201,165 +195,179 @@ def tile_moe_pkd_mlp_relu2_kernel(
             )
         load_w1(0)
         nc.sync.dma_start(out=xw[:], in_=x_words.rearrange("s p t r -> p s (t r)").bitcast(I32))
-        load_w1s(0)
+        load_w1_scales(0)
 
-        in_three = ((0, 64), (64, 96), (96, 100))
-        at_once = ((0, MOVED),)
-        gather_bytes(0, "planes0")
-        move_bytes(0, nc.sync, in_three)
-        gather_bytes(1, "planes1")
+        in_three = ((0, 64), (64, 96), (96, LIVE))
+        at_once = ((0, LIVE),)
+        gather_bytes(0, "pair0")
+        move_bytes(0, in_three)
+        gather_bytes(1, "pair1")
         load_w1(1)
-        move_bytes(1, nc.sync, at_once)
+        move_bytes(1, at_once)
         load_w1(2)
         for e in range(2):
             for s in range(PASSES):
-                first = turns.tile([P, C], U32, name="xg_first", tag="words%d" % (2 * e + s), align_bytes=256)
-                gather_words(s, e * C, (e + 1) * C, first[:])
+                first = turns.tile([P, C], U32, name="xg_first", tag="first%d" % (PASSES * e + s), align_bytes=256)
+                gather_words(e, s, first[:])
         for u in range(4):
             layer1(u)
-        gather_expert(2, "words0")
-        gather_bytes(2, "words1")
-        gather_expert(3, "words2")
+        gather_expert(2, "even")
+        gather_bytes(2, "first0")
+        gather_expert(3, "first1")
+        gather_bytes(3, "first3")
         relu(0)
         relu(1)
+        load_w1_scales(1)
         load_w1(3)
-        move_bytes(2, nc.sync, in_three)
-        load_w1s(1)
         load_w1(4)
+        move_bytes(2, at_once)
+        load_w1_scales(2)
+        load_w1(5)
 
-        turn_cuts = (0, 0, 2, 4, 6, 8, 10, 12, 15)
-        for e in range(1, E - 1):
-            turned_now = range(turn_cuts[e], turn_cuts[e + 1])
-            if e == E - 2:
-                relu(2 * e)
-            for u in turned_now:
-                turn(u)
+        def round_of(e):
+            turn(2 * e - 2)
+            turn(2 * e - 1)
             layer1(2 * e + 2)
             layer1(2 * e + 3)
-            if e == E - 2:
-                first_half(0)
-            else:
-                relu(2 * e)
+            relu(2 * e)
             relu(2 * e + 1)
-            if e == 2:
-                gather_expert(4, "words0")
-                gather_bytes(3, "after2")
-                gather_expert(5, "after3")
-                move_bytes(3, nc.sync, at_once)
-                load_w1s(2)
-                load_w1(5)
-            if e == 3:
-                gather_bytes(4, "words2")
-                move_bytes(4, nc.sync, at_once)
-                load_scales(w2s, w2_scales.rearrange("e s q n -> (e s) q n"))
-                for e0, e1 in ((0, W2_FIRST), (W2_FIRST, E)):
-                    nc.sync.dma_start(
-                        out=w2w[:, e0:e1, :].bitcast(I32),
-                        in_=w2_words[e0:e1].rearrange("e s p b -> p (e s) b").bitcast(I32),
-                    )
-                for r, src in enumerate((pos1, pos2, pos3)):
-                    nc.sync.dma_start(pos_t[r][:], src)
-                nc.sync.dma_start(out=g[:], in_=gate[:, 0:P, :].rearrange("r p t -> p r t"))
-            if e == 4:
-                gather_expert(6, "words0")
-                gather_expert(7, "after6")
-            if e == 5:
-                gather_expert(8, "after3")
-            if e in QUANTISE_AT:
-                for pair, name in QUANTISE_AT[e]:
-                    quantise(pair * PAIR, (pair + 1) * PAIR, place(name, PAIR))
-            for u in turned_now:
-                square(u)
 
-        for u in (2 * E - 2, 2 * E - 1):
-            relu(u)
-        first_half(1)
-        for u in range(2 * E - 3, 2 * E):
+        def squares_of(e):
+            square(2 * e)
+            square(2 * e + 1)
+
+        round_of(1)
+        squares_of(0)
+
+        round_of(2)
+        gather_expert(4, "even")
+        gather_expert(5, "after2")
+        move_bytes(3, at_once)
+        load_w1(6)
+        load_w1_scales(3)
+        load_w1(7)
+        load_w1(8)
+        squares_of(1)
+
+        round_of(3)
+        gather_bytes(4, "first1")
+        move_bytes(4, at_once)
+        load_w2(0, W2_FIRST)
+        load_w2(W2_FIRST, E)
+        for r, src in enumerate((pos1, pos2, pos3)):
+            nc.sync.dma_start(pos_t[r][:], src)
+        nc.sync.dma_start(out=g[:], in_=gate[:, 0:P, :].rearrange("r p t -> p r t"))
+        squares_of(2)
+
+        round_of(4)
+        gather_expert(6, "even")
+        gather_expert(7, "after6")
+        squares_of(3)
+
+        round_of(5)
+        gather_expert(8, "after2")
+        squares_of(4)
+
+        round_of(6)
+        quantise(0, PAIR, "after10")
+        squares_of(5)
+
+        relu(14)
+        for u in (12, 13, 14):
             turn(u)
-        quantise(6 * C, 7 * C, place("after15", C))
-        square(2 * E - 3)
-        quantise(7 * C, 8 * C, place("hq7", C))
-        for u in (2 * E - 2, 2 * E - 1):
+        layer1(16)
+        layer1(17)
+        first_half(0)
+        relu(15)
+        quantise(PAIR, 2 * PAIR, "after12")
+        quantise(2 * PAIR, 3 * PAIR, "after13")
+        for u in (12, 13, 14):
             square(u)
-            quantise(u * P, (u + 1) * P, last_codes if u % 2 else place("hq16", P))
-        for pair in range(2, 4):
-            first_half(pair)
-        for u in (2 * E - 2, 2 * E - 1):
-            layer2(0, u * P, (u + 1) * P, banks[6 + u % 2], nc.vector.tensor_copy)
+        relu(16)
+        relu(17)
+        first_half(1)
+        for u in (15, 16, 17):
+            turn(u)
+        quantise(6 * C, 7 * C, "after15")
+        square(15)
+        quantise(7 * C, 8 * C, "hq7")
+        for u in (16, 17):
+            square(u)
+            quantise(u * P, (u + 1) * P, "hq%d" % u)
+        first_half(2)
+        first_half(3)
+        for u in (16, 17):
+            layer2(0, u * P, (u + 1) * P, 6 + u % 2, nc.vector.tensor_copy)
+
         prod = [[keep.tile([P, T], F32, name="prod%d_%d" % (a, r), align_bytes=64) for r in range(TOP)] for a in range(2)]
         sum_t = [keep.tile([P, T], F32, name="sum_t%d" % a, align_bytes=64) for a in range(2)]
         part = keep.tile([P, T], F32, name="part", align_bytes=64)
         res = [keep.tile([P, T], F32, name="res%d" % a, align_bytes=64) for a in range(2)]
+        fetched = [keep.tile([P, T], F32, name="fetched%d" % a, align_bytes=64) for a in range(2)]
+        third = TOP - 1
 
         def product(a, r, t0, t1):
             nc.vector.tensor_tensor(
                 prod[a][r][:, t0:t1], y[a][:].indirect(pos_t[r][:, t0 // 16 : t1 // 16]), g[:, r, t0:t1], ALU.mult
             )
 
-        fetched = {
-            (a, r): keep.tile([P, T], F32, name="fetched%d_%d" % (a, r), align_bytes=64)
-            for a, r in ((0, 2), (1, 2))
-        }
-        last_r = TOP - 1
+        def fetch_third(a, t1):
+            nc.scalar.activation(out=fetched[a][:, :t1], in_=y[a][:].indirect(pos_t[third][:, : t1 // 16]), func=ACT.Copy)
 
-        def fetch(a, r, t0, t1):
-            nc.scalar.activation(
-                out=fetched[a, r][:, t0:t1], in_=y[a][:].indirect(pos_t[r][:, t0 // 16 : t1 // 16]), func=ACT.Copy
-            )
+        def weigh_third(a, t1):
+            nc.vector.tensor_tensor(prod[a][third][:, :t1], fetched[a][:, :t1], g[:, third, :t1], ALU.mult)
 
-        def weigh(a, r, t0, t1):
-            nc.vector.tensor_tensor(prod[a][r][:, t0:t1], fetched[a, r][:, t0:t1], g[:, r, t0:t1], ALU.mult)
-
-        def add_on_tensor(a, r, t0, bank, start, stop):
+        def add_on_tensor(a, r, t0, bank):
             for lo in range(t0, t0 + HALF_T, P):
                 nc.tensor.matmul(
                     banks[bank][:, lo - t0 : lo - t0 + P],
                     lhsT=prod[a][r][:, lo : lo + P],
                     rhs=ident[:],
                     is_transpose=True,
-                    start=(start and lo == t0),
-                    stop=(stop and lo == t0 + HALF_T - P),
+                    start=(r == 0 and lo == t0),
+                    stop=(r == third and lo == t0 + HALF_T - P),
                 )
 
         def take_sum(a, t0, bank):
             nc.scalar.copy(out=sum_t[a][:, t0 : t0 + HALF_T], in_=banks[bank][:, :HALF_T])
 
-        def turn_back(a, t0, back_bank, queue):
+        def turn_back(a, t0, bank, queue):
             t1 = t0 + HALF_T
             for lo in range(t0, t1, P):
-                nc.tensor.transpose(banks[back_bank][:, lo - t0 : lo - t0 + P], sum_t[a][:, lo : lo + P], ident[:])
-            nc.scalar.copy(out=res[a][:, t0:t1], in_=banks[back_bank][:, :HALF_T])
+                nc.tensor.transpose(banks[bank][:, lo - t0 : lo - t0 + P], sum_t[a][:, lo : lo + P], ident[:])
+            nc.scalar.copy(out=res[a][:, t0:t1], in_=banks[bank][:, :HALF_T])
             queue.dma_start(out=out[a * P : (a + 1) * P, t0:t1], in_=res[a][:, t0:t1])
 
-        fetch(0, last_r, 0, T)
-        for k, j0 in enumerate(range(0, S, 2 * C)):
-            layer2(1, j0, min(j0 + 2 * C, S), banks[k], nc.scalar.copy)
-        fetch(1, last_r, 0, HALF_T)
-        for r in range(TOP - 1):
+        fetch_third(0, T)
+        for pair in range(5):
+            j0, j1 = slots_of(pair)
+            layer2(1, j0, j1, pair, nc.scalar.copy)
+        fetch_third(1, HALF_T)
+        for r in range(third):
             product(0, r, 0, T)
-            add_on_tensor(0, r, 0, 5, r == 0, False)
-            add_on_tensor(0, r, HALF_T, 6, r == 0, False)
-        weigh(0, last_r, 0, T)
-        add_on_tensor(0, last_r, 0, 5, False, True)
-        add_on_tensor(0, last_r, HALF_T, 6, False, True)
+            add_on_tensor(0, r, 0, 5)
+            add_on_tensor(0, r, HALF_T, 6)
+        weigh_third(0, T)
+        add_on_tensor(0, third, 0, 5)
+        add_on_tensor(0, third, HALF_T, 6)
         take_sum(0, 0, 5)
         take_sum(0, HALF_T, 6)
         product(1, 0, 0, HALF_T)
-        add_on_tensor(1, 0, 0, 7, True, False)
+        add_on_tensor(1, 0, 0, 7)
         turn_back(0, 0, 0, nc.sync)
         product(1, 1, 0, HALF_T)
-        add_on_tensor(1, 1, 0, 7, False, False)
-        weigh(1, last_r, 0, HALF_T)
-        add_on_tensor(1, last_r, 0, 7, False, True)
+        add_on_tensor(1, 1, 0, 7)
+        weigh_third(1, HALF_T)
+        add_on_tensor(1, third, 0, 7)
         take_sum(1, 0, 7)
         turn_back(0, HALF_T, 1, nc.scalar)
         turn_back(1, 0, 2, nc.scalar)
 
-        product(1, 0, DIRECT_FROM, T)
-        product(1, 1, DIRECT_FROM, T)
-        product(1, 2, DIRECT_FROM, T - LAST)
-        nc.vector.tensor_tensor(part[:, DIRECT_FROM:], prod[1][0][:, DIRECT_FROM:], prod[1][1][:, DIRECT_FROM:], ALU.add)
-        product(1, 2, T - LAST, T)
-        for t0, t1 in ((DIRECT_FROM, T - LAST), (T - LAST, T)):
-            nc.vector.tensor_tensor(res[1][:, t0:t1], part[:, t0:t1], prod[1][2][:, t0:t1], ALU.add)
+        product(1, 0, HALF_T, T)
+        product(1, 1, HALF_T, T)
+        product(1, third, HALF_T, T - LAST)
+        nc.vector.tensor_tensor(part[:, HALF_T:], prod[1][0][:, HALF_T:], prod[1][1][:, HALF_T:], ALU.add)
+        product(1, third, T - LAST, T)
+        for t0, t1 in ((HALF_T, T - LAST), (T - LAST, T)):
+            nc.vector.tensor_tensor(res[1][:, t0:t1], part[:, t0:t1], prod[1][third][:, t0:t1], ALU.add)
             nc.sync.dma_start(out=out[P:, t0:t1], in_=res[1][:, t0:t1])

@@ -23,10 +23,10 @@ FP4X4 = mybir.dt.float4_e2m1fn_x4
 ACT = mybir.ActivationFunctionType
 ALU = mybir.AluOpType
 
-SCALE_CUTS = (0, 3, 5, 7, 9)
+SCALE_CUTS = (0, 4, 6, 8, 9)
+BYTE_CUTS = (0, 2, 4, 6, 8, 9)
 LIVE = 100
-RELU_ON_VECTOR = (5, 9, 13, 16)
-W2_FIRST = 4
+RELU_ON_VECTOR = (6, 9, 12, 15, 16)
 LAST = 128
 
 
@@ -44,7 +44,6 @@ def tile_moe_pkd_mlp_relu2_kernel(
         pos_t = [keep.tile([P, T // 16], U16, name="pos_t%d" % r) for r in range(TOP)]
         xw = keep.tile([P, PASSES, T], I32, name="xw", align_bytes=64)
         xs = keep.tile([P, T], U8, name="xs", align_bytes=64)
-        w2s = keep.tile([P, E, N], U8, name="w2s", align_bytes=256)
         sg1 = keep.tile([P, S], U8, name="sg1", align_bytes=256)
         hb = keep.tile([P, S, 4], BF16, name="hb", align_bytes=256)
         hs = keep.tile([P, S], U8, name="hs", align_bytes=256)
@@ -57,6 +56,7 @@ def tile_moe_pkd_mlp_relu2_kernel(
         ]
         w2w = keep.tile([P, E, 2 * N], U8, name="w2w", align_bytes=256)
         g = keep.tile([P, TOP, T], F32, name="g", align_bytes=64)
+        w2s = w1s_t[0][:].rearrange("p a (b n) -> p (a b) n", n=N)[:, :E, :]
         w1s = {}
         for c, tile in enumerate(w1s_t):
             for e in range(SCALE_CUTS[c], SCALE_CUTS[c + 1]):
@@ -65,35 +65,31 @@ def tile_moe_pkd_mlp_relu2_kernel(
         w1w = {}
         xg = {}
         sg0 = {}
+        plane0 = {}
         hq = {}
         relu_t = {}
 
-        def slots_of(pair):
-            return pair * PAIR, min((pair + 1) * PAIR, S)
+        def place(shape, dtype, tag):
+            return turns.tile(shape, dtype, name="placed", tag=tag, align_bytes=256)
 
         def zero(planes, engine):
             engine.memset(planes[:].rearrange("p a c -> p (a c)").bitcast(I32), 0)
 
-        def load_scales(planes, src):
+        def load_scales(planes, src, queue):
             for q in (0, 2, 1, 3):
-                nc.sync.dma_start(
+                queue.dma_start(
                     out=planes[32 * q : 32 * q + 4, :, :].bitcast(I32),
                     in_=src[:, 4 * q : 4 * q + 4, :].rearrange("a r c -> r a c").bitcast(I32),
                 )
 
         def load_w1_scales(c):
             rows = w1_scales.rearrange("e s q i -> (e s) q i")
-            load_scales(w1s_t[c], rows[PASSES * SCALE_CUTS[c] : PASSES * SCALE_CUTS[c + 1]])
+            load_scales(w1s_t[c], rows[PASSES * SCALE_CUTS[c] : PASSES * SCALE_CUTS[c + 1]], nc.sync)
 
         def load_w1(e):
             w1w[e] = keep.tile([P, PASSES, 2 * H], U8, name="w1w%d" % e, align_bytes=256)
             nc.sync.dma_start(out=w1w[e][:].bitcast(I32), in_=w1_words[e].rearrange("s p b -> p s b").bitcast(I32))
 
-        def load_w2(e0, e1):
-            load_scales(w2s[:, e0:e1, :], w2_scales.rearrange("e s q n -> (e s) q n")[e0:e1])
-            nc.sync.dma_start(
-                out=w2w[:, e0:e1, :].bitcast(I32), in_=w2_words[e0:e1].rearrange("e s p b -> p (e s) b").bitcast(I32)
-            )
 
         def gather_words(e, s, dst):
             for u in (2 * e, 2 * e + 1):
@@ -101,36 +97,40 @@ def tile_moe_pkd_mlp_relu2_kernel(
             nc.vector.tensor_copy(dst, xw[:, s, :].bitcast(U32).indirect(offs_t[:, e * C // 16 : (e + 1) * C // 16]))
 
         def gather_expert(e, tag):
-            words = turns.tile([P, PASSES, C], U32, name="xg", tag=tag, align_bytes=256)
+            words = place([P, PASSES, C], U32, tag)
             for s in range(PASSES):
                 gather_words(e, s, words[:, s, :])
 
-        def gather_bytes(pair, tag):
-            j0, j1 = slots_of(pair)
-            sg0[pair] = turns.tile([P, j1 - j0], U8, name="sg0", tag=tag, align_bytes=256)
-            nc.vector.tensor_copy(sg0[pair][:], xs[:].indirect(offs_t[:, j0 // 16 : j1 // 16]))
+        def gather_bytes(c, tag):
+            j0, j1 = BYTE_CUTS[c] * C, BYTE_CUTS[c + 1] * C
+            sg0[c] = place([P, j1 - j0], U8, tag)
+            for lo in range(j0, j1, P):
+                plane0[lo // P] = sg0[c][:, lo - j0 : lo - j0 + P]
+            nc.vector.tensor_copy(sg0[c][:], xs[:].indirect(offs_t[:, j0 // 16 : j1 // 16]))
 
-        def move_bytes(pair, cuts):
-            j0, j1 = slots_of(pair)
+        def move_bytes(c, cuts):
+            j0, j1 = BYTE_CUTS[c] * C, BYTE_CUTS[c + 1] * C
             for p0, p1 in cuts:
-                nc.sync.dma_start(out=sg1[p0:p1, j0:j1].bitcast(I32), in_=sg0[pair][4 + p0 : 4 + p1, :].bitcast(I32))
+                nc.sync.dma_start(out=sg1[p0:p1, j0:j1].bitcast(I32), in_=sg0[c][4 + p0 : 4 + p1, :].bitcast(I32))
 
-        def layer1(u):
-            in_pair = u % 4 * P
-            token_scales = (sg0[u // 4][:, in_pair : in_pair + P], sg1[:, u * P : (u + 1) * P])
-            for s in range(PASSES):
-                nc.tensor.matmul_mx(
-                    out=banks[u % 4],
-                    lhsT=xg[u, s].bitcast(FP8X4),
-                    lhsT_scale=token_scales[s],
-                    rhs=w1w[u // 2][:, s, :].bitcast(FP4X4),
-                    rhs_scale=w1s[u // 2, s],
-                    start=(s == 0),
-                    stop=(s == PASSES - 1),
-                )
+        def layer1_pass(u, s):
+            nc.tensor.matmul_mx(
+                out=banks[u % 4],
+                lhsT=xg[u, s].bitcast(FP8X4),
+                lhsT_scale=plane0[u] if s == 0 else sg1[:, u * P : (u + 1) * P],
+                rhs=w1w[u // 2][:, s, :].bitcast(FP4X4),
+                rhs_scale=w1s[u // 2, s],
+                start=(s == 0),
+                stop=(s == PASSES - 1),
+            )
+
+        def layer1(*tiles):
+            for u in tiles:
+                for s in range(PASSES):
+                    layer1_pass(u, s)
 
         def relu(u):
-            relu_t[u] = turns.tile([P, 4, P], F32, name="r_t", tag="after%d" % u, align_bytes=256)
+            relu_t[u] = place([P, 4, P], F32, "after%d" % u)
             src = banks[u % 4].rearrange("j (c d t) -> j c t d", d=4, t=4)
             dst = relu_t[u][:].rearrange("j t (c d) -> j c t d", d=4)
             if u in RELU_ON_VECTOR:
@@ -151,7 +151,7 @@ def tile_moe_pkd_mlp_relu2_kernel(
             )
 
         def quantise(j0, j1, tag):
-            codes = turns.tile([P, j1 - j0], U32, name="hq", tag=tag, align_bytes=256)
+            codes = place([P, j1 - j0], U32, tag)
             for lo in range(j0, j1, P):
                 hq[lo] = codes[:, lo - j0 :]
             nc.vector.quantize_mx(
@@ -173,10 +173,10 @@ def tile_moe_pkd_mlp_relu2_kernel(
                 )
             copy(y[a][:, j0:j1], banks[bank][:, : j1 - j0])
 
-        def first_half(pair):
-            copy = nc.vector.tensor_copy if 2 * pair < W2_FIRST else nc.scalar.copy
-            j0, j1 = slots_of(pair)
-            layer2(0, j0, j1, (pair + 2) % 4, copy)
+        def pair2(a, pair, bank, copy):
+            layer2(a, pair * PAIR, min((pair + 1) * PAIR, S), bank, copy)
+
+        on_vector, on_scalar = nc.vector.tensor_copy, nc.scalar.copy
 
         nc.gpsimd.memset(xs[:].bitcast(I32), 0)
         zero(w1s_t[0], nc.vector)
@@ -184,9 +184,8 @@ def tile_moe_pkd_mlp_relu2_kernel(
         make_identity(nc, ident_src[:])
         nc.scalar.activation(out=ident[:], in_=ident_src[:], func=ACT.Relu)
         zero(w1s_t[1], nc.vector)
-        zero(w1s_t[2], nc.vector)
+        zero(w1s_t[2], nc.gpsimd)
         zero(w1s_t[3], nc.gpsimd)
-        zero(w2s, nc.gpsimd)
 
         nc.sync.dma_start(offs_t[:], offs)
         for q in range(4):
@@ -199,175 +198,159 @@ def tile_moe_pkd_mlp_relu2_kernel(
 
         in_three = ((0, 64), (64, 96), (96, LIVE))
         at_once = ((0, LIVE),)
-        gather_bytes(0, "pair0")
+        gather_bytes(0, "bytes0")
         move_bytes(0, in_three)
-        gather_bytes(1, "pair1")
+        gather_bytes(1, "bytes1")
         load_w1(1)
         move_bytes(1, at_once)
         load_w1(2)
         for e in range(2):
             for s in range(PASSES):
-                first = turns.tile([P, C], U32, name="xg_first", tag="first%d" % (PASSES * e + s), align_bytes=256)
-                gather_words(e, s, first[:])
-        for u in range(4):
-            layer1(u)
+                gather_words(e, s, place([P, C], U32, "first%d%d" % (e, s))[:])
+        layer1(0, 1, 2, 3)
         gather_expert(2, "even")
-        gather_bytes(2, "first0")
-        gather_expert(3, "first1")
-        gather_bytes(3, "first3")
-        relu(0)
-        relu(1)
-        load_w1_scales(1)
+        gather_bytes(2, "first00")
+        gather_expert(3, "first01")
         load_w1(3)
+        load_w1_scales(1)
         load_w1(4)
         move_bytes(2, at_once)
-        load_w1_scales(2)
         load_w1(5)
-
-        def round_of(e):
-            turn(2 * e - 2)
-            turn(2 * e - 1)
-            layer1(2 * e + 2)
-            layer1(2 * e + 3)
-            relu(2 * e)
-            relu(2 * e + 1)
-
-        def squares_of(e):
-            square(2 * e)
-            square(2 * e + 1)
-
-        round_of(1)
-        squares_of(0)
-
-        round_of(2)
-        gather_expert(4, "even")
-        gather_expert(5, "after2")
-        move_bytes(3, at_once)
+        load_w1_scales(2)
         load_w1(6)
-        load_w1_scales(3)
-        load_w1(7)
-        load_w1(8)
-        squares_of(1)
 
-        round_of(3)
-        gather_bytes(4, "first1")
+        def each(step, *tiles):
+            for u in tiles:
+                step(u)
+
+        def round_of(u):
+            layer1(u, u + 1, u + 2)
+            each(relu, u, u + 1, u + 2)
+            each(turn, u - 2, u - 1, u)
+            each(square, u - 2, u - 1, u)
+
+        each(relu, 0, 1, 2, 3)
+        each(turn, 0, 1)
+        each(square, 0, 1)
+        gather_expert(4, "first11")
+        gather_bytes(3, "even")
+        move_bytes(3, at_once)
+        load_w1(7)
+        load_w1_scales(3)
+        load_w1(8)
+        round_of(4)
+        gather_expert(5, "after4")
+        gather_expert(6, "first01")
+        round_of(7)
+        gather_expert(7, "first11")
+        gather_bytes(4, "after4")
         move_bytes(4, at_once)
-        load_w2(0, W2_FIRST)
-        load_w2(W2_FIRST, E)
+        load_scales(w2s, w2_scales.rearrange("e s q n -> (e s) q n"), nc.gpsimd)
+        nc.sync.dma_start(out=w2w[:].bitcast(I32), in_=w2_words.rearrange("e s p b -> p (e s) b").bitcast(I32))
         for r, src in enumerate((pos1, pos2, pos3)):
             nc.sync.dma_start(pos_t[r][:], src)
         nc.sync.dma_start(out=g[:], in_=gate[:, 0:P, :].rearrange("r p t -> p r t"))
-        squares_of(2)
-
-        round_of(4)
-        gather_expert(6, "even")
-        gather_expert(7, "after6")
-        squares_of(3)
-
-        round_of(5)
-        gather_expert(8, "after2")
-        squares_of(4)
-
-        round_of(6)
-        quantise(0, PAIR, "after10")
-        squares_of(5)
-
-        relu(14)
-        for u in (12, 13, 14):
-            turn(u)
-        layer1(16)
-        layer1(17)
-        first_half(0)
-        relu(15)
-        quantise(PAIR, 2 * PAIR, "after12")
-        quantise(2 * PAIR, 3 * PAIR, "after13")
-        for u in (12, 13, 14):
-            square(u)
-        relu(16)
-        relu(17)
-        first_half(1)
-        for u in (15, 16, 17):
-            turn(u)
-        quantise(6 * C, 7 * C, "after15")
-        square(15)
+        round_of(10)
+        gather_expert(8, "first01")
+        layer1(13, 14, 15)
+        quantise(0, PAIR, "even")
+        each(relu, 13, 14, 15)
+        quantise(PAIR, 2 * PAIR, "first11")
+        each(turn, 11, 12, 13, 14)
+        each(square, 11, 12, 13, 14)
+        layer1(16, 17)
+        quantise(2 * PAIR, 3 * PAIR, "hq2")
+        each(relu, 16, 17)
+        pair2(0, 0, 2, on_vector)
+        pair2(0, 1, 3, on_vector)
+        each(turn, 15, 16, 17)
+        each(square, 15, 16, 17)
+        quantise(6 * C, 7 * C, "hq6")
         quantise(7 * C, 8 * C, "hq7")
-        for u in (16, 17):
-            square(u)
-            quantise(u * P, (u + 1) * P, "hq%d" % u)
-        first_half(2)
-        first_half(3)
-        for u in (16, 17):
-            layer2(0, u * P, (u + 1) * P, 6 + u % 2, nc.vector.tensor_copy)
+        pair2(0, 2, 6, on_vector)
+        pair2(1, 0, 0, on_scalar)
+        quantise(16 * P, 17 * P, "hq16")
+        pair2(0, 3, 1, on_vector)
+        pair2(1, 1, 2, on_scalar)
+        quantise(17 * P, 18 * P, "hq17")
+        pair2(1, 2, 4, on_scalar)
+        layer2(0, 16 * P, 17 * P, 3, on_vector)
+        pair2(1, 3, 5, on_scalar)
+        layer2(0, 17 * P, 18 * P, 7, on_vector)
 
         prod = [[keep.tile([P, T], F32, name="prod%d_%d" % (a, r), align_bytes=64) for r in range(TOP)] for a in range(2)]
         sum_t = [keep.tile([P, T], F32, name="sum_t%d" % a, align_bytes=64) for a in range(2)]
         part = keep.tile([P, T], F32, name="part", align_bytes=64)
         res = [keep.tile([P, T], F32, name="res%d" % a, align_bytes=64) for a in range(2)]
-        fetched = [keep.tile([P, T], F32, name="fetched%d" % a, align_bytes=64) for a in range(2)]
-        third = TOP - 1
+        fetched = [[keep.tile([P, T], F32, name="fetched%d_%d" % (a, r), align_bytes=64) for r in range(TOP)] for a in range(2)]
 
         def product(a, r, t0, t1):
             nc.vector.tensor_tensor(
                 prod[a][r][:, t0:t1], y[a][:].indirect(pos_t[r][:, t0 // 16 : t1 // 16]), g[:, r, t0:t1], ALU.mult
             )
 
-        def fetch_third(a, t1):
-            nc.scalar.activation(out=fetched[a][:, :t1], in_=y[a][:].indirect(pos_t[third][:, : t1 // 16]), func=ACT.Copy)
+        def fetch(a, r, t0, t1):
+            nc.scalar.activation(
+                out=fetched[a][r][:, t0:t1], in_=y[a][:].indirect(pos_t[r][:, t0 // 16 : t1 // 16]), func=ACT.Copy
+            )
 
-        def weigh_third(a, t1):
-            nc.vector.tensor_tensor(prod[a][third][:, :t1], fetched[a][:, :t1], g[:, third, :t1], ALU.mult)
+        def weigh(a, r, t0, t1):
+            nc.vector.tensor_tensor(prod[a][r][:, t0:t1], fetched[a][r][:, t0:t1], g[:, r, t0:t1], ALU.mult)
 
-        def add_on_tensor(a, r, t0, bank):
-            for lo in range(t0, t0 + HALF_T, P):
+        def add_on_tensor(a, r, t0, t1, bank, first, last):
+            for lo in range(t0, t1, P):
                 nc.tensor.matmul(
                     banks[bank][:, lo - t0 : lo - t0 + P],
                     lhsT=prod[a][r][:, lo : lo + P],
                     rhs=ident[:],
                     is_transpose=True,
-                    start=(r == 0 and lo == t0),
-                    stop=(r == third and lo == t0 + HALF_T - P),
+                    start=(first and lo == t0),
+                    stop=(last and lo == t1 - P),
                 )
 
-        def take_sum(a, t0, bank):
-            nc.scalar.copy(out=sum_t[a][:, t0 : t0 + HALF_T], in_=banks[bank][:, :HALF_T])
+        def take_sum(a, t0, t1, bank):
+            nc.scalar.copy(out=sum_t[a][:, t0:t1], in_=banks[bank][:, : t1 - t0])
 
-        def turn_back(a, t0, bank, queue):
-            t1 = t0 + HALF_T
+        def turn_back(a, t0, t1, bank, queue):
             for lo in range(t0, t1, P):
                 nc.tensor.transpose(banks[bank][:, lo - t0 : lo - t0 + P], sum_t[a][:, lo : lo + P], ident[:])
-            nc.scalar.copy(out=res[a][:, t0:t1], in_=banks[bank][:, :HALF_T])
+            nc.scalar.copy(out=res[a][:, t0:t1], in_=banks[bank][:, : t1 - t0])
             queue.dma_start(out=out[a * P : (a + 1) * P, t0:t1], in_=res[a][:, t0:t1])
 
-        fetch_third(0, T)
-        for pair in range(5):
-            j0, j1 = slots_of(pair)
-            layer2(1, j0, j1, pair, nc.scalar.copy)
-        fetch_third(1, HALF_T)
-        for r in range(third):
-            product(0, r, 0, T)
-            add_on_tensor(0, r, 0, 5)
-            add_on_tensor(0, r, HALF_T, 6)
-        weigh_third(0, T)
-        add_on_tensor(0, third, 0, 5)
-        add_on_tensor(0, third, HALF_T, 6)
-        take_sum(0, 0, 5)
-        take_sum(0, HALF_T, 6)
-        product(1, 0, 0, HALF_T)
-        add_on_tensor(1, 0, 0, 7)
-        turn_back(0, 0, 0, nc.sync)
-        product(1, 1, 0, HALF_T)
-        add_on_tensor(1, 1, 0, 7)
-        weigh_third(1, HALF_T)
-        add_on_tensor(1, third, 0, 7)
-        take_sum(1, 0, 7)
-        turn_back(0, HALF_T, 1, nc.scalar)
-        turn_back(1, 0, 2, nc.scalar)
+        fetch(0, 2, 0, T)
+        pair2(1, 4, 6, on_scalar)
+        fetch(0, 1, 0, HALF_T)
+        fetch(1, 2, 0, 2 * P)
+        fetch(1, 1, 0, 2 * P)
+        product(0, 0, 0, T)
+        add_on_tensor(0, 0, 0, HALF_T, 0, True, False)
+        add_on_tensor(0, 0, HALF_T, T, 1, True, False)
+        product(0, 1, HALF_T, T)
+        add_on_tensor(0, 1, HALF_T, T, 1, False, False)
+        weigh(0, 2, 0, T)
+        add_on_tensor(0, 2, HALF_T, T, 1, False, True)
+        add_on_tensor(0, 2, 0, HALF_T, 0, False, False)
+        weigh(0, 1, 0, HALF_T)
+        add_on_tensor(0, 1, 0, HALF_T, 0, False, True)
+        product(1, 0, 0, 2 * P)
+        add_on_tensor(1, 0, 0, 2 * P, 2, True, False)
+        weigh(1, 2, 0, 2 * P)
+        add_on_tensor(1, 2, 0, 2 * P, 2, False, False)
+        weigh(1, 1, 0, 2 * P)
+        add_on_tensor(1, 1, 0, 2 * P, 2, False, True)
+        take_sum(0, HALF_T, T, 1)
+        fetch(1, 2, 2 * P, T)
+        take_sum(0, 0, HALF_T, 0)
+        take_sum(1, 0, 2 * P, 2)
+        turn_back(0, HALF_T, T, 3, nc.scalar)
+        turn_back(0, 0, HALF_T, 4, nc.scalar)
+        turn_back(1, 0, 2 * P, 5, nc.scalar)
 
-        product(1, 0, HALF_T, T)
-        product(1, 1, HALF_T, T)
-        product(1, third, HALF_T, T - LAST)
-        nc.vector.tensor_tensor(part[:, HALF_T:], prod[1][0][:, HALF_T:], prod[1][1][:, HALF_T:], ALU.add)
-        product(1, third, T - LAST, T)
-        for t0, t1 in ((HALF_T, T - LAST), (T - LAST, T)):
-            nc.vector.tensor_tensor(res[1][:, t0:t1], part[:, t0:t1], prod[1][third][:, t0:t1], ALU.add)
+        product(1, 0, 2 * P, T)
+        product(1, 1, 2 * P, T - LAST)
+        weigh(1, 2, 2 * P, T)
+        product(1, 1, T - LAST, T)
+        nc.vector.tensor_tensor(part[:, 2 * P:], prod[1][0][:, 2 * P:], prod[1][2][:, 2 * P:], ALU.add)
+        for t0, t1 in ((2 * P, T - LAST), (T - LAST, T)):
+            nc.vector.tensor_tensor(res[1][:, t0:t1], part[:, t0:t1], prod[1][1][:, t0:t1], ALU.add)
             nc.sync.dma_start(out=out[P:, t0:t1], in_=res[1][:, t0:t1])

@@ -27,6 +27,7 @@ SCALE_CUTS = (0, 4, 6, 8, 9)
 BYTE_CUTS = (0, 2, 4, 6, 8, 9)
 LIVE = 100
 RELU_ON_VECTOR = (6, 9, 12, 15, 16)
+W2_FIRST = 4
 LAST = 128
 
 
@@ -56,7 +57,7 @@ def tile_moe_pkd_mlp_relu2_kernel(
         ]
         w2w = keep.tile([P, E, 2 * N], U8, name="w2w", align_bytes=256)
         g = keep.tile([P, TOP, T], F32, name="g", align_bytes=64)
-        w2s = w1s_t[0][:].rearrange("p a (b n) -> p (a b) n", n=N)[:, :E, :]
+        w2s = keep.tile([P, E, N], U8, name="w2s", align_bytes=256)
         w1s = {}
         for c, tile in enumerate(w1s_t):
             for e in range(SCALE_CUTS[c], SCALE_CUTS[c + 1]):
@@ -75,21 +76,27 @@ def tile_moe_pkd_mlp_relu2_kernel(
         def zero(planes, engine):
             engine.memset(planes[:].rearrange("p a c -> p (a c)").bitcast(I32), 0)
 
-        def load_scales(planes, src, queue):
+        def load_scales(planes, src):
             for q in (0, 2, 1, 3):
-                queue.dma_start(
+                nc.sync.dma_start(
                     out=planes[32 * q : 32 * q + 4, :, :].bitcast(I32),
                     in_=src[:, 4 * q : 4 * q + 4, :].rearrange("a r c -> r a c").bitcast(I32),
                 )
 
         def load_w1_scales(c):
             rows = w1_scales.rearrange("e s q i -> (e s) q i")
-            load_scales(w1s_t[c], rows[PASSES * SCALE_CUTS[c] : PASSES * SCALE_CUTS[c + 1]], nc.sync)
+            load_scales(w1s_t[c], rows[PASSES * SCALE_CUTS[c] : PASSES * SCALE_CUTS[c + 1]])
 
         def load_w1(e):
             w1w[e] = keep.tile([P, PASSES, 2 * H], U8, name="w1w%d" % e, align_bytes=256)
             nc.sync.dma_start(out=w1w[e][:].bitcast(I32), in_=w1_words[e].rearrange("s p b -> p s b").bitcast(I32))
 
+
+        def load_w2(e0, e1):
+            load_scales(w2s[:, e0:e1, :], w2_scales.rearrange("e s q n -> (e s) q n")[e0:e1])
+            nc.sync.dma_start(
+                out=w2w[:, e0:e1, :].bitcast(I32), in_=w2_words[e0:e1].rearrange("e s p b -> p (e s) b").bitcast(I32)
+            )
 
         def gather_words(e, s, dst):
             for u in (2 * e, 2 * e + 1):
@@ -186,6 +193,7 @@ def tile_moe_pkd_mlp_relu2_kernel(
         zero(w1s_t[1], nc.vector)
         zero(w1s_t[2], nc.gpsimd)
         zero(w1s_t[3], nc.gpsimd)
+        zero(w2s, nc.gpsimd)
 
         nc.sync.dma_start(offs_t[:], offs)
         for q in range(4):
@@ -245,8 +253,8 @@ def tile_moe_pkd_mlp_relu2_kernel(
         gather_expert(7, "first11")
         gather_bytes(4, "after4")
         move_bytes(4, at_once)
-        load_scales(w2s, w2_scales.rearrange("e s q n -> (e s) q n"), nc.gpsimd)
-        nc.sync.dma_start(out=w2w[:].bitcast(I32), in_=w2_words.rearrange("e s p b -> p (e s) b").bitcast(I32))
+        load_w2(0, W2_FIRST)
+        load_w2(W2_FIRST, E)
         for r, src in enumerate((pos1, pos2, pos3)):
             nc.sync.dma_start(pos_t[r][:], src)
         nc.sync.dma_start(out=g[:], in_=gate[:, 0:P, :].rearrange("r p t -> p r t"))

from contextlib import ExitStack

import concourse.mybir as mybir
from concourse.masks import make_identity

K, T, E, C, H, N = 1024, 768, 9, 256, 512, 256
TOP = 3
S = E * C
P = 128
PASSES = K // 512
PAIR = 2 * C
HALF_T = T // 2
FLOPS = 2 * S * (K * H + H * N)

F32 = mybir.dt.float32
BF16 = mybir.dt.bfloat16
I32 = mybir.dt.int32
U32 = mybir.dt.uint32
U16 = mybir.dt.uint16
U8 = mybir.dt.uint8
FP8X4 = mybir.dt.float8_e4m3fn_x4
FP4X4 = mybir.dt.float4_e2m1fn_x4
ACT = mybir.ActivationFunctionType
ALU = mybir.AluOpType

SCALE_CUTS = (0, 4, 6, 8, 9)
BYTE_CUTS = (0, 2, 4, 6, 8, 9)
LIVE = 100
RELU_ON_VECTOR = (6, 9, 12, 15, 16)
W2_FIRST = 4
LAST = 128


def tile_moe_pkd_mlp_relu2_kernel(
    tc, x_words, x_scales, w1_words, w1_scales, w2_words, w2_scales, gate, offs, pos1, pos2, pos3, out
):
    nc = tc.nc
    with ExitStack() as ctx:
        keep = ctx.enter_context(tc.tile_pool(name="keep", bufs=1))
        turns = ctx.enter_context(tc.tile_pool(name="turns", bufs=1))
        psum = ctx.enter_context(tc.psum_pool(name="psum", bufs=1))
        banks = [psum.tile([P, H], F32, name="bank%d" % b)[:] for b in range(8)]

        offs_t = keep.tile([P, S // 16], U16, name="offs_t")
        pos_t = [keep.tile([P, T // 16], U16, name="pos_t%d" % r) for r in range(TOP)]
        xw = keep.tile([P, PASSES, T], I32, name="xw", align_bytes=64)
        xs = keep.tile([P, T], U8, name="xs", align_bytes=64)
        sg1 = keep.tile([P, S], U8, name="sg1", align_bytes=256)
        hb = keep.tile([P, S, 4], BF16, name="hb", align_bytes=256)
        hs = keep.tile([P, S], U8, name="hs", align_bytes=256)
        y = [keep.tile([P, S], F32, name="y%d" % a, align_bytes=64) for a in range(2)]
        ident = keep.tile([P, P], F32, name="ident", align_bytes=64)
        ident_src = keep.tile([P, P], F32, name="ident_src", align_bytes=64)
        w1s_t = [
            keep.tile([P, PASSES * (SCALE_CUTS[c + 1] - SCALE_CUTS[c]), H], U8, name="w1s%d" % c, align_bytes=256)
            for c in range(len(SCALE_CUTS) - 1)
        ]
        w2w = keep.tile([P, E, 2 * N], U8, name="w2w", align_bytes=256)
        g = keep.tile([P, TOP, T], F32, name="g", align_bytes=64)
        w2s = keep.tile([P, E, N], U8, name="w2s", align_bytes=256)
        w1s = {}
        for c, tile in enumerate(w1s_t):
            for e in range(SCALE_CUTS[c], SCALE_CUTS[c + 1]):
                for s in range(PASSES):
                    w1s[e, s] = tile[:, PASSES * (e - SCALE_CUTS[c]) + s, :]
        w1w = {}
        xg = {}
        sg0 = {}
        plane0 = {}
        hq = {}
        relu_t = {}

        def place(shape, dtype, tag):
            return turns.tile(shape, dtype, name="placed", tag=tag, align_bytes=256)

        def zero(planes, engine):
            engine.memset(planes[:].rearrange("p a c -> p (a c)").bitcast(I32), 0)

        def load_scales(planes, src):
            for q in (0, 2, 1, 3):
                nc.sync.dma_start(
                    out=planes[32 * q : 32 * q + 4, :, :].bitcast(I32),
                    in_=src[:, 4 * q : 4 * q + 4, :].rearrange("a r c -> r a c").bitcast(I32),
                )

        def load_w1_scales(c):
            rows = w1_scales.rearrange("e s q i -> (e s) q i")
            load_scales(w1s_t[c], rows[PASSES * SCALE_CUTS[c] : PASSES * SCALE_CUTS[c + 1]])

        def load_w1(e):
            w1w[e] = keep.tile([P, PASSES, 2 * H], U8, name="w1w%d" % e, align_bytes=256)
            nc.sync.dma_start(out=w1w[e][:].bitcast(I32), in_=w1_words[e].rearrange("s p b -> p s b").bitcast(I32))


        def load_w2(e0, e1):
            load_scales(w2s[:, e0:e1, :], w2_scales.rearrange("e s q n -> (e s) q n")[e0:e1])
            nc.sync.dma_start(
                out=w2w[:, e0:e1, :].bitcast(I32), in_=w2_words[e0:e1].rearrange("e s p b -> p (e s) b").bitcast(I32)
            )

        def gather_words(e, s, dst):
            for u in (2 * e, 2 * e + 1):
                xg[u, s] = dst[:, u * P - e * C : (u + 1) * P - e * C]
            nc.vector.tensor_copy(dst, xw[:, s, :].bitcast(U32).indirect(offs_t[:, e * C // 16 : (e + 1) * C // 16]))

        def gather_expert(e, tag):
            words = place([P, PASSES, C], U32, tag)
            for s in range(PASSES):
                gather_words(e, s, words[:, s, :])

        def gather_bytes(c, tag):
            j0, j1 = BYTE_CUTS[c] * C, BYTE_CUTS[c + 1] * C
            sg0[c] = place([P, j1 - j0], U8, tag)
            for lo in range(j0, j1, P):
                plane0[lo // P] = sg0[c][:, lo - j0 : lo - j0 + P]
            nc.vector.tensor_copy(sg0[c][:], xs[:].indirect(offs_t[:, j0 // 16 : j1 // 16]))

        def move_bytes(c, cuts):
            j0, j1 = BYTE_CUTS[c] * C, BYTE_CUTS[c + 1] * C
            for p0, p1 in cuts:
                nc.sync.dma_start(out=sg1[p0:p1, j0:j1].bitcast(I32), in_=sg0[c][4 + p0 : 4 + p1, :].bitcast(I32))

        def layer1_pass(u, s):
            nc.tensor.matmul_mx(
                out=banks[u % 4],
                lhsT=xg[u, s].bitcast(FP8X4),
                lhsT_scale=plane0[u] if s == 0 else sg1[:, u * P : (u + 1) * P],
                rhs=w1w[u // 2][:, s, :].bitcast(FP4X4),
                rhs_scale=w1s[u // 2, s],
                start=(s == 0),
                stop=(s == PASSES - 1),
            )

        def layer1(*tiles):
            for u in tiles:
                for s in range(PASSES):
                    layer1_pass(u, s)

        def relu(u):
            relu_t[u] = place([P, 4, P], F32, "after%d" % u)
            src = banks[u % 4].rearrange("j (c d t) -> j c t d", d=4, t=4)
            dst = relu_t[u][:].rearrange("j t (c d) -> j c t d", d=4)
            if u in RELU_ON_VECTOR:
                nc.vector.tensor_scalar_max(dst, src, 0.0)
            else:
                nc.scalar.activation(out=dst, in_=src, func=ACT.Relu)

        def turned(u):
            return banks[4 + u % 4].rearrange("p (t j) -> p t j", t=4)

        def turn(u):
            for t in range(4):
                nc.tensor.transpose(turned(u)[:, t, :], relu_t[u][:, t, :], ident[:])

        def square(u):
            nc.scalar.activation(
                out=hb[:, u * P : (u + 1) * P, :], in_=turned(u).rearrange("p t j -> p j t"), func=ACT.Square
            )

        def quantise(j0, j1, tag):
            codes = place([P, j1 - j0], U32, tag)
            for lo in range(j0, j1, P):
                hq[lo] = codes[:, lo - j0 :]
            nc.vector.quantize_mx(
                out=codes[:].bitcast(FP8X4), scales=hs[:, j0:j1], in_=hb[:, j0:j1, :].rearrange("p j t -> p (j t)")
            )

        def layer2(a, j0, j1, bank, copy):
            step = C if j0 < (E - 1) * C else P
            for lo in range(j0, j1, step):
                e = lo // C
                nc.tensor.matmul_mx(
                    out=banks[bank][:, lo - j0 : lo - j0 + step],
                    lhsT=w2w[:, e, a * N : (a + 1) * N].bitcast(FP4X4),
                    lhsT_scale=w2s[:, e, a * P : (a + 1) * P],
                    rhs=hq[lo][:, :step].bitcast(FP8X4),
                    rhs_scale=hs[:, lo : lo + step],
                    start=True,
                    stop=True,
                )
            copy(y[a][:, j0:j1], banks[bank][:, : j1 - j0])

        def pair2(a, pair, bank, copy):
            layer2(a, pair * PAIR, min((pair + 1) * PAIR, S), bank, copy)

        on_vector, on_scalar = nc.vector.tensor_copy, nc.scalar.copy

        nc.gpsimd.memset(xs[:].bitcast(I32), 0)
        zero(w1s_t[0], nc.vector)
        nc.vector.memset(sg1[:].bitcast(I32), 0)
        make_identity(nc, ident_src[:])
        nc.scalar.activation(out=ident[:], in_=ident_src[:], func=ACT.Relu)
        zero(w1s_t[1], nc.vector)
        zero(w1s_t[2], nc.gpsimd)
        zero(w1s_t[3], nc.gpsimd)
        zero(w2s, nc.gpsimd)

        nc.sync.dma_start(offs_t[:], offs)
        for q in range(4):
            nc.sync.dma_start(
                out=xs[32 * q : 32 * q + 8, :].bitcast(I32), in_=x_scales[:, 4 * q : 4 * q + 4, :].bitcast(I32)
            )
        load_w1(0)
        nc.sync.dma_start(out=xw[:], in_=x_words.rearrange("s p t r -> p s (t r)").bitcast(I32))
        load_w1_scales(0)

        in_three = ((0, 64), (64, 96), (96, LIVE))
        at_once = ((0, LIVE),)
        gather_bytes(0, "bytes0")
        move_bytes(0, in_three)
        gather_bytes(1, "bytes1")
        load_w1(1)
        move_bytes(1, at_once)
        load_w1(2)
        for e in range(2):
            for s in range(PASSES):
                gather_words(e, s, place([P, C], U32, "first%d%d" % (e, s))[:])
        layer1(0, 1, 2, 3)
        gather_expert(2, "even")
        gather_bytes(2, "first00")
        gather_expert(3, "first01")
        load_w1(3)
        load_w1_scales(1)
        load_w1(4)
        move_bytes(2, at_once)
        load_w1(5)
        load_w1_scales(2)
        load_w1(6)

        def each(step, *tiles):
            for u in tiles:
                step(u)

        def round_of(u):
            layer1(u, u + 1, u + 2)
            each(relu, u, u + 1, u + 2)
            each(turn, u - 2, u - 1, u)
            each(square, u - 2, u - 1, u)

        each(relu, 0, 1, 2, 3)
        each(turn, 0, 1)
        each(square, 0, 1)
        gather_expert(4, "first11")
        gather_bytes(3, "even")
        move_bytes(3, at_once)
        load_w1(7)
        load_w1_scales(3)
        load_w1(8)
        round_of(4)
        gather_expert(5, "after4")
        gather_expert(6, "first01")
        round_of(7)
        gather_expert(7, "first11")
        gather_bytes(4, "after4")
        move_bytes(4, at_once)
        load_w2(0, W2_FIRST)
        load_w2(W2_FIRST, E)
        for r, src in enumerate((pos1, pos2, pos3)):
            nc.sync.dma_start(pos_t[r][:], src)
        nc.sync.dma_start(out=g[:], in_=gate[:, 0:P, :].rearrange("r p t -> p r t"))
        round_of(10)
        gather_expert(8, "first01")
        layer1(13, 14, 15)
        quantise(0, PAIR, "even")
        each(relu, 13, 14, 15)
        quantise(PAIR, 2 * PAIR, "first11")
        each(turn, 11, 12, 13, 14)
        each(square, 11, 12, 13, 14)
        layer1(16, 17)
        quantise(2 * PAIR, 3 * PAIR, "hq2")
        each(relu, 16, 17)
        pair2(0, 0, 2, on_vector)
        pair2(0, 1, 3, on_vector)
        each(turn, 15, 16, 17)
        each(square, 15, 16, 17)
        quantise(6 * C, 7 * C, "hq6")
        quantise(7 * C, 8 * C, "hq7")
        pair2(0, 2, 6, on_vector)
        pair2(1, 0, 0, on_scalar)
        quantise(16 * P, 17 * P, "hq16")
        pair2(0, 3, 1, on_vector)
        pair2(1, 1, 2, on_scalar)
        quantise(17 * P, 18 * P, "hq17")
        pair2(1, 2, 4, on_scalar)
        layer2(0, 16 * P, 17 * P, 3, on_vector)
        pair2(1, 3, 5, on_scalar)
        layer2(0, 17 * P, 18 * P, 7, on_vector)

        prod = [[keep.tile([P, T], F32, name="prod%d_%d" % (a, r), align_bytes=64) for r in range(TOP)] for a in range(2)]
        sum_t = [keep.tile([P, T], F32, name="sum_t%d" % a, align_bytes=64) for a in range(2)]
        part = keep.tile([P, T], F32, name="part", align_bytes=64)
        res = [keep.tile([P, T], F32, name="res%d" % a, align_bytes=64) for a in range(2)]
        fetched = [[keep.tile([P, T], F32, name="fetched%d_%d" % (a, r), align_bytes=64) for r in range(TOP)] for a in range(2)]

        def product(a, r, t0, t1):
            nc.vector.tensor_tensor(
                prod[a][r][:, t0:t1], y[a][:].indirect(pos_t[r][:, t0 // 16 : t1 // 16]), g[:, r, t0:t1], ALU.mult
            )

        def fetch(a, r, t0, t1):
            nc.scalar.activation(
                out=fetched[a][r][:, t0:t1], in_=y[a][:].indirect(pos_t[r][:, t0 // 16 : t1 // 16]), func=ACT.Copy
            )

        def weigh(a, r, t0, t1):
            nc.vector.tensor_tensor(prod[a][r][:, t0:t1], fetched[a][r][:, t0:t1], g[:, r, t0:t1], ALU.mult)

        def add_on_tensor(a, r, t0, t1, bank, first, last):
            for lo in range(t0, t1, P):
                nc.tensor.matmul(
                    banks[bank][:, lo - t0 : lo - t0 + P],
                    lhsT=prod[a][r][:, lo : lo + P],
                    rhs=ident[:],
                    is_transpose=True,
                    start=(first and lo == t0),
                    stop=(last and lo == t1 - P),
                )

        def take_sum(a, t0, t1, bank):
            nc.scalar.copy(out=sum_t[a][:, t0:t1], in_=banks[bank][:, : t1 - t0])

        def turn_back(a, t0, t1, bank, queue):
            for lo in range(t0, t1, P):
                nc.tensor.transpose(banks[bank][:, lo - t0 : lo - t0 + P], sum_t[a][:, lo : lo + P], ident[:])
            nc.scalar.copy(out=res[a][:, t0:t1], in_=banks[bank][:, : t1 - t0])
            queue.dma_start(out=out[a * P : (a + 1) * P, t0:t1], in_=res[a][:, t0:t1])

        fetch(0, 2, 0, T)
        pair2(1, 4, 6, on_scalar)
        fetch(0, 1, 0, HALF_T)
        fetch(1, 2, 0, 2 * P)
        fetch(1, 1, 0, 2 * P)
        product(0, 0, 0, T)
        add_on_tensor(0, 0, 0, HALF_T, 0, True, False)
        add_on_tensor(0, 0, HALF_T, T, 1, True, False)
        product(0, 1, HALF_T, T)
        add_on_tensor(0, 1, HALF_T, T, 1, False, False)
        weigh(0, 2, 0, T)
        add_on_tensor(0, 2, HALF_T, T, 1, False, True)
        add_on_tensor(0, 2, 0, HALF_T, 0, False, False)
        weigh(0, 1, 0, HALF_T)
        add_on_tensor(0, 1, 0, HALF_T, 0, False, True)
        product(1, 0, 0, 2 * P)
        add_on_tensor(1, 0, 0, 2 * P, 2, True, False)
        weigh(1, 2, 0, 2 * P)
        add_on_tensor(1, 2, 0, 2 * P, 2, False, False)
        weigh(1, 1, 0, 2 * P)
        add_on_tensor(1, 1, 0, 2 * P, 2, False, True)
        take_sum(0, HALF_T, T, 1)
        fetch(1, 2, 2 * P, T)
        take_sum(0, 0, HALF_T, 0)
        take_sum(1, 0, 2 * P, 2)
        turn_back(0, HALF_T, T, 3, nc.scalar)
        turn_back(0, 0, HALF_T, 4, nc.scalar)
        turn_back(1, 0, 2 * P, 5, nc.scalar)

        product(1, 0, 2 * P, T)
        product(1, 1, 2 * P, T - LAST)
        weigh(1, 2, 2 * P, T)
        product(1, 1, T - LAST, T)
        nc.vector.tensor_tensor(part[:, 2 * P:], prod[1][0][:, 2 * P:], prod[1][2][:, 2 * P:], ALU.add)
        for t0, t1 in ((2 * P, T - LAST), (T - LAST, T)):
            nc.vector.tensor_tensor(res[1][:, t0:t1], part[:, t0:t1], prod[1][1][:, t0:t1], ALU.add)
            nc.sync.dma_start(out=out[P:, t0:t1], in_=res[1][:, t0:t1])
